import numpy as np, ml_dtypes
CORES = [51,54,179,182]
N = 4
BF = ml_dtypes.bfloat16
def gentries(a):
    return np.ascontiguousarray(a.reshape(8, 16, -1).transpose(0, 2, 1)).reshape(8, -1)
def gtable(e):
    e = np.asarray(e); return np.ascontiguousarray(e.reshape(8, -1, 16).transpose(0, 2, 1)).reshape(128, -1).astype(np.int32)
W, K, L, V, C, WB = 2048, 6, 256, 5, 16, 11
SH = (N, 8, 16, W)
def join(d0, c0, d1, c1):
    return (d0 + W * c0) + 32768 * (d1 + W * c1)
def goals(rng, hub, share):
    j = rng.integers(0, hub.shape[3], SH)
    return np.where(rng.random(SH, dtype=np.float32) < share, np.take_along_axis(hub, j, 3), rng.integers(0, W, SH))
def field(rng):
    return rng.integers(0, W, (N, 8, 16, K // 2 + 1)), rng.choice(np.array([0.0, 0.25, 0.6, 0.95]), (N, 8, 16, 1))
def parts(rng):
    hub, share = field(rng)
    a = join(goals(rng, hub, share), rng.integers(0, C, SH), goals(rng, hub, share), rng.integers(0, C, SH))
    pay = (0.25 + 0.75 * rng.random(SH, dtype=np.float32)) * np.exp2(rng.integers(-1, 2, (N, 8, 16, 1)))
    ac = 4 * rng.random((N, 8, 16, L)); st = rng.integers(0, W, (N, 8, K, L)); rs = (64 * rng.random((N, 8, K, L)) ** 3).astype(np.int64)
    return a, pay, ac, st, rs
def pack(a, pay, ac, st, rs):
    return {"arcs": np.ascontiguousarray(a.reshape(N, 128, W)).astype(np.int32), "pay": np.ascontiguousarray(pay.reshape(N, 128, W)).astype(BF),
            "ac": np.ascontiguousarray(ac.reshape(N, 128, L)).astype(np.float32), "st0": np.stack([gtable(b) for b in st]), "rs0": np.ascontiguousarray(rs.reshape(N, 8, K * L)).astype(np.int32)}
def setup_inputs(rng):
    return pack(*parts(rng))
def setup_inputs_spread(rng):
    a, pay, ac, st, rs = parts(rng)
    a[:, ::2] = rng.integers(0, 2 ** 30, (N, 4, 16, W))
    pay = (0.25 + 0.75 * rng.random(SH, dtype=np.float32)) * np.exp2(rng.integers(-1, 2, (N, 8, 1, W)))
    ac = np.exp2(12 * rng.random((N, 8, 16, L)) - 6); rs = rng.integers(0, 64, (N, 8, K, L))
    return pack(a, pay, ac, st, rs)
def setup_inputs_ends(rng):
    a, pay, ac, st, rs = parts(rng); top = 2 ** 30 - 1
    low = rng.choice(np.array([0.3, 0.5, 0.7]), (N, 8, 16, 1))
    a = np.where(rng.random(SH, dtype=np.float32) < 0.72, np.where(rng.random(SH, dtype=np.float32) < low, 0, top), a)
    st = np.where(rng.random(st.shape) < 0.75, (W - 1) * rng.integers(0, 2, st.shape), st)
    rs = np.where(rng.random(rs.shape) < 0.8, 63 * rng.integers(0, 2, rs.shape), rs)
    ac = np.where(rng.random(ac.shape) < 0.5, 64.0 * rng.integers(0, 2, ac.shape), ac)
    z = [0] + [W - j for j in range(1, K + 1)]
    for j in range(K + 1):
        a[:, :, 14:, z[j]] = 0 if j == 0 else join(z[j], C - 1, z[min(j + 1, K)], C - 1)
        a[:, 1:V, 13, z[j]] = join(0, C - 1, 0, C - 1) if j == 0 else join(z[j], 0, z[j], 0)
    a[:, 7, :14, W - 1] = top
    l = np.arange(7, L, 8); kind = rng.integers(0, 3, (N, 8, len(l))); kind[:, :, -1] = np.arange(8) % 3
    for k in range(K):
        st[:, :, k, l] = z[k]
        rs[:, :, k, l] = 0 if k == 0 else np.where(kind == 0, 63, np.where(kind == 1, 62, 63 if k <= K // 2 else 62))
    ac[:, :, :14, l] = 64.0; ac[:, :, 14, l] = 64.0 * rng.integers(0, 2, kind.shape); ac[:, :, 15, l] = 0.0
    fall = l[1::4]
    ac[:, 0, :15, fall] = 64.0; ac[:, 0, 15, fall] = 0.0
    ac[:, 1:V, :, fall] = 64.0; ac[:, 1:V, 13, fall] = 0.0
    st[:, :, :, L - 2] = W - 1; rs[:, :, :, L - 2] = 63; ac[:, :, :, L - 2] = 64.0
    over = np.arange(L - 3, 0, -32); y = W // 2 + np.arange(K)
    a[:, :, :, y] = join(rng.integers(0, W, (N, 8, 16, K)), C - 1, rng.integers(0, W, (N, 8, 16, K)), C - 1)
    st[:, :, :, over] = y[:, None]; rs[:, :, :, over] = 63
    best = rng.integers(1, 16, (N, 8, 1, len(over)))
    ac[:, :, :, over] = np.where(np.arange(16)[:, None] == best, 64.0 - rng.integers(1, 5, best.shape), 64.0)
    return pack(a, pay, ac, st, rs)
def setup_inputs_corners(rng):
    a, pay, ac, st, rs = parts(rng); pay[:, :, :, W - 1] = 2.0
    j = np.arange(2 * K); hub = K * ((rng.integers(0, W // K, (N, 8, 16, 1)) + 17 * j) % (W // K)) + j % K
    n = rng.choice(np.array([1, 2, K - 1, K, K + 1, 2 * K]), (N, 8, 16, 1)); cls = np.arange(W) % K
    mode = rng.integers(0, 4, (N, 8, 16, 1)); cost = []
    for u in range(2):
        cost.append(np.where(mode == 0, 0, np.where(mode == 1, C - 1, np.where(mode == 2, (C - 1) * rng.integers(0, 2, SH), rng.integers(0, C, SH)))))
    a = join(np.take_along_axis(hub, np.minimum(cls, n - 1), 3), cost[0], np.take_along_axis(hub, np.minimum(cls + K, n - 1), 3), cost[1])
    k = np.arange(K)[:, None]; nil = np.zeros((K, L), np.int64)
    st = K * rng.integers(0, W // K, (N, 8, K, L)) + k
    ways = (nil, nil + 63, nil + np.where(k == 0, 0, 63), nil + np.where(k == K - 1, 0, 63))
    for q in range(N):
        p = rng.permutation(8); b = rng.permutation(8)
        for i in range(4): rs[q, p[i]] = ways[i]
        st[q, b[:2]] = st[q, b[:2], :1]
        st[q, b[2]] = (W - 1) * rng.integers(0, 2, (K, L))
    return pack(a, pay, ac, st, rs)
def setup_inputs_calm(rng):
    a, pay, ac, st, rs = parts(rng); hub, share = field(rng)
    hc = ((2 * np.arange(N)[:, None] + np.arange(8)) % 4)[:, :, None, None]
    c0 = (rng.random(SH) * (hc + 1)).astype(np.int64); c1 = (rng.random(SH) * (hc + 1)).astype(np.int64)
    a = join(goals(rng, hub, share), c0, goals(rng, hub, share), c1)
    rs = np.minimum(rng.integers(0, 4, rs.shape), hc); col = np.arange(L) % 4; s = ac.shape
    ac = np.where(col == 0, 1.0 * rng.integers(0, 3, s), np.where(col == 1, 1 + 2.0 ** -23 * rng.integers(0, 8, s), np.where(col == 2, 0.5 * rng.integers(0, 6, s), 0.0)))
    h = K // 2; z = rng.permutation(W - 1)[:4 * h]
    i = np.arange(4 * h); lab = np.arange(16)[:, None]
    to = np.where(i < 2 * h, 2 * h, 0) + h * (lab % 2); price = np.where(i < 2 * h, 3, 1)
    a[:, :, :, z] = join(z[to + rng.integers(0, h, (N, 8, 16, 4 * h))], price, z[to + rng.integers(0, h, (N, 8, 16, 4 * h))], price)
    l = np.arange(3, L, 8); k = np.arange(K)[:, None]; b = rng.integers(0, 2, (N, 8, 1, len(l)))
    st[:, :, :, l] = z[np.where(k < h, 0, 2 * h) + h * b + k % h]; rs[:, :, :, l] = np.where(k < h, 0, 1)
    p = rng.integers(0, 15, b.shape); q = p + 1 + 2 * (rng.random(b.shape) * ((16 - p) // 2)).astype(np.int64)
    pair = np.array([[11, 8], [8, 5], [16, 11], [5, 0]]); kind = rng.integers(0, 4, b.shape)
    base = 0.25 + 2.0 ** -21 * rng.integers(0, 2 ** 17, b.shape)
    ac[:, :, :, l] = np.where(lab == p, base + 2.0 ** -25 * pair[kind, 0], np.where(lab == q, base + 2.0 ** -25 * pair[kind, 1], 1 + rng.random((N, 8, 16, len(l)))))
    return pack(a, pay, ac, st, rs)
def check_ranges(d):
    bad = []
    for k, lo, hi in (("arcs", 0, 2 ** 30 - 1), ("st0", 0, W - 1), ("rs0", 0, 63)):
        if not (np.min(d[k]) >= lo and np.max(d[k]) <= hi): bad.append("range of " + k)
    e = np.asarray(d["ac"]).astype(np.float32)
    if not np.all((e == 0) | ((e >= 2.0 ** -51) & (e <= 64))): bad.append("range of ac (0, or from 2**-51 to 64)")
    e = np.asarray(d["pay"]).astype(np.float32)
    if not np.all((e >= 0.125) & (e <= 2)): bad.append("range of pay (from 0.125 to 2)")
    return bad
def reference(arcs, pay, ac, st0, rs0):
    A = arcs.astype(np.int32).reshape(N, 8, 16, W); P = pay.astype(np.float32).reshape(N, 8, 16, W); B = ac.astype(np.float32).reshape(N, 8, 16, L)
    s = np.stack([gentries(b) for b in st0]).astype(np.int64); r = rs0.astype(np.int32)
    no = np.arange(2 * K, dtype=np.int32)[:, None]
    ys = np.zeros((N, 8, 16, L)); ym = np.zeros((N, 8, 16, L))
    for t in range(V):
        back = (-t, -t)
        a = np.take_along_axis(np.roll(A, back, (0, 1)), s[:, :, None, :], 3)
        a = np.concatenate([a & 32767, a >> 15], axis=3).reshape(N, 8, 16, 2 * K, L)
        c = (a >> WB) + np.concatenate([r, r], axis=2).reshape(N, 8, 1, 2 * K, L)
        m = np.min(c, axis=3)
        lab = np.argmin(m.astype(np.float32) + np.roll(B, back, (0, 1)), axis=2)[:, :, None, :]
        d = np.take_along_axis(a, lab[:, :, :, None, :], 2)[:, :, 0] & (W - 1)
        x = np.take_along_axis(c, lab[:, :, :, None, :], 2)[:, :, 0] - np.take_along_axis(m, lab, 2)
        key = x * 16 + no
        dup = np.any((d[:, :, :, None] == d[:, :, None]) & (key[:, :, None] < key[:, :, :, None]), axis=3)
        o = np.argsort(np.where(dup, key + 65536, key), axis=2)[:, :, :K]
        gone = np.take_along_axis(dup, o, 2)
        s = np.where(gone, W - 1, np.take_along_axis(d, o, 2)).astype(np.int64).reshape(N, 8, K * L)
        r = np.where(gone, 64, np.take_along_axis(x, o, 2)).astype(np.int32).reshape(N, 8, K * L)
        v = np.take_along_axis(np.roll(P, back, (0, 1)), s[:, :, None, :], 3).reshape(N, 8, 16, K, L) * np.exp(r.astype(np.float64) * -0.125).reshape(N, 8, 1, K, L)
        ys = ys + np.add.reduce(v, axis=3); ym = ym + np.max(v, axis=3)
    return {"ys": ys.reshape(N, 128, L).astype(np.float32), "ym": ym.reshape(N, 128, L).astype(np.float32)}

def check_inputs(d):
    bad = list(check_ranges(d))
    if not bad:
        for name, y in reference(**d).items():
            for q in range(N):
                v = np.abs(np.asarray(y[q], np.float64)); s = np.sqrt(np.mean(v * v))
                if v.max() > 8 * s or s < 2.0 ** 0: bad.append('%s of rank %d is uneven or too small' % (name, q))
    return bad

@@ -1,0 +1,637 @@
+import numpy as np
+from concourse.bass import DstId, RemoteDMATransfer
+from concourse.mybir import AluOpType as A, ActivationFunctionType as F
+
+W, K, L, V = 2048, 6, 256, 5
+PARTS = [128, 128]
+PE = True
+VS = 2
+GK = 1
+NCH = 4
+CW = W // NCH
+NP = len(PARTS)
+CYC, PCY, FIX = 1.0, 0.5, 15.0
+SAME, CROSS, LOOK = 60.0, 120.0, 0.0
+STAG, ALPHA, NOISE, SEED = 0.0, 0.3, 0.0, 0
+LATS, LATX, ISSUE = 2300.0, 14000.0, 400.0
+
+f32, bf, f16, i32, u16 = "float32", "bfloat16", "float16", "int32", "uint16"
+
+
+def _sb(n, d):
+    return ("sbuf", [128, n], d)
+
+
+SCRATCH = {
+    "raw": _sb(W, i32), "lo": _sb(W, i32), "hi": _sb(W, i32), "mn": _sb(W, f32), "win": _sb(2 * W, i32),
+    "payt": _sb(W, bf), "act": _sb(L, f32), "sti": _sb(96, i32), "rsi": _sb(L, i32),
+    "off0": _sb(96, u16), "sf0": _sb(96, f32), "rf0": _sb(L, bf),
+    "val": _sb(144, bf), "vx": _sb(256, bf), "vd": _sb(128, bf), "col": _sb(136, f32), "pi": _sb(8, i32), "pc": _sb(16, f32),
+    "ex": _sb(7 * 128, bf), "dl": _sb(7 * 128, bf), "one": _sb(128, f32), "oneb": _sb(768, bf), "selw": _sb(768, bf), "self": _sb(136, f32),
+    "ra": _sb(128, bf), "tmpc": _sb(512, bf), "dm": _sb(128, bf), "iw": _sb(256, f32), "iwm": _sb(512, f16 if PE else f32), "iwp": _sb(512, bf),
+    "shh": _sb(7 * 128, f16), "dsh": _sb(8 * 128, f16), "shb": _sb(7 * 128, bf), "rsh": _sb(6 * 128, bf),
+    "fmin": _sb(128, f32), "fbc": _sb(128, f32), "fkill": _sb(128, f32), "fpar": _sb(128, bf), "fr": _sb(64, f32), "zero": _sb(512, bf),
+    "mc": _sb(7 * L, bf), "scn": _sb(7 * L, f32), "sc": _sb(L, f32), "xs": _sb(L, f32), "ss": _sb(L, f32),
+    "zl": _sb(L, f32), "step": _sb(L, bf), "ps": _sb(L, bf), "stg": _sb(L, bf), "msk": _sb(GK * L, f32),
+    "sf": _sb(96, f32), "off2": _sb(96, u16), "mg": _sb(6 * L, f32), "cc": _sb(L, bf if PE else f32), "tt": _sb(L, f32),
+    "xf": _sb(L, f32), "key": _sb(L, f32), "dd": _sb(L, f32), "s1": _sb(6 * L, f32), "eq": _sb(L, f32),
+    "kf": _sb(L, f16), "dfr": _sb(L, f16), "sg": _sb(18 * L, bf), "zd": _sb(96, f16), "ka": _sb(96, f32),
+    "zz": _sb(6 * L, f32), "kr": _sb(128, f32), "c16": _sb(128, f32), "df": _sb(128, f32), "rw": _sb(128, f32),
+    "qq": _sb(128, f32), "nn": _sb(128, f32), "rt": _sb(L, bf), "offu": _sb(96, u16),
+    "pg": _sb(6 * L, bf), "mx": _sb(5 * L, f32), "outb": _sb(512, f32),
+    "offs": _sb(4 * 96, u16), "offl": _sb(4 * 96, u16), "rfs": _sb(5 * L, bf), "rfl": _sb(4 * L, bf),
+    "xx": _sb(30 * L, f32), "land": _sb(8 * L, f32),
+}
+for _b in range(8):
+    SCRATCH["pb%d" % _b] = ("psum", [128, 512], f32)
+
+SEMAPHORES = (["eV", "eS", "eP", "eG", "loc", "dst", "drs", "dac", "dpay", "dw0", "dw1", "dout"] + ["dar%d" % c for c in range(NCH)]
+              + ["a%s%d" % (s, j) for s in "orx" for j in range(4 * NP)])
+
+
+def reg(name, c0, c1, cs=1, p0=0, p1=128, ps=1):
+    cm = ((1 << (cs * len(range(c0, c1, cs)))) - 1) // ((1 << cs) - 1) << c0
+    pm = ((1 << (ps * len(range(p0, p1, ps)))) - 1) // ((1 << ps) - 1) << p0
+    return {"n": name, "c": (c0, c1, cs), "p": (p0, p1, ps), "cm": cm, "pm": pm, "w": len(range(c0, c1, cs))}
+
+
+def ap(T, r):
+    if not isinstance(r, dict):
+        return r
+    (c0, c1, cs), (p0, p1, ps) = r["c"], r["p"]
+    return T[r["n"]][slice(p0, p1) if ps == 1 else slice(p0, p1, ps), slice(c0, c1) if cs == 1 else slice(c0, c1, cs)]
+
+
+def two(r):
+    return SCRATCH[r["n"]][2] in (bf, u16, f16)
+
+
+def psum(r):
+    return SCRATCH[r["n"]][0] == "psum"
+
+
+def build():
+    ops = []
+    grp = [0, None]
+
+    def add(eng, emit, outs, ins, cost, **kw):
+        o = {"e": eng, "f": emit, "o": outs, "i": [x for x in ins if isinstance(x, dict)], "cost": cost, "id": len(ops), "x": [], "part": grp[0]}
+        o.update(kw)
+        ops.append(o)
+        return o
+
+    def vc(n):
+        return FIX + max(64, n) * CYC
+
+    def half(rs):
+        return 0.5 if all(two(r) for r in rs) else 1.0
+
+    def ts(out, in0, s1, s2, op0, op1=None):
+        def f(g, T):
+            if op1 is None:
+                return g.vector.tensor_scalar(ap(T, out), ap(T, in0), ap(T, s1), None, op0)
+            return g.vector.tensor_scalar(ap(T, out), ap(T, in0), ap(T, s1), ap(T, s2), op0, op1)
+        return add("V", f, [out], [in0, s1, s2], vc(out["w"] * half([out, in0])))
+
+    def tt(out, a, b, op, off=None):
+        if off:
+            return add("V", lambda g, T: g.vector.tensor_tensor(ap(T, out), ap(T, a).indirect(ap(T, off)), ap(T, b), op), [out], [a, b, off],
+                       50 + out["w"] * 1.56 * CYC, gat=out["w"])
+        return add("V", lambda g, T: g.vector.tensor_tensor(ap(T, out), ap(T, a), ap(T, b), op), [out], [a, b],
+                   vc(out["w"] * (1 if (psum(a) or psum(b)) else 2)))
+
+    def cp(out, a):
+        return add("V", lambda g, T: g.vector.tensor_copy(ap(T, out), ap(T, a)), [out], [a], vc(out["w"] * half([out, a])))
+
+    def scan(out, d0, d1, op0, op1):
+        return add("V", lambda g, T: g.vector.tensor_tensor_scan(ap(T, out), ap(T, d0), ap(T, d1), 0.0, op0, op1), [out], [d0, d1],
+                   vc(out["w"] * half([out, d0, d1])))
+
+    def tr(out, a):
+        return add("V", lambda g, T: g.vector.transpose(ap(T, out), ap(T, a)), [out], [a], vc(out["w"] * half([out, a])))
+
+    def ms(out, v):
+        return add("V", lambda g, T: g.vector.memset(ap(T, out), v), [out], [], vc(out["w"] * half([out])))
+
+    def act(out, a, func, bias=0.0, scale=1.0, off=None, extra=0.0):
+        def f(g, T):
+            src = ap(T, a).indirect(ap(T, off)) if off else ap(T, a)
+            if func == F.Copy:
+                return g.scalar.activation(ap(T, out), src, func)
+            return g.scalar.activation(ap(T, out), src, func, bias=ap(T, bias), scale=ap(T, scale))
+        return add("S", f, [out], [a, off, bias, scale], extra + ((65 + out["w"] * 1.56 * CYC) if off else vc(out["w"])), gat=out["w"] if off else 0)
+
+    def mm(out, l, r_, start, stop, acc=False):
+        o = add("P", lambda g, T, close=False: g.tensor.matmul(ap(T, out), ap(T, l), ap(T, r_), start, stop or close), [out], [l, r_],
+                max(64, out["w"]) * (1 if two(l) else 4) * PCY + 5, start=start, stop=stop, acc=acc)
+        if not acc and not start:
+            o["x"].append(grp[1])
+        grp[1] = o["id"]
+        return o
+
+    def iota(out, pat, base, cm):
+        def f(g, T):
+            if SCRATCH[out["n"]][2] == i32:
+                return g.iota(ap(T, out), pat, base, cm)
+            return g.iota(ap(T, out), pat, base, cm, allow_small_or_imprecise_dtypes=True)
+        return add("G", f, [out], [], 130 + 2 * out["w"] * CYC)
+
+    def sel(out, a, pat, op, fill, base, cm):
+        return add("G", lambda g, T: g.affine_select(ap(T, out), ap(T, a), pat, op, fill, base, cm), [out], [a], 170 + 2 * out["w"] * CYC)
+
+    def dma(q, sem, out, src, nbytes):
+        def f(g, T):
+            return (g.sync if q == "Y" else g.scalar).dma_start(ap(T, out) if isinstance(out, dict) else out(T),
+                                                                ap(T, src) if isinstance(src, dict) else src(T))
+        return add(q, f, [out] if isinstance(out, dict) else [], [src], 60, dma=sem, lat=1600 + nbytes / 180.0)
+
+    r = reg
+    blk = lambda n, j, w=128: r(n, w * j, w * j + w)
+    UF = 1024.0 if PE else 2.0 ** -12
+    UX = 1.0 if PE else UF
+    E12 = 2.0 ** -12
+    for c in range(NCH):
+        dma("Y", "dar%d" % c, blk("raw", c, CW), lambda T, c=c: T.arcs[:, c * CW:(c + 1) * CW], (c + 1) * 128 * CW * 4)
+    dma("S", "dst", r("sti", 0, 96), lambda T: T.st0[:, :], 49152)
+    ms(r("rsi", 0, L), 65)
+    for gq in range(8):
+        p = 16 * ((gq - 1) % 8)
+        dma("S", "drs", r("rsi", 0, L, 1, p, p + 12, 2), lambda T, gq=gq: T.rs0[gq, :], 49152)
+    dma("S", "dac", r("act", 0, L), lambda T: T.ac[:, :], 2 ** 20)
+    dma("Y", "dpay", r("payt", 0, W), lambda T: T.pay[:, :], 2 ** 21)
+    iota(r("val", 0, 16), [[0, 16]], -112, 1)
+    iota(r("val", 16, 144), [[-16, 8], [0, 16]], 0, 1)
+    iota(r("pi", 0, 1), [[0, 1]], 0, 1)
+    iota(r("col", 0, 136), [[1, 136]], -8, 0)
+    iota(r("vd", 0, 128), [[-2, 64], [0, 2]], 0, 1)
+    iota(r("one", 0, 128), [[0, 128]], 1, 0)
+    for b in range(2):
+        sel(blk("iw", b), r("one", 0, 128), [[-1, 128]], A.is_equal, 0.0, 0, 1)
+    ms(r("oneb", 0, 768), 1.0)
+    sel(r("selw", 0, 768), r("oneb", 0, 768), [[-2, 6], [-16, 8], [0, 16]], A.is_equal, 0.0, 0, 1)
+    valr = r("val", 0, 128)
+    for j in range(6):
+        ts(blk("ex", j), valr, float(2 * j), None, A.is_equal)
+    ts(blk("ex", 6), valr, 1.0, 128.0, A.is_equal, A.mult)
+    ts(blk("dl", 0), valr, 1.0, 1024.0, A.is_equal, A.mult)
+    tt(r("dl", 128, 896), r("ex", 0, 768), r("ex", 128, 896), A.subtract)
+    pcol = lambda j: r("pc", j, j + 1)
+    picol = lambda j: r("pi", j, j + 1)
+    ts(picol(1), picol(0), 0x70, None, A.bitwise_and)
+    ts(picol(2), picol(0), 1, None, A.bitwise_and)
+    ts(picol(3), picol(0), 15, None, A.bitwise_and)
+    ts(picol(5), picol(0), 4, 1, A.logical_shift_right, A.bitwise_and)
+    ts(pcol(0), picol(2), 6.0, 1.0, A.mult, A.add)
+    tt(pcol(1), pcol(0), picol(1), A.add)
+    ts(pcol(2), picol(3), 15.0, -1.0, A.not_equal, A.mult)
+    sk, ok, pad = (2.0 ** -14, -7.0, 2000.0) if PE else (UX, 1033.0, 4001.0 - 2 * E12)
+    ts(pcol(3), picol(3), ok, sk, A.add, A.mult)
+    ts(pcol(4), picol(3), 12.5, None, A.is_gt)
+    ts(pcol(10), picol(3), 0.5, pcol(4), A.is_lt, A.max)
+    ts(pcol(11), pcol(10), -1.0, 1.0, A.mult, A.add)
+    ts(pcol(12), pcol(10), pad * sk, None, A.mult)
+    ts(pcol(5), pcol(3), pcol(11), pcol(12), A.mult, A.add)
+    ts(pcol(6), picol(5), 0.0, None, A.is_equal)
+    ts(pcol(7), picol(5), 1.0, None, A.is_equal)
+    ts(pcol(8), picol(5), 0.0, 2048.0, A.is_equal, A.mult)
+    ts(pcol(9), picol(5), 1.0, 2048.0, A.is_equal, A.mult)
+    ts(r("self", 0, 136), r("col", 0, 136), pcol(1), UF / 2048, A.is_equal, A.mult)
+    ts(blk("tmpc", 0), valr, 1.0, -0.5 * UF, A.is_equal, A.mult)
+    ts(blk("tmpc", 1), valr, 3.0, UF * E12, A.is_equal, A.mult)
+    ms(blk("tmpc", 2), 0.0)
+    for x in range(1, 13):
+        act(r("tmpc", 256 + x, 384, 16), r("ex", 128 * ((x - 1) % 6) + x, 128 * ((x - 1) % 6) + 128, 16), F.Identity, scale=UF)
+    tt(blk("tmpc", 3), blk("tmpc", 0), blk("tmpc", 1), A.add)
+    tt(r("ra", 0, 128), blk("tmpc", 2), blk("tmpc", 3), A.add)
+    ts(blk("tmpc", 0), r("vd", 0, 128), 1.0, None, A.is_equal)
+    ts(blk("tmpc", 1), r("vd", 0, 128), -1.0, pcol(2), A.is_equal, A.mult)
+    tt(r("dm", 0, 128), blk("tmpc", 0), blk("tmpc", 1), A.add)
+    for c0 in range(2):
+        act(blk("iwp", c0, 256), r("iw", 0, 256), F.Identity, scale=pcol(8 + c0))
+        if PE:
+            ts(blk("iwm", c0, 256), r("iw", 0, 256), pcol(6 + c0), None, A.mult)
+        else:
+            act(blk("iwm", c0, 256), r("iw", 0, 256), F.Identity, scale=pcol(6 + c0))
+    if PE:
+        vx, vt = blk("vx", 0), blk("vx", 1)
+        iota(vx, [[-1, 128]], 0, 1)
+        sel(vx, vx, [[-16, 8], [0, 16]], A.is_ge, 99.0, -1, 1)
+        sel(vx, vx, [[16, 8], [0, 16]], A.is_ge, 99.0, 12, -1)
+        ts(vt, vx, 0.0, 12.0, A.is_lt, A.mult)
+        tt(vx, vx, vt, A.add)
+        for s in range(7):
+            ts(blk("shh", s), vx, float(s), None, A.is_equal)
+        for s in range(1, 7):
+            tt(blk("dsh", s - 1), blk("shh", 0), blk("shh", s), A.subtract)
+        ts(blk("dsh", 6), blk("iw", 0), 2.0 ** 14, None, A.mult)
+        ts(blk("dsh", 7), blk("iw", 0), 1.0 / UF, None, A.mult)
+        ts(blk("shb", 0), vx, 0.0, 4096.0, A.is_equal, A.mult)
+        ts(blk("shb", 6), vx, 0.0, -4096.0, A.is_equal, A.mult)
+        for s in range(1, 6):
+            ts(blk("shb", s), vx, float(12 - s), 4096.0, A.is_equal, A.mult)
+            if s <= 6 - VS:
+                tt(blk("rsh", s - 1), blk("shb", 0), blk("shb", s), A.subtract)
+        if VS:
+            ts(blk("rsh", 5), valr, 1.0, -0.125, A.is_equal, A.mult)
+    else:
+        ms(r("fkill", 0, 128), 1.0); ms(r("fkill", 0, 128, 16), 0.0); ms(r("fkill", 13, 128, 16), 0.0)
+        ms(r("zz", 0, 768), 0.0); ms(r("zz", 768, 1536), 0.0)
+    ms(r("mc", 6, 7 * L, 7), 4096.0)
+    ms(r("fmin", 0, 128), 0.0); ms(r("fmin", 0, 128, 16), 8192.0)
+    ms(r("fbc", 0, 128), 1.0); ms(r("fbc", 0, 128, 16), 0.0)
+    ms(r("fpar", 0, 128), -1.0); ms(r("fpar", 0, 128, 16), 0.0)
+    ms(r("fr", 0, 64), 1.0); ms(r("fr", 0, 64, 8), 0.0)
+    ms(r("zl", 0, L), 0.0)
+    ms(r("kr", 0, 128), 4096.0 * UX); ms(r("df", 0, 128, 16), 0.0); ms(r("rt", 0, L), 1.0); ms(r("zero", 0, 512), 0.0)
+    sums = []
+    cp(r("off0", 0, 96), r("sti", 0, 96))
+    cp(r("sf0", 0, 96), r("sti", 0, 96))
+    ts(r("rf0", 0, L), r("rsi", 0, L), -64.0, None, A.add)
+    for c in range(NCH):
+        a, b = c * CW, (c + 1) * CW
+        ts(r("lo", a, b), r("raw", a, b), 32767, None, A.bitwise_and)
+        ts(r("hi", a, b), r("raw", a, b), 15, None, A.logical_shift_right)
+        tt(r("mn", a, b), r("lo", a, b), r("hi", a, b), A.min)
+        if (c + 1) % (NCH // 2) == 0:
+            a = b - W // 2
+            for par in range(2):
+                for u, nm in enumerate(("lo", "hi")):
+                    dma("Y", "dw%d" % (a // (W // 2)), r("win", par * W + a, par * W + b, 1, u, 128, 2), r(nm, a, b, 1, par, 128, 2), 2 ** 20)
+
+    turn = [0, 0]
+    for t in range(V):
+        used = [0, 0]
+        for p in range(NP):
+            n, l0 = PARTS[p], sum(PARTS[:p])
+            grp[0] = p
+            e, m = n // 16, 6 * n // 16
+            j, jl = NP * t + p, NP * (t - 1) + p
+            H = lambda nm, a=0, b=n, s=1, w=1: r(nm, w * l0 + a, w * l0 + b, s)
+            M = lambda nm, a=0, b=m, s=1, tt_=0: r(nm, 96 * tt_ + 6 * l0 // 16 + a, 96 * tt_ + 6 * l0 // 16 + b, s)
+            Q = lambda nm, a=0, b=n // 2, s=1: r(nm, l0 // 2 + a, l0 // 2 + b, s)
+            nb = min(6, 512 // n)
+            pb, o0 = "pb%d" % (5 + p % 2), used[p % 2]
+            used[p % 2] += 2 * n + 2 * m
+            O = lambda a, b, s=1: r(pb, o0 + a, o0 + b, s)
+            Fp, Mp, pa, fx = O(0, n), O(n, 2 * n), 2 * n, 2 * n + m
+            if t == 0:
+                offk = lambda k: r("off0", 16 * k + l0 // 16, 16 * k + l0 // 16 + e)
+                rfin = lambda a, b: H("rf0", a, b)
+            else:
+                offk = lambda k: M("offl", e * k, e * k + e, 1, t - 1)
+                rfin = lambda a, b: r("rfl", L * (t - 1) + l0 + a, L * (t - 1) + l0 + b)
+                add("R", None, [M("offl", 0, m, 1, t - 1)], [], 0, recv="ao%d" % jl, after=("o", jl))
+                add("R", None, [rfin(0, n)], [], 0, recv="ar%d" % jl, after=("r", jl))
+                cp(M("sf"), M("offl", 0, m, 1, t - 1))
+            for k in range(K):
+                act(H("mc", k, 7 * n, 7, 7), r("mn", 0, W), F.Identity, bias=191.5 + E12, scale=1.0 / 2048, off=offk(k))
+            for a in range(0, n, 64):
+                b = min(n, a + 64)
+                bk = "pb%d" % (turn[0] % 2)
+                turn[0] += 1
+                for jj in range(7):
+                    mm(r(bk, jj, 7 * (b - a), 7), blk("dl", jj), rfin(a, b), True, True)
+                scan(H("scn", 7 * a, 7 * b, 1, 7), r(bk, 0, 7 * (b - a)), H("mc", 7 * a, 7 * b, 1, 7), A.add, A.min)
+            X, B = r("pb4", 2 * l0, 2 * l0 + n), r("pb4", 2 * l0 + n, 2 * l0 + 2 * n)
+            AC = H("act")
+            if PE:
+                AC, B = B, X
+                if t == 0:
+                    act(AC, H("act"), F.Copy)
+            tt(H("sc"), H("scn", 6, 7 * n, 7, 7), AC, A.add)
+            tr(H("xs"), H("sc"))
+            scan(H("ss"), r("fmin", 0, n), H("xs"), A.add, A.min)
+            cp(H("zl", 0, n, 16), H("ss", 15, n, 16))
+            scan(B, r("fbc", 0, n), H("zl"), A.mult, A.add)
+            tt(H("step"), H("ss"), B, A.is_equal)
+            scan(H("ps"), r("fpar", 0, n), H("step"), A.mult, A.add)
+            tr(H("stg"), H("step"))
+            for k in range(K):
+                if t == 0:
+                    mm(O(pa + e * k, pa + e * k + e), blk("iw", 0), r("sf0", 16 * k + l0 // 16, 16 * k + l0 // 16 + e), True, False)
+                elif k == 0:
+                    mm(O(pa, pa + m), blk("iw", 0), M("sf"), True, False)
+                for c0 in range(2):
+                    for h0 in range(2):
+                        o = 256 * c0 + (16 * (c0 - h0)) % 128
+                        last = mm(O(pa + e * k + c0, pa + e * k + e, 2), r("iwp", o, o + 128), H("ps", 15 + 16 * h0, n, 32), False,
+                                  c0 == 1 and h0 == 1 and (t == 0 or k == K - 1))
+            mk = mm(Mp, r("dm", 0, 128), H("stg"), True, True)
+            c2 = cp(M("off2"), O(pa, pa + m))
+            cm_ = [act(H("msk", n * b, n * b + n, 1, GK), Mp, F.Copy) for b in range(GK)]
+            mm(Fp, r("ra", 0, 128), rfin(0, n), True, False)["x"] += [c2["id"]] + [c["id"] for c in cm_]
+            for kk in range(0, K, GK):
+                tt(H("mg", n * kk, n * (kk + GK), 1, 6), r("win", 0, 2 * W), H("msk", 0, GK * n, 1, GK), A.mult, off=M("off2", e * kk, e * (kk + GK)))
+                for k in range(kk, kk + GK):
+                    mm(Fp, r("self", 8 - k, 136 - k), H("mg", n * k, n * k + n, 1, 6), False, k == K - 1)
+            CF, C1, C16 = 1.5 * 2.0 ** 23 * UF, 1.5 * 2.0 ** 23 * UX, 1.5 * 2.0 ** 27 * UX
+            ts(H("cc"), Fp, CF, CF, A.add, A.subtract)
+            if PE:
+                tt(H("dfr"), Fp, H("cc"), A.subtract)
+                ts(H("kf"), H("cc"), 2.0 ** -20, pcol(5), A.mult, A.add)
+                Xp = Mp
+                if nb == 6:
+                    b3 = "pb3" if p % 2 else "pb7"
+                else:
+                    b3, nb = "pb3", 6 - (VS or 3)
+                place = lambda s: r(b3, n * (s - 1), n * s) if s <= nb else r("pb7", n * (s - nb - 1), n * (s - nb))
+                onv = lambda s: VS and s > nb
+                for s in range(1, 7):
+                    mm(place(s), blk("dsh", s - 1), H("dfr"), True, False)
+                    if onv(s):
+                        mm(place(s), blk("rsh", 5), rfin(0, n), False, False)
+                    mm(place(s), blk("dsh", s - 1), H("kf"), False, True)
+                first = True
+                for v, bias in enumerate((0.0, -0.25, 0.25)):
+                    SG = lambda s0, s1: H("sg", n * (6 * v + s0), n * (6 * v + s1), 1, 18)
+                    top = 5 if v == 2 else 6
+                    act(SG(0, min(nb, top)), r(b3, 0, n * min(nb, top)), F.Sign, bias=bias)
+                    if top > nb and not onv(top):
+                        act(SG(nb, top), r("pb7", 0, n * (top - nb)), F.Sign, bias=bias)
+                    elif top > nb and v != 1:
+                        CQ = 1.5 * 2.0 ** 21
+                        ts(SG(nb, top), r("pb7", 0, n * (top - nb)), CQ, CQ - 0.125 * v, A.add, A.is_equal)
+                for v in range(3):
+                    top = 5 if v == 2 else 6
+                    for s in range(1, top + 1):
+                        pos = s - 1
+                        if onv(s) and v < 2:
+                            if v == 0:
+                                mm(Xp, blk("shb", 0), H("sg", n * pos, n * (pos + 1), 1, 18), first, False)
+                            continue
+                        lh = blk("shb", 6) if v == 1 else blk("shb", s) if v == 2 else blk("rsh", s - 1) if s < 6 else blk("shb", 0)
+                        mm(Xp, lh, H("sg", n * (6 * v + pos), n * (6 * v + pos + 1), 1, 18), first, False)
+                        first = False
+                mm(Xp, blk("dsh", 6), H("kf"), False, False)
+                mm(Xp, blk("dsh", 7), H("dfr"), False, True)
+                ts(H("xf"), Xp, 1900.5 - E12, None, A.min)
+                tr(X, H("xf"))
+                fin = 15
+                for k in range(K):
+                    scan(H("s1", n * k, n * k + n, 1, 6), r("fmin", 0, n), X, A.add, A.min)
+                    act(Q("kr", k, n // 2, 8), H("s1", n * k + fin, n * k + n, 16, 6), F.Copy)
+                    if k < K - 1:
+                        X1 = r("pb4", 2 * l0 + 1, 2 * l0 + n)
+                        tt(X1, X1, H("s1", n * k, n * k + n - 1, 1, 6), A.max)
+                ts(M("ka"), H("s1", fin, 6 * n, 16, 6), C1, C1, A.add, A.subtract)
+                tt(M("zd"), H("s1", fin, 6 * n, 16, 6), M("ka"), A.subtract)
+                frac = lambda h0: M("zd", h0, m, 2)
+            else:
+                ts(H("tt"), H("cc"), 15.0, pcol(5), A.mult, A.add)
+                tt(H("xf"), H("tt"), Fp, A.add)
+                tr(X, H("xf"))
+                ts(H("key"), X, C1, C1, A.add, A.subtract)
+                tt(H("dd"), X, H("key"), A.subtract)
+                for k in range(K):
+                    scan(H("s1"), r("fmin", 0, n), X, A.add, A.min)
+                    ts(Q("kr", k, n // 2, 8), H("s1", 15, n, 16), C1, C1, A.add, A.subtract)
+                    tt(H("zz", n * k, n * k + n, 16, 6), H("s1", 15, n, 16), Q("kr", k, n // 2, 8), A.subtract)
+                    if k < K - 1:
+                        scan(B, r("fkill", 0, n), H("zz", n * k, n * k + n, 1, 6), A.mult, A.add)
+                        tt(H("eq"), B, H("dd"), A.is_equal)
+                        tt(X, X, H("eq"), A.max)
+                frac = lambda h0: H("zz", 16 * h0, 6 * n, 32, 6)
+            for rot in ((1, 0) if t < V - 1 else (0,)):
+                base = fx if rot else pa
+                for c0 in range(2):
+                    for h0 in range(2):
+                        o = 256 * c0 + (16 * (c0 - h0 - rot)) % 128
+                        mm(O(base + c0, base + m, 2), r("iwm", o, o + 128), frac(h0), h0 == 0, h0 == 1)
+                dst = M("offs", 0, m, 1, t) if rot else M("offu")
+                ts(dst, O(base, base + m), 2048.0 / UX, 1023.5, A.mult, A.add)
+                if rot:
+                    add("G", None, [], [dst], ISSUE, send=("o", j), lat=LATS, to=M("offl", 0, m, 1, t))
+            ts(Q("c16"), Q("kr"), C16, C16, A.add, A.subtract)
+            tt(Q("df", 1), Q("c16", 1), Q("c16", 0, n // 2 - 1), A.subtract)
+            ts(Q("nn"), Q("c16"), (1500.0 if PE else 3000.0) * UX, None, A.is_le)
+            scan(Q("rw"), Q("df"), r("fr", 0, n // 2), A.add, A.mult)
+            ts(Q("qq"), Q("rw"), 1.0 / (16 * UX), -64.0, A.mult, A.add)
+            tt(H("rt", 0, n, 2), Q("qq"), Q("nn"), A.mult)
+            rfo = lambda a=0, b=n: r("rfs", L * t + l0 + a, L * t + l0 + b)
+            tr(rfo(), H("rt"))
+            if t < V - 1:
+                add("G", None, [], [rfo()], ISSUE, send=("r", j), lat=LATS, to=r("rfl", L * t + l0, L * t + l0 + n))
+            act(H("pg", 0, 6 * n, 1, 6), r("payt", 0, W), F.Copy, off=M("offu"))
+            XX = lambda a, b: r("xx", 6 * L * t + 6 * l0 + a, 6 * L * t + 6 * l0 + b)
+            kb = 6 if 6 * n <= 512 else 3
+            for b in range(0, K, kb):
+                bk = "pb2" if PE else "pb%d" % (2 + turn[1] % 2)
+                turn[1] += 1
+                for k in range(kb):
+                    mm(r(bk, n * k, n * k + n), blk("selw", b + k), rfo(), True, True)
+                act(r(bk, 0, n * kb), r(bk, 0, n * kb), F.Exp, bias=-8.0, scale=-0.125, extra=1300.0 if turn[1] == 1 else 0.0)
+                tt(XX(n * b, n * (b + kb)), H("pg", n * b, n * (b + kb), 1, 6), r(bk, 0, n * kb), A.mult)
+            rotm = r("iw", 16 * t, 16 * t + 128)
+            if t < V - 1:
+                LD = lambda b: r("land", 2 * L * t + 2 * l0 + n * b, 2 * L * t + 2 * l0 + n * b + n)
+                add("G", None, [], [XX(0, 6 * n)], ISSUE, send=("x", j), lat=LATX, srcs=[XX(n * k, n * k + n) for k in range(K)], to=[LD(0), LD(1)])
+                add("R", None, [LD(0), LD(1)], [], 0, recv="ax%d" % j, after=("x", j))
+                sums += [(r("pb0", L * b + l0, L * b + l0 + n), rotm, LD(b)) for b in range(2)]
+            else:
+                sums += [(r("pb0", l0, l0 + n), rotm, XX(n * k, n * k + n)) for k in range(K)]
+                MX = lambda a, b: H("mx", a * n, b * n, 1, 5)
+                tt(MX(0, 3), XX(0, 3 * n), XX(3 * n, 6 * n), A.max)
+                tt(MX(3, 4), MX(0, 1), MX(1, 2), A.max)
+                tt(MX(4, 5), MX(3, 4), MX(2, 3), A.max)
+                sums.append((r("pb0", L + l0, L + l0 + n), rotm, MX(4, 5)))
+    mm(r("pb0", 0, 512), r("zero", 0, 128), r("zero", 0, 512), True, False)
+    for out, l, x in sums:
+        mm(out, l, x, False, False, True)
+    act(r("outb", 0, 512), r("pb0", 0, 512), F.Copy)
+    dma("Y", "dout", lambda T: T.ys[:, :], r("outb", 0, 256), 2 ** 17)
+    dma("S", "dout", lambda T: T.ym[:, :], r("outb", 256, 512), 2 ** 17)
+    return ops
+
+
+def meet(a, b):
+    return a["cm"] & b["cm"] and a["pm"] & b["pm"]
+
+
+def plan():
+    ops = build()
+    n = len(ops)
+    hist, sends, groups = {}, {}, {}
+    for o in ops:
+        deps = set(o["x"])
+        for x in o["i"]:
+            deps.update(p for (p, y, w) in hist.get(x["n"], []) if w and meet(x, y))
+        for x in o["o"]:
+            deps.update(p for (p, y, w) in hist.get(x["n"], []) if meet(x, y) and not (o.get("acc") and ops[p].get("acc")))
+        for x in o["o"]:
+            if not o.get("acc"):
+                hist[x["n"]] = [e for e in hist.get(x["n"], []) if (e[1]["cm"] & ~x["cm"]) or (e[1]["pm"] & ~x["pm"])]
+            hist.setdefault(x["n"], []).append((o["id"], x, True))
+        for x in o["i"]:
+            hist.setdefault(x["n"], []).append((o["id"], x, False))
+        if "send" in o:
+            sends[o["send"]] = o["id"]
+        if "after" in o:
+            deps.add(sends[o["after"]])
+        if "dma" in o:
+            groups.setdefault(o["dma"], []).append(o["id"])
+        deps.discard(o["id"])
+        o["d"] = deps
+        o["banks"] = set(x["n"] for x in o["i"] + o["o"] if psum(x))
+    for o in ops:
+        for p in list(o["d"]):
+            if "dma" in ops[p] and o.get("dma") != ops[p]["dma"]:
+                o["d"].update(groups[ops[p]["dma"]])
+    succ = [[] for _ in range(n)]
+    for o in ops:
+        for p in o["d"]:
+            succ[p].append(o["id"])
+
+    def gap(p, o):
+        if p["e"] == "P" and o["e"] == "P":
+            return 0.0
+        return SAME if p["e"] == o["e"] else CROSS
+    order, left = [], [len(o["d"]) for o in ops]
+    st = [o["id"] for o in ops if not o["d"]]
+    while st:
+        a = st.pop()
+        order.append(a)
+        for s in succ[a]:
+            left[s] -= 1
+            if left[s] == 0:
+                st.append(s)
+    pr = [0.0] * n
+    for a in reversed(order):
+        o = ops[a]
+        pr[a] = o["cost"] + o.get("lat", 0.0) + max([pr[s] + gap(o, ops[s]) for s in succ[a]] + [0.0])
+    rng = np.random.default_rng(SEED)
+    pr = [pr[a] - STAG * ops[a]["part"] + NOISE * float(rng.random()) for a in range(n)]
+    free, bank, opened = {}, {}, set()
+    end, rdy = [0.0] * n, [0.0] * n
+    left = [len(o["d"]) for o in ops]
+    ready = [o["id"] for o in ops if not o["d"]]
+    seq = []
+    while ready:
+        est = {}
+        for a in ready:
+            o = ops[a]
+            if o.get("start") and o["o"][0]["n"] in opened:
+                continue
+            s = max(rdy[a], free.get(o["e"], 0.0))
+            for b in o["banks"]:
+                for e2, t2 in bank.get(b, {}).items():
+                    if e2 != o["e"]:
+                        s = max(s, t2 + CROSS)
+            est[a] = s
+        a0 = min(est, key=lambda a: est[a])
+        e = ops[a0]["e"]
+        a = max([c for c in est if ops[c]["e"] == e and est[c] <= est[a0] + LOOK], key=lambda c: pr[c])
+        a = max([c for c in est if ops[c]["e"] == e and est[c] <= est[a] + ALPHA * ops[a]["cost"]], key=lambda c: pr[c])
+        for c in est:
+            if ops[c]["e"] == "R":
+                a, e = c, "R"
+        o = ops[a]
+        ready.remove(a)
+        seq.append(a)
+        o["t0"] = est[a]
+        if o.get("start"):
+            opened.add(o["o"][0]["n"])
+        if o.get("stop"):
+            opened.discard(o["o"][0]["n"])
+        if e != "R":
+            free[e] = est[a] + o["cost"]
+        end[a] = est[a] + o["cost"] + o.get("lat", 0.0)
+        for b in o["banks"]:
+            bank.setdefault(b, {})[e] = est[a] + o["cost"]
+        for s in succ[a]:
+            rdy[s] = max(rdy[s], end[a] + gap(o, ops[s]))
+            left[s] -= 1
+            if left[s] == 0:
+                ready.append(s)
+    lastb = {}
+    for a in seq:
+        o = ops[a]
+        for b in o["banks"]:
+            o["d"].update(p for e2, p in lastb.get(b, {}).items() if e2 != o["e"])
+            lastb.setdefault(b, {})[o["e"]] = a
+    ops[[a for a in seq if ops[a].get("acc")][-1]]["close"] = True
+    return ops, seq, max(end)
+
+
+PLAN = []
+
+
+def helper_of(core, T, topo):
+    return [c for c in topo.cores_of(core) if T.rank_of(c) is None and topo.die(c) == topo.die(core)][0]
+
+
+def bits(engines):
+    return sum(1 << e for e in engines)
+
+
+def rank_program(g, core, T, topo):
+    rank = T.rank_of(core)
+    N = len(T.cores)
+    if rank is None:
+        for q in range(N):
+            if helper_of(T.cores[q], T, topo) == core:
+                for j in range(NP * (V - 1)):
+                    t, p = j // NP, j % NP
+                    owner = T.cores[(q - t) % N]
+                    rid, pid = topo.addr(owner, core)
+                    a = 2 * L * t + 2 * sum(PARTS[:p])
+                    g.wait_ge(T.sem["ao%d" % j], 8)
+                    g.remote_dma(T.land[:, a:a + 2 * PARTS[p]], T.land[:, a:a + 2 * PARTS[p]], T.sem["ax%d" % j], T.sem.loc,
+                                 pid, rid, bits(topo.engines(core, owner)[:8]))
+                g.wait_ge(T.sem.loc, 8 * NP * (V - 1))
+        return
+    if not PLAN:
+        PLAN.append(plan())
+    ops, seq, _ = PLAN[0]
+    nxt = T.cores[(rank + 1) % N]
+    hlp = helper_of(core, T, topo)
+    nrid, npid = topo.addr(nxt, core)
+    hrid, hpid = topo.addr(hlp, core)
+    en = topo.engines(core, nxt)[:8]
+    eh = [e for e in topo.engines(core, hlp) if e not in en]
+    queue = {"V": g.vector, "S": g.scalar, "P": g.tensor, "G": g, "Y": g.sync}
+    esem = {"V": "eV", "S": "eS", "P": "eP", "G": "eG"}
+    needed = set(p for o in ops for p in o["d"] if not (o["e"] == "P" and ops[p]["e"] == "P") and o["e"] != "R")
+    cnt, tok, waited = {}, {}, {}
+    loc = 0
+    for a in seq:
+        o = ops[a]
+        e = o["e"]
+        if e == "R":
+            tok[a] = (o["recv"], 8 if o["recv"][1] == "x" else 4)
+            cnt[o["recv"]] = tok[a][1]
+            continue
+        want = {}
+        for p in o["d"]:
+            if not (e == "P" and ops[p]["e"] == "P"):
+                want[tok[p][0]] = max(want.get(tok[p][0], 0), tok[p][1])
+        for s in sorted(want):
+            if waited.get((e, s), 0) < want[s]:
+                queue[e].wait_ge(T.sem[s], want[s])
+                waited[(e, s)] = want[s]
+        if "send" in o:
+            kind, j = o["send"]
+            if kind != "x":
+                g.remote_dma(ap(T, o["to"]), ap(T, o["i"][0]), T.sem["a%s%d" % (kind, j)], T.sem.loc, npid, nrid,
+                             bits(en[:4] if kind == "o" else en[4:]))
+                loc += 4
+            else:
+                g.remote_dma_fused([RemoteDMATransfer(dst_ids=[DstId(rid=hrid, pnc=hpid)], dma_engine_mask=bits(eh[4 * b:4 * b + 4]),
+                                                      remote_sem=T.sem["ao%d" % j], srcs=[ap(T, x) for x in o["srcs"]],
+                                                      dsts=[ap(T, o["to"][b])], alu_op=1 + b) for b in range(2)], local_sem=T.sem.loc)
+                loc += 8
+            continue
+        ins = o["f"](g, T, True) if o.get("close") else o["f"](g, T)
+        if "dma" in o:
+            s = o["dma"]
+            cnt[s] = cnt.get(s, 0) + 16
+            ins.then_inc(T.sem[s], 16)
+            tok[a] = (s, cnt[s])
+        elif a in needed:
+            s = esem[e]
+            cnt[s] = cnt.get(s, 0) + 1
+            ins.then_inc(T.sem[s], 1)
+            tok[a] = (s, cnt[s])
+    for s in sorted(cnt):
+        if max(waited.get((e, s), 0) for e in queue) < cnt[s]:
+            g.wait_ge(T.sem[s], cnt[s])
+    g.wait_ge(T.sem.loc, loc)

@@ -1,4 +1,3 @@
-import numpy as np
 from concourse.bass import DstId, RemoteDMATransfer
 from concourse.mybir import AluOpType as A, ActivationFunctionType as F
 
@@ -6,14 +5,21 @@ W, K, L, V = 2048, 6, 256, 5
 PARTS = [128, 128]
 PE = True
 VS = 2
+SUB = 64
+REP = 6
+KV = 0
 GK = 1
 NCH = 4
 CW = W // NCH
 NP = len(PARTS)
-CYC, PCY, FIX = 1.0, 0.5, 15.0
-SAME, CROSS, LOOK = 60.0, 120.0, 0.0
-STAG, ALPHA, NOISE, SEED = 0.0, 0.3, 0.0, 0
-LATS, LATX, ISSUE = 2300.0, 14000.0, 400.0
+CYC, PCY, FIX = 0.83, 0.55, 30.0
+SAME, CROSS, LOOK = 150.0, 280.0, 0.0
+ALPHA = 0.6
+BIAS = {'Vrsh0': 100.0, 'Vzl0': 1000.0, 'Smc0': 300.0, 'Ppb21': 700.0, 'Gval0': -100.0, 'Ppb30': -400.0, 'Spg1': -6500.0, 'Vmg1': -200.0,
+        'Vxx1': -1900.0, 'Vdm0': -600.0, 'Voffu0': -300.0, 'Voffs1': 600.0, 'Vmg0': -900.0, 'Siwp0': -400.0, 'Vscn1': -200.0, 'Vs11': 400.0,
+        'Vstep0': -3300.0, 'Smsk1': -800.0, 'Vsf1': 100.0, 'Vss0': 2500.0, 'Vstg0': 600.0, 'Gxx0': -2500.0, 'Vnn1': -2900.0, 'Vzl1': 3300.0,
+        'Vfr0': -2300.0}
+LATS, LATX, ISSUE = 3000.0, 14000.0, 400.0
 
 f32, bf, f16, i32, u16 = "float32", "bfloat16", "float16", "int32", "uint16"
 
@@ -35,7 +41,7 @@ SCRATCH = {
     "zl": _sb(L, f32), "step": _sb(L, bf), "ps": _sb(L, bf), "stg": _sb(L, bf), "msk": _sb(GK * L, f32),
     "sf": _sb(96, f32), "off2": _sb(96, u16), "mg": _sb(6 * L, f32), "cc": _sb(L, bf if PE else f32), "tt": _sb(L, f32),
     "xf": _sb(L, f32), "key": _sb(L, f32), "dd": _sb(L, f32), "s1": _sb(6 * L, f32), "eq": _sb(L, f32),
-    "kf": _sb(L, f16), "dfr": _sb(L, f16), "sg": _sb(18 * L, bf), "zd": _sb(96, f16), "ka": _sb(96, f32),
+    "kf": _sb(L, f16), "dfr": _sb(L, f16), "sg": _sb(18 * L, bf), "zd": _sb(96, f16), "p6": _sb(96, bf), "ka": _sb(96, f32),
     "zz": _sb(6 * L, f32), "kr": _sb(128, f32), "c16": _sb(128, f32), "df": _sb(128, f32), "rw": _sb(128, f32),
     "qq": _sb(128, f32), "nn": _sb(128, f32), "rt": _sb(L, bf), "offu": _sb(96, u16),
     "pg": _sb(6 * L, bf), "mx": _sb(5 * L, f32), "outb": _sb(512, f32),
@@ -283,8 +289,11 @@ def build():
                 add("R", None, [M("offl", 0, m, 1, t - 1)], [], 0, recv="ao%d" % jl, after=("o", jl))
                 add("R", None, [rfin(0, n)], [], 0, recv="ar%d" % jl, after=("r", jl))
                 cp(M("sf"), M("offl", 0, m, 1, t - 1))
-            for k in range(K):
-                act(H("mc", k, 7 * n, 7, 7), r("mn", 0, W), F.Identity, bias=191.5 + E12, scale=1.0 / 2048, off=offk(k))
+            for a in range(0, n, SUB):
+                for k in range(K):
+                    c0 = offk(k)["c"][0] + a // 16
+                    act(H("mc", 7 * a + k, 7 * min(n, a + SUB), 7, 7), r("mn", 0, W), F.Identity, bias=191.5 + E12, scale=1.0 / 2048,
+                        off=r(offk(k)["n"], c0, c0 + (min(n, a + SUB) - a) // 16))
             for a in range(0, n, 64):
                 b = min(n, a + 64)
                 bk = "pb%d" % (turn[0] % 2)
@@ -304,22 +313,26 @@ def build():
             cp(H("zl", 0, n, 16), H("ss", 15, n, 16))
             scan(B, r("fbc", 0, n), H("zl"), A.mult, A.add)
             tt(H("step"), H("ss"), B, A.is_equal)
-            scan(H("ps"), r("fpar", 0, n), H("step"), A.mult, A.add)
+            lastps = scan(H("ps"), r("fpar", 0, n), H("step"), A.mult, A.add)
             tr(H("stg"), H("step"))
-            for k in range(K):
+            PA = lambda a, b, s=1: r("pb%d" % (p % 2), 448 + a, 448 + b, s)
+            rep = REP if t else 1
+            for k in range(rep if rep > 1 else 0):
+                act(M("p6", e * k, e * k + e), H("ps", 15, n, 16), F.Copy)
+            for k in range(0, K, rep):
                 if t == 0:
-                    mm(O(pa + e * k, pa + e * k + e), blk("iw", 0), r("sf0", 16 * k + l0 // 16, 16 * k + l0 // 16 + e), True, False)
+                    mm(PA(e * k, e * k + e), blk("iw", 0), r("sf0", 16 * k + l0 // 16, 16 * k + l0 // 16 + e), True, False)["x"].append(lastps["id"])
                 elif k == 0:
-                    mm(O(pa, pa + m), blk("iw", 0), M("sf"), True, False)
+                    mm(PA(0, m), blk("iw", 0), M("sf"), True, False)["x"].append(lastps["id"])
                 for c0 in range(2):
                     for h0 in range(2):
                         o = 256 * c0 + (16 * (c0 - h0)) % 128
-                        last = mm(O(pa + e * k + c0, pa + e * k + e, 2), r("iwp", o, o + 128), H("ps", 15 + 16 * h0, n, 32), False,
-                                  c0 == 1 and h0 == 1 and (t == 0 or k == K - 1))
-            mk = mm(Mp, r("dm", 0, 128), H("stg"), True, True)
-            c2 = cp(M("off2"), O(pa, pa + m))
+                        mm(PA(e * k + c0, e * (k + rep), 2), r("iwp", o, o + 128), H("ps", 15 + 16 * h0, n, 32) if rep == 1 else M("p6", h0, e * rep, 2),
+                           False, c0 == 1 and h0 == 1 and (t == 0 or k == K - rep))
+            mm(Mp, r("dm", 0, 128), H("stg"), True, True)
+            c2 = cp(M("off2"), PA(0, m))
             cm_ = [act(H("msk", n * b, n * b + n, 1, GK), Mp, F.Copy) for b in range(GK)]
-            mm(Fp, r("ra", 0, 128), rfin(0, n), True, False)["x"] += [c2["id"]] + [c["id"] for c in cm_]
+            mm(Fp, r("ra", 0, 128), rfin(0, n), True, False)["x"] += [c["id"] for c in cm_]
             for kk in range(0, K, GK):
                 tt(H("mg", n * kk, n * (kk + GK), 1, 6), r("win", 0, 2 * W), H("msk", 0, GK * n, 1, GK), A.mult, off=M("off2", e * kk, e * (kk + GK)))
                 for k in range(kk, kk + GK):
@@ -369,7 +382,10 @@ def build():
                 fin = 15
                 for k in range(K):
                     scan(H("s1", n * k, n * k + n, 1, 6), r("fmin", 0, n), X, A.add, A.min)
-                    act(Q("kr", k, n // 2, 8), H("s1", n * k + fin, n * k + n, 16, 6), F.Copy)
+                    if k < K - KV:
+                        act(Q("kr", k, n // 2, 8), H("s1", n * k + fin, n * k + n, 16, 6), F.Copy)
+                    else:
+                        cp(Q("kr", k, n // 2, 8), H("s1", n * k + fin, n * k + n, 16, 6))
                     if k < K - 1:
                         X1 = r("pb4", 2 * l0 + 1, 2 * l0 + n)
                         tt(X1, X1, H("s1", n * k, n * k + n - 1, 1, 6), A.max)
@@ -443,6 +459,10 @@ def build():
     return ops
 
 
+def kind(o):
+    return "%s%s%d" % (o["e"], (o["o"] or o["i"])[0]["n"], o["part"])
+
+
 def meet(a, b):
     return a["cm"] & b["cm"] and a["pm"] & b["pm"]
 
@@ -498,8 +518,7 @@ def plan():
     for a in reversed(order):
         o = ops[a]
         pr[a] = o["cost"] + o.get("lat", 0.0) + max([pr[s] + gap(o, ops[s]) for s in succ[a]] + [0.0])
-    rng = np.random.default_rng(SEED)
-    pr = [pr[a] - STAG * ops[a]["part"] + NOISE * float(rng.random()) for a in range(n)]
+    pr = [pr[a] + BIAS.get(kind(ops[a]), 0.0) for a in range(n)]
     free, bank, opened = {}, {}, set()
     end, rdy = [0.0] * n, [0.0] * n
     left = [len(o["d"]) for o in ops]
@@ -597,7 +616,7 @@ def rank_program(g, core, T, topo):
         o = ops[a]
         e = o["e"]
         if e == "R":
-            tok[a] = (o["recv"], 8 if o["recv"][1] == "x" else 4)
+            tok[a] = (o["recv"], 8)
             cnt[o["recv"]] = tok[a][1]
             continue
         want = {}
@@ -612,8 +631,8 @@ def rank_program(g, core, T, topo):
             kind, j = o["send"]
             if kind != "x":
                 g.remote_dma(ap(T, o["to"]), ap(T, o["i"][0]), T.sem["a%s%d" % (kind, j)], T.sem.loc, npid, nrid,
-                             bits(en[:4] if kind == "o" else en[4:]))
-                loc += 4
+                             bits(en))
+                loc += 8
             else:
                 g.remote_dma_fused([RemoteDMATransfer(dst_ids=[DstId(rid=hrid, pnc=hpid)], dma_engine_mask=bits(eh[4 * b:4 * b + 4]),
                                                       remote_sem=T.sem["ao%d" % j], srcs=[ap(T, x) for x in o["srcs"]],

@@ -1,27 +1,24 @@
+import numpy as np
 from concourse.bass import DstId, RemoteDMATransfer
 from concourse.mybir import AluOpType as A, ActivationFunctionType as F
 
 W, K, L, V = 2048, 6, 256, 5
 PARTS = [128, 128]
-PE = True
-VS = 2
+VS = 1
 SUB = 64
 REP = 6
-KV = 0
-GK = 1
+GP = 3
 NCH = 4
 CW = W // NCH
 NP = len(PARTS)
 CYC, PCY, FIX = 0.83, 0.55, 30.0
 SAME, CROSS, LOOK = 150.0, 280.0, 0.0
 ALPHA = 0.6
-BIAS = {'Vrsh0': 100.0, 'Vzl0': 1000.0, 'Smc0': 300.0, 'Ppb21': 700.0, 'Gval0': -100.0, 'Ppb30': -400.0, 'Spg1': -6500.0, 'Vmg1': -200.0,
-        'Vxx1': -1900.0, 'Vdm0': -600.0, 'Voffu0': -300.0, 'Voffs1': 600.0, 'Vmg0': -900.0, 'Siwp0': -400.0, 'Vscn1': -200.0, 'Vs11': 400.0,
-        'Vstep0': -3300.0, 'Smsk1': -800.0, 'Vsf1': 100.0, 'Vss0': 2500.0, 'Vstg0': 600.0, 'Gxx0': -2500.0, 'Vnn1': -2900.0, 'Vzl1': 3300.0,
-        'Vfr0': -2300.0}
+BIAS = {}
 LATS, LATX, ISSUE = 3000.0, 14000.0, 400.0
 
 f32, bf, f16, i32, u16 = "float32", "bfloat16", "float16", "int32", "uint16"
+LP = L + 16 * NP
 
 
 def _sb(n, d):
@@ -29,23 +26,23 @@ def _sb(n, d):
 
 
 SCRATCH = {
-    "raw": _sb(W, i32), "lo": _sb(W, i32), "hi": _sb(W, i32), "mn": _sb(W, f32), "win": _sb(2 * W, i32),
-    "payt": _sb(W, bf), "act": _sb(L, f32), "sti": _sb(96, i32), "rsi": _sb(L, i32),
-    "off0": _sb(96, u16), "sf0": _sb(96, f32), "rf0": _sb(L, bf),
-    "val": _sb(144, bf), "vx": _sb(256, bf), "vd": _sb(128, bf), "col": _sb(136, f32), "pi": _sb(8, i32), "pc": _sb(16, f32),
-    "ex": _sb(7 * 128, bf), "dl": _sb(7 * 128, bf), "one": _sb(128, f32), "oneb": _sb(768, bf), "selw": _sb(768, bf), "self": _sb(136, f32),
-    "ra": _sb(128, bf), "tmpc": _sb(512, bf), "dm": _sb(128, bf), "iw": _sb(256, f32), "iwm": _sb(512, f16 if PE else f32), "iwp": _sb(512, bf),
-    "shh": _sb(7 * 128, f16), "dsh": _sb(8 * 128, f16), "shb": _sb(7 * 128, bf), "rsh": _sb(6 * 128, bf),
-    "fmin": _sb(128, f32), "fbc": _sb(128, f32), "fkill": _sb(128, f32), "fpar": _sb(128, bf), "fr": _sb(64, f32), "zero": _sb(512, bf),
-    "mc": _sb(7 * L, bf), "scn": _sb(7 * L, f32), "sc": _sb(L, f32), "xs": _sb(L, f32), "ss": _sb(L, f32),
-    "zl": _sb(L, f32), "step": _sb(L, bf), "ps": _sb(L, bf), "stg": _sb(L, bf), "msk": _sb(GK * L, f32),
-    "sf": _sb(96, f32), "off2": _sb(96, u16), "mg": _sb(6 * L, f32), "cc": _sb(L, bf if PE else f32), "tt": _sb(L, f32),
-    "xf": _sb(L, f32), "key": _sb(L, f32), "dd": _sb(L, f32), "s1": _sb(6 * L, f32), "eq": _sb(L, f32),
-    "kf": _sb(L, f16), "dfr": _sb(L, f16), "sg": _sb(18 * L, bf), "zd": _sb(96, f16), "p6": _sb(96, bf), "ka": _sb(96, f32),
-    "zz": _sb(6 * L, f32), "kr": _sb(128, f32), "c16": _sb(128, f32), "df": _sb(128, f32), "rw": _sb(128, f32),
-    "qq": _sb(128, f32), "nn": _sb(128, f32), "rt": _sb(L, bf), "offu": _sb(96, u16),
-    "pg": _sb(6 * L, bf), "mx": _sb(5 * L, f32), "outb": _sb(512, f32),
-    "offs": _sb(4 * 96, u16), "offl": _sb(4 * 96, u16), "rfs": _sb(5 * L, bf), "rfl": _sb(4 * L, bf),
+    "raw": _sb(W, i32), "lo": _sb(W, i32), "hi": _sb(W, i32), "mn": _sb(W, f32), "mnb": _sb(W, bf), "win": _sb(2 * W, i32),
+    "payt": _sb(W, bf), "act": _sb(L, f32), "sti": ("sbuf", [128, K, 16], i32), "rsi": _sb(L, i32),
+    "sf0": _sb(96, f16), "rf0": _sb(L, bf),
+    "val": _sb(144, bf), "bm": _sb(144, bf), "vd": _sb(128, bf), "col": _sb(136, f32), "pi": _sb(8, i32), "pc": _sb(16, f32),
+    "ee": _sb(16, f32), "cr": _sb(32, f32), "pq": _sb(96, f32), "yv": _sb(256, bf),
+    "rk": _sb(6 * 144, bf), "dl": _sb(6 * 128, bf), "one": _sb(128, f32), "self": _sb(136, f32),
+    "ra": _sb(128, bf), "tmpc": _sb(256, bf), "dm": _sb(128, bf), "iw": _sb(256, f32), "iwm": _sb(512, f16), "iwb": _sb(512, bf),
+    "idf": _sb(128, f16), "ccx": _sb(128, bf), "kla": _sb(640, bf), "klb": _sb(640, bf), "kl0": _sb(640, bf), "kls": _sb(128, bf),
+    "dct": _sb(640, bf), "dc": _sb(640, bf), "ddt": _sb(640, f16), "dd": _sb(640, f16),
+    "fss": _sb(128, f32), "fs1": _sb(128, f32), "frv": _sb(128, bf), "fpar": _sb(128, bf), "thr": _sb(64, f32), "f6": _sb(768, bf),
+    "zero": _sb(512, bf),
+    "mc0": _sb(8 * L, bf), "mc": _sb(7 * L, bf), "scn": _sb(8 * L, f32), "xs": _sb(LP, f32), "ge": _sb(LP, bf),
+    "step": _sb(L, bf), "ps": _sb(L, bf), "stg": _sb(L, bf), "msk": _sb(L, f32), "p6": _sb(96, bf),
+    "off1": _sb(96, u16), "off2": _sb(96, u16), "offu": _sb(96, u16), "mg": _sb(6 * L, f32), "cc": _sb(L, bf), "dfr": _sb(L, f16),
+    "sg": _sb(13 * L, bf), "xt": _sb(L, f32), "s1": _sb(6 * L + 16 * NP, f32), "ka": _sb(96, f32),
+    "kr": _sb(128, f32), "df": _sb(128, f32), "rt": _sb(L, bf), "ww": _sb(6 * L, f32), "mx": _sb(6 * L, f32), "outb": _sb(512, f32),
+    "zds": _sb(5 * 96, f16), "zdl": _sb(4 * 96, f16), "rfs": _sb(5 * L, bf), "rfl": _sb(4 * L, bf),
     "xx": _sb(30 * L, f32), "land": _sb(8 * L, f32),
 }
 for _b in range(8):
@@ -55,17 +52,28 @@ SEMAPHORES = (["eV", "eS", "eP", "eG", "loc", "dst", "drs", "dac", "dpay", "dw0"
               + ["a%s%d" % (s, j) for s in "orx" for j in range(4 * NP)])
 
 
+def bitmask(idx):
+    m = np.zeros(int(np.max(idx)) + 1, np.uint8)
+    m[idx] = 1
+    return int.from_bytes(np.packbits(m, bitorder="little").tobytes(), "little")
+
+
+def view(name, cols, part=slice(0, 128)):
+    shape = SCRATCH[name][1][1:]
+    idx = np.arange(int(np.prod(shape))).reshape(shape)[cols].ravel()
+    return {"n": name, "ix": (part,) + cols, "cm": bitmask(idx), "pm": bitmask(np.arange(128)[part]), "w": len(idx)}
+
+
 def reg(name, c0, c1, cs=1, p0=0, p1=128, ps=1):
-    cm = ((1 << (cs * len(range(c0, c1, cs)))) - 1) // ((1 << cs) - 1) << c0
-    pm = ((1 << (ps * len(range(p0, p1, ps)))) - 1) // ((1 << ps) - 1) << p0
-    return {"n": name, "c": (c0, c1, cs), "p": (p0, p1, ps), "cm": cm, "pm": pm, "w": len(range(c0, c1, cs))}
+    return view(name, (slice(c0, c1) if cs == 1 else slice(c0, c1, cs),), slice(p0, p1) if ps == 1 else slice(p0, p1, ps))
+
+
+def rev(name, c0, c1):
+    return view(name, (slice(c1 - 1, c0 - 1 if c0 else None, -1),))
 
 
 def ap(T, r):
-    if not isinstance(r, dict):
-        return r
-    (c0, c1, cs), (p0, p1, ps) = r["c"], r["p"]
-    return T[r["n"]][slice(p0, p1) if ps == 1 else slice(p0, p1, ps), slice(c0, c1) if cs == 1 else slice(c0, c1, cs)]
+    return T[r["n"]][r["ix"]] if isinstance(r, dict) else r
 
 
 def two(r):
@@ -130,9 +138,10 @@ def build():
     def mm(out, l, r_, start, stop, acc=False):
         o = add("P", lambda g, T, close=False: g.tensor.matmul(ap(T, out), ap(T, l), ap(T, r_), start, stop or close), [out], [l, r_],
                 max(64, out["w"]) * (1 if two(l) else 4) * PCY + 5, start=start, stop=stop, acc=acc)
-        if not acc and not start:
-            o["x"].append(grp[1])
-        grp[1] = o["id"]
+        if not acc:
+            if not start:
+                o["x"].append(grp[1])
+            grp[1] = o["id"]
         return o
 
     def iota(out, pat, base, cm):
@@ -153,120 +162,139 @@ def build():
 
     r = reg
     blk = lambda n, j, w=128: r(n, w * j, w * j + w)
-    UF = 1024.0 if PE else 2.0 ** -12
-    UX = 1.0 if PE else UF
-    E12 = 2.0 ** -12
+    E12, MAG, KILL = 2.0 ** -12, 1.5 * 2.0 ** 23, 4096.0
+    SENT = 1900.5 - E12
+    NS = 4 - VS
     for c in range(NCH):
         dma("Y", "dar%d" % c, blk("raw", c, CW), lambda T, c=c: T.arcs[:, c * CW:(c + 1) * CW], (c + 1) * 128 * CW * 4)
-    dma("S", "dst", r("sti", 0, 96), lambda T: T.st0[:, :], 49152)
-    ms(r("rsi", 0, L), 65)
+    dma("S", "dst", view("sti", (slice(0, K), slice(0, 16))), lambda T: T.st0[:, :], 49152)
+    ms(r("rsi", 0, L), 1)
     for gq in range(8):
         p = 16 * ((gq - 1) % 8)
         dma("S", "drs", r("rsi", 0, L, 1, p, p + 12, 2), lambda T, gq=gq: T.rs0[gq, :], 49152)
     dma("S", "dac", r("act", 0, L), lambda T: T.ac[:, :], 2 ** 20)
     dma("Y", "dpay", r("payt", 0, W), lambda T: T.pay[:, :], 2 ** 21)
+    iota(r("pi", 0, 1), [[0, 1]], 0, 1)
     iota(r("val", 0, 16), [[0, 16]], -112, 1)
     iota(r("val", 16, 144), [[-16, 8], [0, 16]], 0, 1)
-    iota(r("pi", 0, 1), [[0, 1]], 0, 1)
     iota(r("col", 0, 136), [[1, 136]], -8, 0)
-    iota(r("vd", 0, 128), [[-2, 64], [0, 2]], 0, 1)
     iota(r("one", 0, 128), [[0, 128]], 1, 0)
     for b in range(2):
         sel(blk("iw", b), r("one", 0, 128), [[-1, 128]], A.is_equal, 0.0, 0, 1)
-    ms(r("oneb", 0, 768), 1.0)
-    sel(r("selw", 0, 768), r("oneb", 0, 768), [[-2, 6], [-16, 8], [0, 16]], A.is_equal, 0.0, 0, 1)
-    valr = r("val", 0, 128)
-    for j in range(6):
-        ts(blk("ex", j), valr, float(2 * j), None, A.is_equal)
-    ts(blk("ex", 6), valr, 1.0, 128.0, A.is_equal, A.mult)
-    ts(blk("dl", 0), valr, 1.0, 1024.0, A.is_equal, A.mult)
-    tt(r("dl", 128, 896), r("ex", 0, 768), r("ex", 128, 896), A.subtract)
+    iota(r("vd", 0, 128), [[-2, 64], [0, 2]], 0, 1)
+    iota(blk("yv", 0), [[0, 8], [1, 16]], -7, 0)
     pcol = lambda j: r("pc", j, j + 1)
     picol = lambda j: r("pi", j, j + 1)
+    ecol = lambda j: r("ee", j, j + 1)
+    ccol = lambda j: r("cr", j, j + 1)
     ts(picol(1), picol(0), 0x70, None, A.bitwise_and)
     ts(picol(2), picol(0), 1, None, A.bitwise_and)
     ts(picol(3), picol(0), 15, None, A.bitwise_and)
     ts(picol(5), picol(0), 4, 1, A.logical_shift_right, A.bitwise_and)
+    cp(pcol(3), picol(3))
+    ts(r("bm", 0, 144), r("val", 0, 144), pcol(3), None, A.is_equal)
+    ts(r("ee", 0, 16), r("col", 8, 24), pcol(3), None, A.is_equal)
+    ts(pcol(4), ecol(13), 64.0, None, A.mult)
+    ts(r("cr", 25, 30), r("ee", 3, 12, 2), -64.0, pcol(4), A.mult, A.add)
+    tt(r("cr", 1, 6), r("ee", 2, 12, 2), r("cr", 25, 30), A.add)
+    cp(ccol(0), ecol(0))
+    ts(ccol(8), ecol(13), 1024.0, None, A.mult)
+    tt(r("cr", 9, 14), rev("cr", 1, 6), rev("cr", 0, 5), A.subtract)
+    ts(pcol(10), ecol(15), E12, None, A.mult)
+    ts(pcol(11), ecol(13), -64.5, pcol(10), A.mult, A.add)
+    ts(r("cr", 16, 22), r("cr", 0, 6), pcol(11), None, A.add)
+    for j in range(K):
+        act(blk("dl", j), r("bm", 0, 128), F.Identity, scale=ccol(8 + j))
+    for k in range(K):
+        act(blk("rk", k, 144), r("bm", 0, 144), F.Identity, scale=ccol(k))
+    ms(r("ra", 0, 128), 0.0)
+    for y in range(1, 15):
+        act(r("ra", y, 128, 16), r("bm", y, 128, 16), F.Identity, scale=ccol(16 + (y - 1) % 6) if y < 13 else ecol(13))
     ts(pcol(0), picol(2), 6.0, 1.0, A.mult, A.add)
     tt(pcol(1), pcol(0), picol(1), A.add)
     ts(pcol(2), picol(3), 15.0, -1.0, A.not_equal, A.mult)
-    sk, ok, pad = (2.0 ** -14, -7.0, 2000.0) if PE else (UX, 1033.0, 4001.0 - 2 * E12)
-    ts(pcol(3), picol(3), ok, sk, A.add, A.mult)
-    ts(pcol(4), picol(3), 12.5, None, A.is_gt)
-    ts(pcol(10), picol(3), 0.5, pcol(4), A.is_lt, A.max)
-    ts(pcol(11), pcol(10), -1.0, 1.0, A.mult, A.add)
-    ts(pcol(12), pcol(10), pad * sk, None, A.mult)
-    ts(pcol(5), pcol(3), pcol(11), pcol(12), A.mult, A.add)
     ts(pcol(6), picol(5), 0.0, None, A.is_equal)
     ts(pcol(7), picol(5), 1.0, None, A.is_equal)
-    ts(pcol(8), picol(5), 0.0, 2048.0, A.is_equal, A.mult)
-    ts(pcol(9), picol(5), 1.0, 2048.0, A.is_equal, A.mult)
-    ts(r("self", 0, 136), r("col", 0, 136), pcol(1), UF / 2048, A.is_equal, A.mult)
-    ts(blk("tmpc", 0), valr, 1.0, -0.5 * UF, A.is_equal, A.mult)
-    ts(blk("tmpc", 1), valr, 3.0, UF * E12, A.is_equal, A.mult)
-    ms(blk("tmpc", 2), 0.0)
-    for x in range(1, 13):
-        act(r("tmpc", 256 + x, 384, 16), r("ex", 128 * ((x - 1) % 6) + x, 128 * ((x - 1) % 6) + 128, 16), F.Identity, scale=UF)
-    tt(blk("tmpc", 3), blk("tmpc", 0), blk("tmpc", 1), A.add)
-    tt(r("ra", 0, 128), blk("tmpc", 2), blk("tmpc", 3), A.add)
+    ts(r("self", 0, 136), r("col", 0, 136), pcol(1), 1.0 / 2048, A.is_equal, A.mult)
     ts(blk("tmpc", 0), r("vd", 0, 128), 1.0, None, A.is_equal)
     ts(blk("tmpc", 1), r("vd", 0, 128), -1.0, pcol(2), A.is_equal, A.mult)
     tt(r("dm", 0, 128), blk("tmpc", 0), blk("tmpc", 1), A.add)
     for c0 in range(2):
-        act(blk("iwp", c0, 256), r("iw", 0, 256), F.Identity, scale=pcol(8 + c0))
-        if PE:
-            ts(blk("iwm", c0, 256), r("iw", 0, 256), pcol(6 + c0), None, A.mult)
-        else:
-            act(blk("iwm", c0, 256), r("iw", 0, 256), F.Identity, scale=pcol(6 + c0))
-    if PE:
-        vx, vt = blk("vx", 0), blk("vx", 1)
-        iota(vx, [[-1, 128]], 0, 1)
-        sel(vx, vx, [[-16, 8], [0, 16]], A.is_ge, 99.0, -1, 1)
-        sel(vx, vx, [[16, 8], [0, 16]], A.is_ge, 99.0, 12, -1)
-        ts(vt, vx, 0.0, 12.0, A.is_lt, A.mult)
-        tt(vx, vx, vt, A.add)
-        for s in range(7):
-            ts(blk("shh", s), vx, float(s), None, A.is_equal)
-        for s in range(1, 7):
-            tt(blk("dsh", s - 1), blk("shh", 0), blk("shh", s), A.subtract)
-        ts(blk("dsh", 6), blk("iw", 0), 2.0 ** 14, None, A.mult)
-        ts(blk("dsh", 7), blk("iw", 0), 1.0 / UF, None, A.mult)
-        ts(blk("shb", 0), vx, 0.0, 4096.0, A.is_equal, A.mult)
-        ts(blk("shb", 6), vx, 0.0, -4096.0, A.is_equal, A.mult)
-        for s in range(1, 6):
-            ts(blk("shb", s), vx, float(12 - s), 4096.0, A.is_equal, A.mult)
-            if s <= 6 - VS:
-                tt(blk("rsh", s - 1), blk("shb", 0), blk("shb", s), A.subtract)
-        if VS:
-            ts(blk("rsh", 5), valr, 1.0, -0.125, A.is_equal, A.mult)
-    else:
-        ms(r("fkill", 0, 128), 1.0); ms(r("fkill", 0, 128, 16), 0.0); ms(r("fkill", 13, 128, 16), 0.0)
-        ms(r("zz", 0, 768), 0.0); ms(r("zz", 768, 1536), 0.0)
+        act(blk("iwb", c0, 256), r("iw", 0, 256), F.Identity, scale=pcol(6 + c0))
+        cp(blk("iwm", c0, 256), blk("iwb", c0, 256))
+    cp(r("idf", 0, 128), blk("iw", 0))
+    pq = lambda j, a=0, b=5: r("pq", 8 * j + a, 8 * j + b)
+    ts(pq(0), r("col", 8, 88, 16), pcol(3), None, A.add)
+    ts(pq(0, 4, 5), picol(2), 64.0, None, A.add)
+    ts(pq(1), pq(0), 1.0 / 12, -11.0 / 24, A.mult, A.add)
+    ts(pq(2), pq(1), MAG, MAG, A.add, A.subtract)
+    ts(pq(3), pq(2), -12.0, None, A.mult)
+    tt(pq(4), pq(3), pq(0), A.add)
+    ts(pq(5), pq(2), 1.0, None, A.add)
+    tt(pq(6), pq(5), pq(4), A.add)
+    ts(pq(7), pq(6), 11.5, -12.0, A.is_gt, A.mult)
+    tt(pq(8), pq(6), pq(7), A.add)
+    tt(pq(9), pq(4), pq(8), A.subtract)
+    ts(pq(9), pq(9), 2.0 ** -14, None, A.mult)
+    ts(pcol(8), picol(1), 1.0, None, A.add)
+    ts(pq(10), pq(4), pcol(8), None, A.add)
+    ts(pq(11), pq(8), pcol(8), None, A.add)
+    ts(pcol(9), pcol(3), 5.5, KILL, A.is_lt, A.mult)
+    for b in range(5):
+        ts(blk("kla", b), r("col", 8, 136), pq(10, b, b + 1), KILL if b < 4 else pcol(9), A.is_equal, A.mult)
+        ts(blk("klb", b), r("col", 8, 136), pq(11, b, b + 1), KILL if b < 4 else pcol(9), A.is_equal, A.mult)
+        tt(blk("kl0", b), blk("kla", b), blk("klb", b), A.subtract)
+    tt(r("cr", 24, 27), r("ee", 0, 6, 2), r("ee", 1, 6, 2), A.add)
+    tt(pcol(12), ccol(24), ccol(25), A.subtract)
+    tt(pcol(13), ccol(26), ccol(24), A.subtract)
+    tt(pcol(14), ccol(26), ccol(25), A.subtract)
+    ts(pcol(14), pcol(14), 0.25, None, A.mult)
+    act(blk("tmpc", 0), blk("kla", 4), F.Identity, scale=pcol(12))
+    act(blk("tmpc", 1), blk("klb", 4), F.Identity, scale=pcol(13))
+    tt(r("kls", 0, 128), blk("tmpc", 0), blk("tmpc", 1), A.add)
+    ts(r("ddt", 0, 640), r("kl0", 0, 640), 1024.0 / KILL, None, A.mult)
+    tr(r("dd", 0, 640), r("ddt", 0, 640))
+    ts(r("dct", 0, 640), r("kl0", 0, 640), 2.0 ** -10 / KILL, None, A.mult)
+    for b in range(5):
+        act(r("dct", 128 * b + 13, 128 * b + 128, 16), r("bm", 16, 144, 16), F.Identity, scale=pq(9, b, b + 1))
+        if b >= NS:
+            act(r("dct", 128 * b + 14, 128 * b + 128, 16), r("bm", 16, 144, 16), F.Identity, scale=pcol(14) if b == 4 else -0.125)
+    tr(r("dc", 0, 640), r("dct", 0, 640))
+    tt(blk("yv", 1), blk("yv", 0), r("bm", 16, 144), A.mult)
+    act(blk("yv", 0), blk("yv", 1), F.Identity, scale=ecol(13))
+    act(blk("yv", 1), blk("iw", 0), F.Identity, scale=16.0)
+    tt(r("ccx", 0, 128), blk("yv", 0), blk("yv", 1), A.add)
+    ms(r("mc0", 0, 8 * L), 4096.0)
     ms(r("mc", 6, 7 * L, 7), 4096.0)
-    ms(r("fmin", 0, 128), 0.0); ms(r("fmin", 0, 128, 16), 8192.0)
-    ms(r("fbc", 0, 128), 1.0); ms(r("fbc", 0, 128, 16), 0.0)
-    ms(r("fpar", 0, 128), -1.0); ms(r("fpar", 0, 128, 16), 0.0)
-    ms(r("fr", 0, 64), 1.0); ms(r("fr", 0, 64, 8), 0.0)
-    ms(r("zl", 0, L), 0.0)
-    ms(r("kr", 0, 128), 4096.0 * UX); ms(r("df", 0, 128, 16), 0.0); ms(r("rt", 0, L), 1.0); ms(r("zero", 0, 512), 0.0)
-    sums = []
-    cp(r("off0", 0, 96), r("sti", 0, 96))
-    cp(r("sf0", 0, 96), r("sti", 0, 96))
-    ts(r("rf0", 0, L), r("rsi", 0, L), -64.0, None, A.add)
+    ms(r("fss", 0, 128), -1.0); ms(r("fss", 0, 128, 16), 8192.0)
+    ms(r("fs1", 0, 128), -8192.0); ms(r("fs1", 0, 128, 16), SENT)
+    ms(r("frv", 0, 128), 0.0); ms(r("frv", 15, 128, 16), 1.0)
+    ms(r("fpar", 0, 128), 1.0); ms(r("fpar", 0, 128, 2), -1.0)
+    ms(r("thr", 0, 64), MAG + 100); ms(r("thr", 0, 64, 8), -1.0); ms(r("thr", 6, 64, 8), 2 * MAG); ms(r("thr", 7, 64, 8), 2 * MAG)
+    ms(r("f6", 0, 768), 1.0); ms(r("f6", 0, 768, 6), 0.0)
+    ms(r("kr", 0, 128), MAG); ms(r("df", 0, 128), 0.0); ms(r("zero", 0, 512), 0.0)
+    for p in range(NP):
+        n, l0 = PARTS[p], sum(PARTS[:p])
+        ms(r("xs", l0 + 16 * p, l0 + 16 * p + 16), 0.0)
+        ms(r("ge", l0 + 16 * p + n, l0 + 16 * p + n + 16), 0.0)
+        ms(r("s1", 6 * l0 + 16 * p, 6 * l0 + 16 * p + 16), 0.0)
+        ms(r("ww", 6 * l0, 6 * l0 + n), 1.0)
+    ts(r("rf0", 0, L), r("rsi", 0, L), 0.0, None, A.add)
     for c in range(NCH):
         a, b = c * CW, (c + 1) * CW
         ts(r("lo", a, b), r("raw", a, b), 32767, None, A.bitwise_and)
         ts(r("hi", a, b), r("raw", a, b), 15, None, A.logical_shift_right)
         tt(r("mn", a, b), r("lo", a, b), r("hi", a, b), A.min)
+        act(r("mnb", a, b), r("mn", a, b), F.Identity, bias=191.5 + E12, scale=1.0 / 2048)
         if (c + 1) % (NCH // 2) == 0:
             a = b - W // 2
             for par in range(2):
                 for u, nm in enumerate(("lo", "hi")):
-                    dma("Y", "dw%d" % (a // (W // 2)), r("win", par * W + a, par * W + b, 1, u, 128, 2), r(nm, a, b, 1, par, 128, 2), 2 ** 20)
+                    o = (1 - par) * W
+                    dma("Y", "dw%d" % (a // (W // 2)), r("win", o + a, o + b, 1, u, 128, 2), r(nm, a, b, 1, par, 128, 2), 2 ** 20)
 
-    turn = [0, 0]
+    turn, sums = [0, 0], []
     for t in range(V):
-        used = [0, 0]
         for p in range(NP):
             n, l0 = PARTS[p], sum(PARTS[:p])
             grp[0] = p
@@ -275,185 +303,139 @@ def build():
             H = lambda nm, a=0, b=n, s=1, w=1: r(nm, w * l0 + a, w * l0 + b, s)
             M = lambda nm, a=0, b=m, s=1, tt_=0: r(nm, 96 * tt_ + 6 * l0 // 16 + a, 96 * tt_ + 6 * l0 // 16 + b, s)
             Q = lambda nm, a=0, b=n // 2, s=1: r(nm, l0 // 2 + a, l0 // 2 + b, s)
-            nb = min(6, 512 // n)
-            pb, o0 = "pb%d" % (5 + p % 2), used[p % 2]
-            used[p % 2] += 2 * n + 2 * m
-            O = lambda a, b, s=1: r(pb, o0 + a, o0 + b, s)
-            Fp, Mp, pa, fx = O(0, n), O(n, 2 * n), 2 * n, 2 * n + m
+            pb = "pb%d" % (5 + p % 2)
+            O = lambda a, b, s=1: r(pb, a, b, s)
+            Fp, Mp = O(0, n), O(128, 128 + n)
+
+            def turn_lists(out, src, mat, rot, first, last, w=m):
+                for c0 in range(2):
+                    for h0 in range(2):
+                        o = 256 * c0 + (16 * (c0 - h0 - rot)) % 128
+                        mm(out(c0, w, 2), r(mat, o, o + 128), src(h0), first and h0 == 0, (h0 == 1) if first else (last and c0 == 1 and h0 == 1))
+
             if t == 0:
-                offk = lambda k: r("off0", 16 * k + l0 // 16, 16 * k + l0 // 16 + e)
+                st3 = view("sti", (slice(0, K), slice(l0 // 16, l0 // 16 + e)))
+                cp(M("off1"), st3)
+                ts(M("sf0"), st3, 1.0 / 2048, -1023.5 / 2048, A.mult, A.add)
                 rfin = lambda a, b: H("rf0", a, b)
             else:
-                offk = lambda k: M("offl", e * k, e * k + e, 1, t - 1)
                 rfin = lambda a, b: r("rfl", L * (t - 1) + l0 + a, L * (t - 1) + l0 + b)
-                add("R", None, [M("offl", 0, m, 1, t - 1)], [], 0, recv="ao%d" % jl, after=("o", jl))
+                add("R", None, [M("zdl", 0, m, 1, t - 1)], [], 0, recv="ao%d" % jl, after=("o", jl))
                 add("R", None, [rfin(0, n)], [], 0, recv="ar%d" % jl, after=("r", jl))
-                cp(M("sf"), M("offl", 0, m, 1, t - 1))
+                zin = lambda h0: M("zdl", h0, m, 2, t - 1)
+                turn_lists(lambda a, b, s: O(256 + a, 256 + b, s), zin, "iwm", 1, True, True)
+                ts(M("off1"), O(256, 256 + m), 2048.0, 1023.5, A.mult, A.add)
+            cw = 8 if t == 0 else 7
+            mc = "mc0" if t == 0 else "mc"
             for a in range(0, n, SUB):
-                for k in range(K):
-                    c0 = offk(k)["c"][0] + a // 16
-                    act(H("mc", 7 * a + k, 7 * min(n, a + SUB), 7, 7), r("mn", 0, W), F.Identity, bias=191.5 + E12, scale=1.0 / 2048,
-                        off=r(offk(k)["n"], c0, c0 + (min(n, a + SUB) - a) // 16))
+                b = min(n, a + SUB)
+                for k in range(K - 1, -1, -1):
+                    act(H(mc, cw * a + 5 - k, cw * b, cw, cw), r("mnb", 0, W), F.Identity, bias=-192.0, off=M("off1", e * k + a // 16, e * k + b // 16))
             for a in range(0, n, 64):
                 b = min(n, a + 64)
                 bk = "pb%d" % (turn[0] % 2)
                 turn[0] += 1
-                for jj in range(7):
-                    mm(r(bk, jj, 7 * (b - a), 7), blk("dl", jj), rfin(a, b), True, True)
-                scan(H("scn", 7 * a, 7 * b, 1, 7), r(bk, 0, 7 * (b - a)), H("mc", 7 * a, 7 * b, 1, 7), A.add, A.min)
-            X, B = r("pb4", 2 * l0, 2 * l0 + n), r("pb4", 2 * l0 + n, 2 * l0 + 2 * n)
-            AC = H("act")
-            if PE:
-                AC, B = B, X
-                if t == 0:
-                    act(AC, H("act"), F.Copy)
-            tt(H("sc"), H("scn", 6, 7 * n, 7, 7), AC, A.add)
-            tr(H("xs"), H("sc"))
-            scan(H("ss"), r("fmin", 0, n), H("xs"), A.add, A.min)
-            cp(H("zl", 0, n, 16), H("ss", 15, n, 16))
-            scan(B, r("fbc", 0, n), H("zl"), A.mult, A.add)
-            tt(H("step"), H("ss"), B, A.is_equal)
-            lastps = scan(H("ps"), r("fpar", 0, n), H("step"), A.mult, A.add)
+                mm(r(bk, cw - 1, cw * (b - a), cw), blk("iw", 0), H("act", a, b), True, True)
+                for jj in range(cw - 1):
+                    mm(r(bk, jj, cw * (b - a), cw), blk("dl", jj) if jj < K else r("rk", 0, 128), rfin(a, b), True, True)
+                scan(H("scn", cw * a, cw * b, 1, 8), r(bk, 0, cw * (b - a)), H(mc, cw * a, cw * b, 1, cw), A.add, A.min)
+            x0 = l0 + 16 * p
+            SS = r("pb7", 256 + l0, 256 + l0 + n)
+            tr(r("xs", x0 + 16, x0 + 16 + n), H("scn", cw - 1, cw * n, cw, 8))
+            scan(SS, r("xs", x0 + 15, x0 + 15 + n), r("fss", 0, n), A.min, A.max)
+            tt(r("ge", x0, x0 + n), r("xs", x0 + 16, x0 + 16 + n), SS, A.is_ge)
+            lastps = scan(H("ps"), r("fpar", 0, n), r("ge", x0, x0 + n), A.add, A.mult)
+            scan(rev("step", l0, l0 + n), rev("ge", x0 + 1, x0 + 1 + n), rev("frv", 0, n), A.min, A.max)
             tr(H("stg"), H("step"))
-            PA = lambda a, b, s=1: r("pb%d" % (p % 2), 448 + a, 448 + b, s)
-            rep = REP if t else 1
-            for k in range(rep if rep > 1 else 0):
+            pab, pa0 = ("pb%d" % (p % 2), 448) if t else ("pb%d" % (2 + 2 * (p % 2)), 0)
+            PA = lambda a, b, s=1: r(pab, pa0 + a, pa0 + b, s)
+            for k in range(REP if REP > 1 else 0):
                 act(M("p6", e * k, e * k + e), H("ps", 15, n, 16), F.Copy)
-            for k in range(0, K, rep):
-                if t == 0:
-                    mm(PA(e * k, e * k + e), blk("iw", 0), r("sf0", 16 * k + l0 // 16, 16 * k + l0 // 16 + e), True, False)["x"].append(lastps["id"])
-                elif k == 0:
-                    mm(PA(0, m), blk("iw", 0), M("sf"), True, False)["x"].append(lastps["id"])
-                for c0 in range(2):
-                    for h0 in range(2):
-                        o = 256 * c0 + (16 * (c0 - h0)) % 128
-                        mm(PA(e * k + c0, e * (k + rep), 2), r("iwp", o, o + 128), H("ps", 15 + 16 * h0, n, 32) if rep == 1 else M("p6", h0, e * rep, 2),
-                           False, c0 == 1 and h0 == 1 and (t == 0 or k == K - rep))
-            mm(Mp, r("dm", 0, 128), H("stg"), True, True)
-            c2 = cp(M("off2"), PA(0, m))
-            cm_ = [act(H("msk", n * b, n * b + n, 1, GK), Mp, F.Copy) for b in range(GK)]
-            mm(Fp, r("ra", 0, 128), rfin(0, n), True, False)["x"] += [c["id"] for c in cm_]
-            for kk in range(0, K, GK):
-                tt(H("mg", n * kk, n * (kk + GK), 1, 6), r("win", 0, 2 * W), H("msk", 0, GK * n, 1, GK), A.mult, off=M("off2", e * kk, e * (kk + GK)))
-                for k in range(kk, kk + GK):
-                    mm(Fp, r("self", 8 - k, 136 - k), H("mg", n * k, n * k + n, 1, 6), False, k == K - 1)
-            CF, C1, C16 = 1.5 * 2.0 ** 23 * UF, 1.5 * 2.0 ** 23 * UX, 1.5 * 2.0 ** 27 * UX
-            ts(H("cc"), Fp, CF, CF, A.add, A.subtract)
-            if PE:
-                tt(H("dfr"), Fp, H("cc"), A.subtract)
-                ts(H("kf"), H("cc"), 2.0 ** -20, pcol(5), A.mult, A.add)
-                Xp = Mp
-                if nb == 6:
-                    b3 = "pb3" if p % 2 else "pb7"
-                else:
-                    b3, nb = "pb3", 6 - (VS or 3)
-                place = lambda s: r(b3, n * (s - 1), n * s) if s <= nb else r("pb7", n * (s - nb - 1), n * (s - nb))
-                onv = lambda s: VS and s > nb
-                for s in range(1, 7):
-                    mm(place(s), blk("dsh", s - 1), H("dfr"), True, False)
-                    if onv(s):
-                        mm(place(s), blk("rsh", 5), rfin(0, n), False, False)
-                    mm(place(s), blk("dsh", s - 1), H("kf"), False, True)
-                first = True
-                for v, bias in enumerate((0.0, -0.25, 0.25)):
-                    SG = lambda s0, s1: H("sg", n * (6 * v + s0), n * (6 * v + s1), 1, 18)
-                    top = 5 if v == 2 else 6
-                    act(SG(0, min(nb, top)), r(b3, 0, n * min(nb, top)), F.Sign, bias=bias)
-                    if top > nb and not onv(top):
-                        act(SG(nb, top), r("pb7", 0, n * (top - nb)), F.Sign, bias=bias)
-                    elif top > nb and v != 1:
-                        CQ = 1.5 * 2.0 ** 21
-                        ts(SG(nb, top), r("pb7", 0, n * (top - nb)), CQ, CQ - 0.125 * v, A.add, A.is_equal)
-                for v in range(3):
-                    top = 5 if v == 2 else 6
-                    for s in range(1, top + 1):
-                        pos = s - 1
-                        if onv(s) and v < 2:
-                            if v == 0:
-                                mm(Xp, blk("shb", 0), H("sg", n * pos, n * (pos + 1), 1, 18), first, False)
-                            continue
-                        lh = blk("shb", 6) if v == 1 else blk("shb", s) if v == 2 else blk("rsh", s - 1) if s < 6 else blk("shb", 0)
-                        mm(Xp, lh, H("sg", n * (6 * v + pos), n * (6 * v + pos + 1), 1, 18), first, False)
-                        first = False
-                mm(Xp, blk("dsh", 6), H("kf"), False, False)
-                mm(Xp, blk("dsh", 7), H("dfr"), False, True)
-                ts(H("xf"), Xp, 1900.5 - E12, None, A.min)
-                tr(X, H("xf"))
-                fin = 15
-                for k in range(K):
-                    scan(H("s1", n * k, n * k + n, 1, 6), r("fmin", 0, n), X, A.add, A.min)
-                    if k < K - KV:
-                        act(Q("kr", k, n // 2, 8), H("s1", n * k + fin, n * k + n, 16, 6), F.Copy)
-                    else:
-                        cp(Q("kr", k, n // 2, 8), H("s1", n * k + fin, n * k + n, 16, 6))
-                    if k < K - 1:
-                        X1 = r("pb4", 2 * l0 + 1, 2 * l0 + n)
-                        tt(X1, X1, H("s1", n * k, n * k + n - 1, 1, 6), A.max)
-                ts(M("ka"), H("s1", fin, 6 * n, 16, 6), C1, C1, A.add, A.subtract)
-                tt(M("zd"), H("s1", fin, 6 * n, 16, 6), M("ka"), A.subtract)
-                frac = lambda h0: M("zd", h0, m, 2)
+            if t == 0:
+                mm(PA(0, m), r("idf", 0, 128), M("sf0"), True, False)["x"].append(lastps["id"])
             else:
-                ts(H("tt"), H("cc"), 15.0, pcol(5), A.mult, A.add)
-                tt(H("xf"), H("tt"), Fp, A.add)
-                tr(X, H("xf"))
-                ts(H("key"), X, C1, C1, A.add, A.subtract)
-                tt(H("dd"), X, H("key"), A.subtract)
-                for k in range(K):
-                    scan(H("s1"), r("fmin", 0, n), X, A.add, A.min)
-                    ts(Q("kr", k, n // 2, 8), H("s1", 15, n, 16), C1, C1, A.add, A.subtract)
-                    tt(H("zz", n * k, n * k + n, 16, 6), H("s1", 15, n, 16), Q("kr", k, n // 2, 8), A.subtract)
-                    if k < K - 1:
-                        scan(B, r("fkill", 0, n), H("zz", n * k, n * k + n, 1, 6), A.mult, A.add)
-                        tt(H("eq"), B, H("dd"), A.is_equal)
-                        tt(X, X, H("eq"), A.max)
-                frac = lambda h0: H("zz", 16 * h0, 6 * n, 32, 6)
-            for rot in ((1, 0) if t < V - 1 else (0,)):
-                base = fx if rot else pa
-                for c0 in range(2):
-                    for h0 in range(2):
-                        o = 256 * c0 + (16 * (c0 - h0 - rot)) % 128
-                        mm(O(base + c0, base + m, 2), r("iwm", o, o + 128), frac(h0), h0 == 0, h0 == 1)
-                dst = M("offs", 0, m, 1, t) if rot else M("offu")
-                ts(dst, O(base, base + m), 2048.0 / UX, 1023.5, A.mult, A.add)
-                if rot:
-                    add("G", None, [], [dst], ISSUE, send=("o", j), lat=LATS, to=M("offl", 0, m, 1, t))
-            ts(Q("c16"), Q("kr"), C16, C16, A.add, A.subtract)
-            tt(Q("df", 1), Q("c16", 1), Q("c16", 0, n // 2 - 1), A.subtract)
-            ts(Q("nn"), Q("c16"), (1500.0 if PE else 3000.0) * UX, None, A.is_le)
-            scan(Q("rw"), Q("df"), r("fr", 0, n // 2), A.add, A.mult)
-            ts(Q("qq"), Q("rw"), 1.0 / (16 * UX), -64.0, A.mult, A.add)
-            tt(H("rt", 0, n, 2), Q("qq"), Q("nn"), A.mult)
+                mm(PA(0, m), r("zero", 0, 128), r("zero", 0, m), True, False)["x"].append(lastps["id"])
+                turn_lists(PA, zin, "iwm", 1, False, False)
+            for k in range(0, K, REP):
+                turn_lists(lambda a, b, s: PA(e * k + a, e * k + b, s), lambda h0: H("ps", 15 + 16 * h0, n, 32) if REP == 1 else M("p6", h0, e * REP, 2),
+                           "iwb", 0, False, k == K - REP, e * REP)
+            mm(Mp, r("dm", 0, 128), H("stg"), True, True)
+            ts(M("off2"), PA(0, m), 2048.0, 1023.5, A.mult, A.add)
+            cm_ = act(H("msk"), Mp, F.Copy)
+            mm(Fp, r("ra", 0, 128), rfin(0, n), True, False)["x"].append(cm_["id"])
+            for k in range(K):
+                tt(H("mg", n * k, n * (k + 1), 1, 6), r("win", 0, 2 * W), H("msk"), A.mult, off=M("off2", e * k, e * (k + 1)))
+                mm(Fp, r("self", 8 - k, 136 - k), H("mg", n * k, n * k + n, 1, 6), False, k == K - 1)
+            ts(H("cc"), Fp, MAG, MAG, A.add, A.subtract)
+            tt(H("dfr"), Fp, H("cc"), A.subtract)
+            order = list(range(NS, 4)) + list(range(NS)) + [4]
+            place = lambda b: r("pb7", n * (b - NS), n * (b - NS + 1)) if NS <= b < 4 else r("pb3", n * min(b, NS), n * min(b, NS) + n)
+            for b in order:
+                mm(place(b), blk("dc", b), H("cc"), True, False)
+                mm(place(b), blk("dd", b), H("dfr"), False, True)
+            SG = lambda a, b: H("sg", n * a, n * b, 1, 13)
+            CQ = 1.5 * 2.0 ** 21
+            kills = []
+            for v in range(2):
+                ts(SG(VS * v, VS * v + VS), r("pb7", 0, n * VS), CQ, CQ - 0.25 * v, A.add, A.is_equal)
+                kills += [(blk("klb" if v else "kla", NS + b), VS * v + b) for b in range(VS)]
+            s0 = 2 * VS
+            act(SG(s0, s0 + NS + 1), r("pb3", 0, n * (NS + 1)), F.Sign)
+            kills += [(blk("kl0", b), s0 + b) for b in range(NS)] + [(r("kls", 0, 128), s0 + NS)]
+            for v in range(2):
+                s1 = s0 + NS + 1 + NS * v
+                act(SG(s1, s1 + NS), r("pb3", 0, n * NS), F.Sign, bias=0.25, scale=1.0 if v else -1.0)
+                kills += [(blk("klb" if v else "kla", b), s1 + b) for b in range(NS)]
+            Xp = Mp
+            for i, (lh, s) in enumerate(kills):
+                mm(Xp, lh, SG(s, s + 1), i == 0, False)
+            mm(Xp, r("ccx", 0, 128), H("cc"), False, False)
+            mm(Xp, r("idf", 0, 128), H("dfr"), False, True)
+            tr(H("xt"), Xp)
+            sb = 6 * l0 + 16 * p + 16
+            S1 = lambda a, b, s=1: r("s1", sb + a, sb + b, s)
+            for k in range(K):
+                scan(S1(n * k, n * k + n), H("xt"), r("fs1", 0, n) if k == 0 else S1(n * k - n - 1, n * k - 1), A.min, A.max)
+                act(Q("kr", k, n // 2, 8), S1(n * k + 12, n * k + n, 16), F.Identity, bias=MAG, scale=1.0 / 16)
+            zd = lambda a=0, s=1: M("zds", a, m, s, t)
+            ts(M("ka"), S1(12, 6 * n, 16), MAG, MAG, A.add, A.subtract)
+            tt(zd(), S1(12, 6 * n, 16), M("ka"), A.subtract)
+            if t < V - 1:
+                add("G", None, [], [zd()], ISSUE, send=("o", j), lat=LATS, to=M("zdl", 0, m, 1, t))
+            turn_lists(lambda a, b, s: O(304 + a, 304 + b, s), lambda h0: zd(h0, 2), "iwm", 0, True, True)
+            ts(M("offu"), O(304, 304 + m), 2048.0, 1023.5, A.mult, A.add)
+            tt(Q("df", 1), Q("kr", 1), Q("kr", 0, n // 2 - 1), A.subtract)
+            tt(H("rt", 1, n, 2), Q("kr"), r("thr", 0, n // 2), A.is_lt)
+            scan(H("rt", 0, n, 2), Q("df"), H("rt", 1, n, 2), A.add, A.mult)
             rfo = lambda a=0, b=n: r("rfs", L * t + l0 + a, L * t + l0 + b)
             tr(rfo(), H("rt"))
             if t < V - 1:
                 add("G", None, [], [rfo()], ISSUE, send=("r", j), lat=LATS, to=r("rfl", L * t + l0, L * t + l0 + n))
-            act(H("pg", 0, 6 * n, 1, 6), r("payt", 0, W), F.Copy, off=M("offu"))
-            XX = lambda a, b: r("xx", 6 * L * t + 6 * l0 + a, 6 * L * t + 6 * l0 + b)
-            kb = 6 if 6 * n <= 512 else 3
-            for b in range(0, K, kb):
-                bk = "pb2" if PE else "pb%d" % (2 + turn[1] % 2)
+            for k0, k1 in ((1, 4), (4, 6)):
+                for k in range(k0, k1):
+                    mm(r("pb2", n * (k - k0), n * (k - k0 + 1)), r("rk", 144 * k + 16, 144 * k + 144), rfo(), True, True)
                 turn[1] += 1
-                for k in range(kb):
-                    mm(r(bk, n * k, n * k + n), blk("selw", b + k), rfo(), True, True)
-                act(r(bk, 0, n * kb), r(bk, 0, n * kb), F.Exp, bias=-8.0, scale=-0.125, extra=1300.0 if turn[1] == 1 else 0.0)
-                tt(XX(n * b, n * (b + kb)), H("pg", n * b, n * (b + kb), 1, 6), r(bk, 0, n * kb), A.mult)
+                act(H("ww", n * k0, n * k1, 1, 6), r("pb2", 0, n * (k1 - k0)), F.Exp, scale=-0.125, extra=1300.0 if turn[1] == 1 else 0.0)
+            XX = lambda a, b, s=1: r("xx", 6 * L * t + 6 * l0 + a, 6 * L * t + 6 * l0 + b, s)
             rotm = r("iw", 16 * t, 16 * t + 128)
             if t < V - 1:
+                for k in range(0, K, GP):
+                    tt(XX(n * k, n * (k + GP)), r("payt", 0, W), H("ww", n * k, n * (k + GP), 1, 6), A.mult, off=M("offu", e * k, e * (k + GP)))
                 LD = lambda b: r("land", 2 * L * t + 2 * l0 + n * b, 2 * L * t + 2 * l0 + n * b + n)
                 add("G", None, [], [XX(0, 6 * n)], ISSUE, send=("x", j), lat=LATX, srcs=[XX(n * k, n * k + n) for k in range(K)], to=[LD(0), LD(1)])
                 add("R", None, [LD(0), LD(1)], [], 0, recv="ax%d" % j, after=("x", j))
-                sums += [(r("pb0", L * b + l0, L * b + l0 + n), rotm, LD(b)) for b in range(2)]
+                sums += [(r("pb4", L * b + l0, L * b + l0 + n), rotm, LD(b)) for b in range(2)]
+                if j == NP - 1:
+                    mm(r("pb4", 0, 512), r("zero", 0, 128), r("zero", 0, 512), True, False)
+                while sums and j >= NP - 1:
+                    mm(*sums.pop(), False, False, True)
             else:
-                sums += [(r("pb0", l0, l0 + n), rotm, XX(n * k, n * k + n)) for k in range(K)]
-                MX = lambda a, b: H("mx", a * n, b * n, 1, 5)
-                tt(MX(0, 3), XX(0, 3 * n), XX(3 * n, 6 * n), A.max)
-                tt(MX(3, 4), MX(0, 1), MX(1, 2), A.max)
-                tt(MX(4, 5), MX(3, 4), MX(2, 3), A.max)
-                sums.append((r("pb0", L + l0, L + l0 + n), rotm, MX(4, 5)))
-    mm(r("pb0", 0, 512), r("zero", 0, 128), r("zero", 0, 512), True, False)
-    for out, l, x in sums:
-        mm(out, l, x, False, False, True)
-    act(r("outb", 0, 512), r("pb0", 0, 512), F.Copy)
+                for k in range(K):
+                    tt(XX(k, 6 * n, 6), r("payt", 0, W), H("ww", n * k, n * k + n, 1, 6), A.mult, off=M("offu", e * k, e * k + e))
+                    mm(r("pb4", l0, l0 + n), rotm, XX(k, 6 * n, 6), False, False, True)
+                scan(H("mx", 0, 6 * n, 1, 6), r("f6", 0, 6 * n), XX(0, 6 * n), A.mult, A.max)
+                mm(r("pb4", L + l0, L + l0 + n), rotm, H("mx", 5, 6 * n, 6, 6), False, False, True)
+    act(r("outb", 0, 512), r("pb4", 0, 512), F.Copy)
     dma("Y", "dout", lambda T: T.ys[:, :], r("outb", 0, 256), 2 ** 17)
     dma("S", "dout", lambda T: T.ym[:, :], r("outb", 256, 512), 2 ** 17)
     return ops

@@ -4,18 +4,41 @@ from concourse.mybir import AluOpType as A, ActivationFunctionType as F
 
 W, K, L, V = 2048, 6, 256, 5
 PARTS = [128, 128]
-VS = 1
-SUB = 64
-REP = 6
+VS = 2
+SUB = 128
+LATE = 0
+GV = [2, 0, 0, 0]
+MV = 1
+KO = 3
+SF = 0
+ZS = 0
+TS = 1
+MT = 0
+O1S = 1
+OUS = 1
+SPL = 0
+KV = 0
+W0 = 0
+ZC = "GG"
+XS = 1
+REP = 3
 GP = 3
 NCH = 4
 CW = W // NCH
 NP = len(PARTS)
-CYC, PCY, FIX = 0.83, 0.55, 30.0
+BANKS = {"own": [5, 6], "dif": [0, 1, 2], "par": [0, 1, 2], "st": [3], "vt": [7], "pay": [0, 1, 2], "fin": [3, 7]}
+PCY = 0.45
+CYC, FIX = 0.83, 30.0
 SAME, CROSS, LOOK = 150.0, 280.0, 0.0
 ALPHA = 0.6
-BIAS = {}
-LATS, LATX, ISSUE = 3000.0, 14000.0, 400.0
+STAG = 2000.0
+BIAS = {'Sra0': -3700, 'Pxx1': -9800, 'Pmg0': -300, 'Vs11': 4700, 'Pcc0': 8700, 'Gmc00': -3300, 'Vpq0': -9800, 'Vmg0': -2600, 'Pdfr0': 12600, 'Gval0': 16000, 'Gfss0': -3400, 'Pzdl0': 6800, 'Gdm0': -5800, 'Vmsk1': -10200, 'Gccx0': -2700, 'Pp61': 400, 'Voff21': -5700, 'Skla0': -1800, 'Vxx0': -1500, 'Gs10': 2700, 'Smc01': -2000, 'Vmc00': -15000, 'Vpb61': 1500, 'Sxx1': 5300}
+LATS = 3000.0
+LATX = 19000.0
+LATD = 11000.0
+DIRECT = 3
+ISSUE = 400.0
+BW = 180.0
 
 f32, bf, f16, i32, u16 = "float32", "bfloat16", "float16", "int32", "uint16"
 LP = L + 16 * NP
@@ -29,27 +52,27 @@ SCRATCH = {
     "raw": _sb(W, i32), "lo": _sb(W, i32), "hi": _sb(W, i32), "mn": _sb(W, f32), "mnb": _sb(W, bf), "win": _sb(2 * W, i32),
     "payt": _sb(W, bf), "act": _sb(L, f32), "sti": ("sbuf", [128, K, 16], i32), "rsi": _sb(L, i32),
     "sf0": _sb(96, f16), "rf0": _sb(L, bf),
-    "val": _sb(144, bf), "bm": _sb(144, bf), "vd": _sb(128, bf), "col": _sb(136, f32), "pi": _sb(8, i32), "pc": _sb(16, f32),
-    "ee": _sb(16, f32), "cr": _sb(32, f32), "pq": _sb(96, f32), "yv": _sb(256, bf),
+    "val": _sb(144, bf), "bm": _sb(144, bf), "cob": _sb(128, bf), "col": _sb(144, f32), "self0": _sb(144, f32), "dm0": _sb(128, bf), "pi": _sb(8, i32), "pc": _sb(16, f32),
+    "ee": _sb(16, f32), "cr": _sb(32, f32), "pq": _sb(96, f32),
     "rk": _sb(6 * 144, bf), "dl": _sb(6 * 128, bf), "one": _sb(128, f32), "self": _sb(136, f32),
-    "ra": _sb(128, bf), "tmpc": _sb(256, bf), "dm": _sb(128, bf), "iw": _sb(256, f32), "iwm": _sb(512, f16), "iwb": _sb(512, bf),
-    "idf": _sb(128, f16), "ccx": _sb(128, bf), "kla": _sb(640, bf), "klb": _sb(640, bf), "kl0": _sb(640, bf), "kls": _sb(128, bf),
-    "dct": _sb(640, bf), "dc": _sb(640, bf), "ddt": _sb(640, f16), "dd": _sb(640, f16),
+    "ra": _sb(128, bf), "tmpc": _sb(256, bf), "dm": _sb(128, bf), "iw": _sb(256, f32), "iwb": _sb(512, bf),
+    "idb": _sb(256, bf), "ccx": _sb(128, bf), "kla": _sb(640, bf), "klb": _sb(640, bf), "kl0": _sb(512, bf),
+    "dc": _sb(640, bf), "dd": _sb(640, bf), "accb": _sb(512, f32),
     "fss": _sb(128, f32), "fs1": _sb(128, f32), "frv": _sb(128, bf), "fpar": _sb(128, bf), "thr": _sb(64, f32), "f6": _sb(768, bf),
     "zero": _sb(512, bf),
     "mc0": _sb(8 * L, bf), "mc": _sb(7 * L, bf), "scn": _sb(8 * L, f32), "xs": _sb(LP, f32), "ge": _sb(LP, bf),
     "step": _sb(L, bf), "ps": _sb(L, bf), "stg": _sb(L, bf), "msk": _sb(L, f32), "p6": _sb(96, bf),
-    "off1": _sb(96, u16), "off2": _sb(96, u16), "offu": _sb(96, u16), "mg": _sb(6 * L, f32), "cc": _sb(L, bf), "dfr": _sb(L, f16),
+    "off1": _sb(96, u16), "off2": _sb(96, u16), "offu": _sb(96, u16), "mg": _sb(12 * L, f32), "cc": _sb(L, bf), "dfr": _sb(L, f16),
     "sg": _sb(13 * L, bf), "xt": _sb(L, f32), "s1": _sb(6 * L + 16 * NP, f32), "ka": _sb(96, f32),
-    "kr": _sb(128, f32), "df": _sb(128, f32), "rt": _sb(L, bf), "ww": _sb(6 * L, f32), "mx": _sb(6 * L, f32), "outb": _sb(512, f32),
+    "kr": _sb(128, f32), "df": _sb(128, f32), "rt": _sb(L, bf), "ww": _sb(6 * L, f32), "pg": _sb(6 * L, bf), "mx": _sb(6 * L, f32), "outb": _sb(512, f32),
     "zds": _sb(5 * 96, f16), "zdl": _sb(4 * 96, f16), "rfs": _sb(5 * L, bf), "rfl": _sb(4 * L, bf),
     "xx": _sb(30 * L, f32), "land": _sb(8 * L, f32),
 }
 for _b in range(8):
     SCRATCH["pb%d" % _b] = ("psum", [128, 512], f32)
 
-SEMAPHORES = (["eV", "eS", "eP", "eG", "loc", "dst", "drs", "dac", "dpay", "dw0", "dw1", "dout"] + ["dar%d" % c for c in range(NCH)]
-              + ["a%s%d" % (s, j) for s in "orx" for j in range(4 * NP)])
+SEMAPHORES = (["eV", "eS", "eP", "eG", "loc", "dst", "drs", "dac", "dpay", "dw0", "dw1", "dout"] + ["d%s%d" % (s, c) for s in ("ar", "wa", "wb") for c in range(NCH)]
+              + ["a%s%d" % (s, j) for s in "eorx" for j in range(4 * NP)])
 
 
 def bitmask(idx):
@@ -59,9 +82,11 @@ def bitmask(idx):
 
 
 def view(name, cols, part=slice(0, 128)):
+    loan = name if isinstance(name, dict) else None
+    name = "pb0" if loan else name
     shape = SCRATCH[name][1][1:]
     idx = np.arange(int(np.prod(shape))).reshape(shape)[cols].ravel()
-    return {"n": name, "ix": (part,) + cols, "cm": bitmask(idx), "pm": bitmask(np.arange(128)[part]), "w": len(idx)}
+    return {"n": name, "loan": loan, "key": loan["key"] if loan else name, "ix": (part,) + cols, "cm": bitmask(idx), "pm": bitmask(np.arange(128)[part]), "w": len(idx)}
 
 
 def reg(name, c0, c1, cs=1, p0=0, p1=128, ps=1):
@@ -72,8 +97,12 @@ def rev(name, c0, c1):
     return view(name, (slice(c1 - 1, c0 - 1 if c0 else None, -1),))
 
 
+def place_of(r):
+    return r["loan"]["bank"] if r["loan"] else r["n"]
+
+
 def ap(T, r):
-    return T[r["n"]][r["ix"]] if isinstance(r, dict) else r
+    return T[place_of(r)][r["ix"]] if isinstance(r, dict) else r
 
 
 def two(r):
@@ -86,10 +115,10 @@ def psum(r):
 
 def build():
     ops = []
-    grp = [0, None]
+    grp = [0, None, False]
 
     def add(eng, emit, outs, ins, cost, **kw):
-        o = {"e": eng, "f": emit, "o": outs, "i": [x for x in ins if isinstance(x, dict)], "cost": cost, "id": len(ops), "x": [], "part": grp[0]}
+        o = {"e": eng, "f": emit, "o": outs, "i": [x for x in ins if isinstance(x, dict)], "cost": cost, "id": len(ops), "x": [], "part": grp[0], "last": grp[2]}
         o.update(kw)
         ops.append(o)
         return o
@@ -113,6 +142,10 @@ def build():
                        50 + out["w"] * 1.56 * CYC, gat=out["w"])
         return add("V", lambda g, T: g.vector.tensor_tensor(ap(T, out), ap(T, a), ap(T, b), op), [out], [a, b],
                    vc(out["w"] * (1 if (psum(a) or psum(b)) else 2)))
+
+    def tsg(out, a, c, off):
+        return add("V", lambda g, T: g.vector.tensor_scalar(ap(T, out), ap(T, a).indirect(ap(T, off)), c, None, A.add), [out], [a, off],
+                   50 + out["w"] * 1.56 * CYC, gat=out["w"])
 
     def cp(out, a):
         return add("V", lambda g, T: g.vector.tensor_copy(ap(T, out), ap(T, a)), [out], [a], vc(out["w"] * half([out, a])))
@@ -158,7 +191,7 @@ def build():
         def f(g, T):
             return (g.sync if q == "Y" else g.scalar).dma_start(ap(T, out) if isinstance(out, dict) else out(T),
                                                                 ap(T, src) if isinstance(src, dict) else src(T))
-        return add(q, f, [out] if isinstance(out, dict) else [], [src], 60, dma=sem, lat=1600 + nbytes / 180.0)
+        return add(q, f, [out] if isinstance(out, dict) else [], [src], 60, dma=sem, lat=1600 + nbytes / BW, nb=nbytes)
 
     r = reg
     blk = lambda n, j, w=128: r(n, w * j, w * j + w)
@@ -166,23 +199,22 @@ def build():
     SENT = 1900.5 - E12
     NS = 4 - VS
     for c in range(NCH):
-        dma("Y", "dar%d" % c, blk("raw", c, CW), lambda T, c=c: T.arcs[:, c * CW:(c + 1) * CW], (c + 1) * 128 * CW * 4)
+        dma("Y", "dar%d" % c, blk("raw", c, CW), lambda T, c=c: T.arcs[:, c * CW:(c + 1) * CW], 128 * CW * 4)
     dma("S", "dst", view("sti", (slice(0, K), slice(0, 16))), lambda T: T.st0[:, :], 49152)
     ms(r("rsi", 0, L), 1)
     for gq in range(8):
         p = 16 * ((gq - 1) % 8)
-        dma("S", "drs", r("rsi", 0, L, 1, p, p + 12, 2), lambda T, gq=gq: T.rs0[gq, :], 49152)
-    dma("S", "dac", r("act", 0, L), lambda T: T.ac[:, :], 2 ** 20)
-    dma("Y", "dpay", r("payt", 0, W), lambda T: T.pay[:, :], 2 ** 21)
+        dma("S", "drs", r("rsi", 0, L, 1, p, p + 12, 2), lambda T, gq=gq: T.rs0[gq, :], 6144)
+    dma("Y", "dac", r("act", 0, L), lambda T: T.ac[:, :], 2 ** 17)
     iota(r("pi", 0, 1), [[0, 1]], 0, 1)
     iota(r("val", 0, 16), [[0, 16]], -112, 1)
     iota(r("val", 16, 144), [[-16, 8], [0, 16]], 0, 1)
-    iota(r("col", 0, 136), [[1, 136]], -8, 0)
+    iota(r("col", 0, 144), [[1, 144]], -16, 0)
     iota(r("one", 0, 128), [[0, 128]], 1, 0)
     for b in range(2):
         sel(blk("iw", b), r("one", 0, 128), [[-1, 128]], A.is_equal, 0.0, 0, 1)
-    iota(r("vd", 0, 128), [[-2, 64], [0, 2]], 0, 1)
-    iota(blk("yv", 0), [[0, 8], [1, 16]], -7, 0)
+    iota(r("cob", 0, 128), [[1, 128]], 0, 0)
+    fill = lambda out, v: iota(out, [[0, out["w"]]], int(v), 0)
     pcol = lambda j: r("pc", j, j + 1)
     picol = lambda j: r("pi", j, j + 1)
     ecol = lambda j: r("ee", j, j + 1)
@@ -193,7 +225,7 @@ def build():
     ts(picol(5), picol(0), 4, 1, A.logical_shift_right, A.bitwise_and)
     cp(pcol(3), picol(3))
     ts(r("bm", 0, 144), r("val", 0, 144), pcol(3), None, A.is_equal)
-    ts(r("ee", 0, 16), r("col", 8, 24), pcol(3), None, A.is_equal)
+    ts(r("ee", 0, 16), r("col", 16, 32), pcol(3), None, A.is_equal)
     ts(pcol(4), ecol(13), 64.0, None, A.mult)
     ts(r("cr", 25, 30), r("ee", 3, 12, 2), -64.0, pcol(4), A.mult, A.add)
     tt(r("cr", 1, 6), r("ee", 2, 12, 2), r("cr", 25, 30), A.add)
@@ -207,24 +239,42 @@ def build():
         act(blk("dl", j), r("bm", 0, 128), F.Identity, scale=ccol(8 + j))
     for k in range(K):
         act(blk("rk", k, 144), r("bm", 0, 144), F.Identity, scale=ccol(k))
-    ms(r("ra", 0, 128), 0.0)
+    fill(r("ra", 0, 128, 16), 0)
+    fill(r("ra", 15, 128, 16), 0)
     for y in range(1, 15):
         act(r("ra", y, 128, 16), r("bm", y, 128, 16), F.Identity, scale=ccol(16 + (y - 1) % 6) if y < 13 else ecol(13))
     ts(pcol(0), picol(2), 6.0, 1.0, A.mult, A.add)
     tt(pcol(1), pcol(0), picol(1), A.add)
-    ts(pcol(2), picol(3), 15.0, -1.0, A.not_equal, A.mult)
     ts(pcol(6), picol(5), 0.0, None, A.is_equal)
     ts(pcol(7), picol(5), 1.0, None, A.is_equal)
-    ts(r("self", 0, 136), r("col", 0, 136), pcol(1), 1.0 / 2048, A.is_equal, A.mult)
-    ts(blk("tmpc", 0), r("vd", 0, 128), 1.0, None, A.is_equal)
-    ts(blk("tmpc", 1), r("vd", 0, 128), -1.0, pcol(2), A.is_equal, A.mult)
-    tt(r("dm", 0, 128), blk("tmpc", 0), blk("tmpc", 1), A.add)
+    ts(r("self", 0, 136), r("col", 8, 144), pcol(1), 1.0 / 2048, A.is_equal, A.mult)
+    dm, pair, group = r("dm", 0, 128), [[-2, 64], [0, 2]], [[-16, 8], [0, 16]]
+    if W0:
+        cp(ccol(31), picol(1))
+        ts(r("self0", 0, 144), r("col", 0, 144), ccol(31), 1.0 / 2048, A.is_equal, A.mult)
+        ts(ccol(30), pcol(3), -14.0, None, A.add)
+        dm0 = r("dm0", 0, 128)
+        fill(dm0, 1)
+        sel(dm0, dm0, [[-1, 128]], A.is_gt, 0.0, 0, 1)
+        sel(dm0, dm0, [[-1, 128]], A.not_equal, -1.0, 0, 1)
+        sel(dm0, dm0, [[16, 8], [0, 16]], A.is_ge, 0.0, 15, -1)
+    if MV:
+        fill(dm, 2)
+        sel(dm, dm, pair, A.is_ge, -1.0, -2, 1)
+        sel(dm, dm, pair, A.is_ge, 0.0, 0, 1)
+        sel(dm, dm, [[16, 8], [0, 16]], A.is_ge, 0.0, 15, -1)
+        tt(pcol(5), picol(3), picol(2), A.subtract)
+        ts(pcol(15), pcol(5), -2.0, 26.5, A.mult, A.add)
+    else:
+        fill(dm, 0)
+        sel(dm, dm, pair, A.not_equal, 1.0, -1, 1)
+        sel(dm, dm, pair, A.not_equal, -1.0, 1, 1)
+        sel(dm, dm, group, A.is_ge, 0.0, 0, 1)
     for c0 in range(2):
         act(blk("iwb", c0, 256), r("iw", 0, 256), F.Identity, scale=pcol(6 + c0))
-        cp(blk("iwm", c0, 256), blk("iwb", c0, 256))
-    cp(r("idf", 0, 128), blk("iw", 0))
+        act(blk("idb", c0), blk("iw", 0), F.Identity, scale=1.0 - 2 * c0)
     pq = lambda j, a=0, b=5: r("pq", 8 * j + a, 8 * j + b)
-    ts(pq(0), r("col", 8, 88, 16), pcol(3), None, A.add)
+    ts(pq(0), r("col", 16, 96, 16), pcol(3), None, A.add)
     ts(pq(0, 4, 5), picol(2), 64.0, None, A.add)
     ts(pq(1), pq(0), 1.0 / 12, -11.0 / 24, A.mult, A.add)
     ts(pq(2), pq(1), MAG, MAG, A.add, A.subtract)
@@ -235,75 +285,100 @@ def build():
     ts(pq(7), pq(6), 11.5, -12.0, A.is_gt, A.mult)
     tt(pq(8), pq(6), pq(7), A.add)
     tt(pq(9), pq(4), pq(8), A.subtract)
-    ts(pq(9), pq(9), 2.0 ** -14, None, A.mult)
+    ts(pq(9), pq(9), 2.0 ** 8, None, A.mult)
     ts(pcol(8), picol(1), 1.0, None, A.add)
     ts(pq(10), pq(4), pcol(8), None, A.add)
     ts(pq(11), pq(8), pcol(8), None, A.add)
     ts(pcol(9), pcol(3), 5.5, KILL, A.is_lt, A.mult)
     for b in range(5):
-        ts(blk("kla", b), r("col", 8, 136), pq(10, b, b + 1), KILL if b < 4 else pcol(9), A.is_equal, A.mult)
-        ts(blk("klb", b), r("col", 8, 136), pq(11, b, b + 1), KILL if b < 4 else pcol(9), A.is_equal, A.mult)
-        tt(blk("kl0", b), blk("kla", b), blk("klb", b), A.subtract)
+        ts(blk("kla", b), r("cob", 0, 128), pq(10, b, b + 1), KILL if b < 4 else pcol(9), A.is_equal, A.mult)
+        ts(blk("klb", b), r("cob", 0, 128), pq(11, b, b + 1), KILL if b < 4 else pcol(9), A.is_equal, A.mult)
     tt(r("cr", 24, 27), r("ee", 0, 6, 2), r("ee", 1, 6, 2), A.add)
     tt(pcol(12), ccol(24), ccol(25), A.subtract)
     tt(pcol(13), ccol(26), ccol(24), A.subtract)
-    tt(pcol(14), ccol(26), ccol(25), A.subtract)
-    ts(pcol(14), pcol(14), 0.25, None, A.mult)
-    act(blk("tmpc", 0), blk("kla", 4), F.Identity, scale=pcol(12))
-    act(blk("tmpc", 1), blk("klb", 4), F.Identity, scale=pcol(13))
-    tt(r("kls", 0, 128), blk("tmpc", 0), blk("tmpc", 1), A.add)
-    ts(r("ddt", 0, 640), r("kl0", 0, 640), 1024.0 / KILL, None, A.mult)
-    tr(r("dd", 0, 640), r("ddt", 0, 640))
-    ts(r("dct", 0, 640), r("kl0", 0, 640), 2.0 ** -10 / KILL, None, A.mult)
+    tt(pcol(2), ccol(26), ccol(25), A.subtract)
+    ts(pcol(14), pcol(2), 2.0 ** 20, None, A.mult)
     for b in range(5):
-        act(r("dct", 128 * b + 13, 128 * b + 128, 16), r("bm", 16, 144, 16), F.Identity, scale=pq(9, b, b + 1))
+        act(r("kla", 128 * b + 13, 128 * b + 128, 16), r("bm", 16, 144, 16), F.Identity, scale=pq(9, b, b + 1))
         if b >= NS:
-            act(r("dct", 128 * b + 14, 128 * b + 128, 16), r("bm", 16, 144, 16), F.Identity, scale=pcol(14) if b == 4 else -0.125)
-    tr(r("dc", 0, 640), r("dct", 0, 640))
-    tt(blk("yv", 1), blk("yv", 0), r("bm", 16, 144), A.mult)
-    act(blk("yv", 0), blk("yv", 1), F.Identity, scale=ecol(13))
-    act(blk("yv", 1), blk("iw", 0), F.Identity, scale=16.0)
-    tt(r("ccx", 0, 128), blk("yv", 0), blk("yv", 1), A.add)
-    ms(r("mc0", 0, 8 * L), 4096.0)
-    ms(r("mc", 6, 7 * L, 7), 4096.0)
-    ms(r("fss", 0, 128), -1.0); ms(r("fss", 0, 128, 16), 8192.0)
-    ms(r("fs1", 0, 128), -8192.0); ms(r("fs1", 0, 128, 16), SENT)
-    ms(r("frv", 0, 128), 0.0); ms(r("frv", 15, 128, 16), 1.0)
-    ms(r("fpar", 0, 128), 1.0); ms(r("fpar", 0, 128, 2), -1.0)
-    ms(r("thr", 0, 64), MAG + 100); ms(r("thr", 0, 64, 8), -1.0); ms(r("thr", 6, 64, 8), 2 * MAG); ms(r("thr", 7, 64, 8), 2 * MAG)
-    ms(r("f6", 0, 768), 1.0); ms(r("f6", 0, 768, 6), 0.0)
-    ms(r("kr", 0, 128), MAG); ms(r("df", 0, 128), 0.0); ms(r("zero", 0, 512), 0.0)
+            act(r("kla", 128 * b + 14, 128 * b + 128, 16), r("bm", 16, 144, 16), F.Identity, scale=pcol(14) if b == 4 else -2.0 ** 19)
+        to = r("pb%d" % (5 + b // 4), 128 * (b % 4), 128 * (b % 4) + 128)
+        mm(to, blk("kla", b), blk("idb", 0), True, False)
+        mm(to, blk("klb", b), blk("idb", 1), False, True)
+    for a, b, pbk in ((0, 512, "pb5"), (512, 640, "pb6")):
+        act(r("dc", a, b), r(pbk, 0, b - a), F.Identity, scale=2.0 ** -22)
+        act(r("dd", a, b), r(pbk, 0, b - a), F.Identity, scale=0.25)
+    mm(r("pb4", 0, 128 * NS), blk("idb", 0), r("kla", 0, 128 * NS), True, False)
+    mm(r("pb4", 0, 128 * NS), blk("idb", 1), r("klb", 0, 128 * NS), False, True)
+    for b in range(2):
+        act(blk("tmpc", b), blk("iw", 0), F.Identity, scale=pcol(12 + b))
+        mm(blk("pb4", NS), blk("tmpc", b), blk("klb" if b else "kla", 4), b == 0, b == 1)
+    act(r("kl0", 0, 128 * NS + 128), r("pb4", 0, 128 * NS + 128), F.Copy)
+    ccx = r("ccx", 0, 128)
+    iota(ccx, [[0, 8], [1, 16]], -7, 0)
+    sel(ccx, ccx, group, A.is_equal, 0.0, -13, 1)
+    sel(ccx, ccx, [[-1, 128]], A.not_equal, 16.0, 0, 1)
+    for nm, a, b, s, v in (("mc0", 6, 8 * L, 8, 4096), ("mc0", 7, 8 * L, 8, 4096), ("fss", 0, 128, 1, -1), ("fss", 0, 128, 16, 8192),
+                           ("fpar", 0, 128, 2, -1), ("fpar", 1, 128, 2, 1), ("frv", 0, 128, 1, 0), ("frv", 15, 128, 16, 1), ("zero", 0, 512, 1, 0),
+                           ("fs1", 0, 128, 1, -8192), ("kr", 0, 128, 1, MAG), ("df", 0, 128, 1, 0), ("thr", 0, 64, 1, MAG + 100), ("thr", 0, 64, 8, -1),
+                           ("thr", 6, 64, 8, MAG + 999), ("thr", 7, 64, 8, MAG + 999), ("mc", 6, 7 * L, 7, 4096), ("f6", 0, 768, 1, 1), ("f6", 0, 768, 6, 0)):
+        if (nm != "frv" or not MV) and (nm != "f6" or not MT):
+            fill(r(nm, a, b, s), v)
+    ms(r("fs1", 0, 128, 16), SENT)
     for p in range(NP):
         n, l0 = PARTS[p], sum(PARTS[:p])
-        ms(r("xs", l0 + 16 * p, l0 + 16 * p + 16), 0.0)
-        ms(r("ge", l0 + 16 * p + n, l0 + 16 * p + n + 16), 0.0)
-        ms(r("s1", 6 * l0 + 16 * p, 6 * l0 + 16 * p + 16), 0.0)
-        ms(r("ww", 6 * l0, 6 * l0 + n), 1.0)
-    ts(r("rf0", 0, L), r("rsi", 0, L), 0.0, None, A.add)
+        fill(r("xs", l0 + 16 * p, l0 + 16 * p + 16), 0)
+        if not MV:
+            fill(r("ge", l0 + 16 * p + n, l0 + 16 * p + n + 16), 0)
+        fill(r("s1", 6 * l0 + 16 * p, 6 * l0 + 16 * p + 16), 0)
+        fill(r("ww", 6 * l0, 6 * l0 + n), 1)
+    act(r("rf0", 0, L), r("rsi", 0, L), F.Copy)
     for c in range(NCH):
         a, b = c * CW, (c + 1) * CW
-        ts(r("lo", a, b), r("raw", a, b), 32767, None, A.bitwise_and)
         ts(r("hi", a, b), r("raw", a, b), 15, None, A.logical_shift_right)
-        tt(r("mn", a, b), r("lo", a, b), r("hi", a, b), A.min)
+        lo = r("win", W + a, W + b) if len(ZC) == 1 else r("lo", a, b)
+        lolast = ts(lo, r("raw", a, b), 32767, None, A.bitwise_and)
+        if TS:
+            act(r("pb%d" % (c % 4), 0, CW), r("hi", a, b), F.Copy)
+            tt(r("mn", a, b), lo, r("pb%d" % (c % 4), 0, CW), A.min)
+        else:
+            tt(r("mn", a, b), lo, r("hi", a, b), A.min)
         act(r("mnb", a, b), r("mn", a, b), F.Identity, bias=191.5 + E12, scale=1.0 / 2048)
-        if (c + 1) % (NCH // 2) == 0:
+        for q, to, src in zip(ZC, (r("win", a, b), r("win", W + a, W + b)), (r("hi", a, b), lo)):
+            if q == "S":
+                act(to, src, F.Copy)
+            else:
+                sel(to, src, [[0, CW]], A.is_ge, 0.0, 0, 0)
+        if ZC:
+            src = r("win", W + a, W + b, 1, 1, 128, 2) if len(ZC) == 1 else r("lo", a, b, 1, 1, 128, 2)
+            dma("Y", "dwa%d" % c, r("win", a, b, 1, 0, 128, 2), src, 256 * CW)
+            dma("Y", "dwb%d" % c, r("win", W + a, W + b, 1, 1, 128, 2), r("hi", a, b, 1, 0, 128, 2), 256 * CW)
+        elif (c + 1) % (NCH // 2) == 0:
             a = b - W // 2
             for par in range(2):
                 for u, nm in enumerate(("lo", "hi")):
                     o = (1 - par) * W
-                    dma("Y", "dw%d" % (a // (W // 2)), r("win", o + a, o + b, 1, u, 128, 2), r(nm, a, b, 1, par, 128, 2), 2 ** 20)
+                    dma("Y", "dw%d" % (a // (W // 2)), r("win", o + a, o + b, 1, u, 128, 2), r(nm, a, b, 1, par, 128, 2), 2 ** 18)
+    dma("Y", "dpay", r("payt", 0, W), lambda T: T.pay[:, :], 2 ** 19)["x"].append(lolast["id"])
+
+    def lists(out, src, scalar):
+        if scalar:
+            act(out, src, F.Identity, bias=1023.5, scale=2048.0)
+        else:
+            ts(out, src, 2048.0, 1023.5, A.mult, A.add)
 
     turn, sums = [0, 0], []
     for t in range(V):
         for p in range(NP):
             n, l0 = PARTS[p], sum(PARTS[:p])
-            grp[0] = p
+            grp[0], grp[2] = p, t == V - 1
             e, m = n // 16, 6 * n // 16
             j, jl = NP * t + p, NP * (t - 1) + p
             H = lambda nm, a=0, b=n, s=1, w=1: r(nm, w * l0 + a, w * l0 + b, s)
             M = lambda nm, a=0, b=m, s=1, tt_=0: r(nm, 96 * tt_ + 6 * l0 // 16 + a, 96 * tt_ + 6 * l0 // 16 + b, s)
             Q = lambda nm, a=0, b=n // 2, s=1: r(nm, l0 // 2 + a, l0 // 2 + b, s)
-            pb = "pb%d" % (5 + p % 2)
+            bank = lambda use: {"use": use, "key": "%s%d" % (use, len(ops)), "bank": None, "ops": set()}
+            pb = "pb%d" % BANKS["own"][p]
             O = lambda a, b, s=1: r(pb, a, b, s)
             Fp, Mp = O(0, n), O(128, 128 + n)
 
@@ -313,6 +388,7 @@ def build():
                         o = 256 * c0 + (16 * (c0 - h0 - rot)) % 128
                         mm(out(c0, w, 2), r(mat, o, o + 128), src(h0), first and h0 == 0, (h0 == 1) if first else (last and c0 == 1 and h0 == 1))
 
+            waves = ([("e", 0, e * SPL)] if SPL else []) + [("o", e * SPL, m)]
             if t == 0:
                 st3 = view("sti", (slice(0, K), slice(l0 // 16, l0 // 16 + e)))
                 cp(M("off1"), st3)
@@ -320,90 +396,125 @@ def build():
                 rfin = lambda a, b: H("rf0", a, b)
             else:
                 rfin = lambda a, b: r("rfl", L * (t - 1) + l0 + a, L * (t - 1) + l0 + b)
-                add("R", None, [M("zdl", 0, m, 1, t - 1)], [], 0, recv="ao%d" % jl, after=("o", jl))
                 add("R", None, [rfin(0, n)], [], 0, recv="ar%d" % jl, after=("r", jl))
-                zin = lambda h0: M("zdl", h0, m, 2, t - 1)
-                turn_lists(lambda a, b, s: O(256 + a, 256 + b, s), zin, "iwm", 1, True, True)
-                ts(M("off1"), O(256, 256 + m), 2048.0, 1023.5, A.mult, A.add)
+                for nm, c0, c1 in waves:
+                    add("R", None, [M("zdl", c0, c1, 1, t - 1)], [], 0, recv="a%s%d" % (nm, jl), after=(nm, jl))
+                    turn_lists(lambda a, b, s: O(256 + c0 + a, 256 + c0 + b, s), lambda h0: M("zdl", c0 + h0, c1, 2, t - 1), "iwb", 1, True, True, c1 - c0)
+                    lists(M("off1", c0, c1), O(256 + c0, 256 + c1), O1S)
             cw = 8 if t == 0 else 7
             mc = "mc0" if t == 0 else "mc"
-            for a in range(0, n, SUB):
-                b = min(n, a + SUB)
-                for k in range(K - 1, -1, -1):
-                    act(H(mc, cw * a + 5 - k, cw * b, cw, cw), r("mnb", 0, W), F.Identity, bias=-192.0, off=M("off1", e * k + a // 16, e * k + b // 16))
-            for a in range(0, n, 64):
-                b = min(n, a + 64)
-                bk = "pb%d" % (turn[0] % 2)
-                turn[0] += 1
-                mm(r(bk, cw - 1, cw * (b - a), cw), blk("iw", 0), H("act", a, b), True, True)
+            gat = {}
+            for k in range(K):
+                if k >= K - GV[p]:
+                    tsg(H(mc, 5 - k, cw * n, cw, cw), r("mnb", 0, W), -192.0, M("off1", e * k, e * k + e))
+                    continue
+                sub = n if k < SPL and t else SUB
+                for a in range(0, n, sub):
+                    b = min(n, a + sub)
+                    o = act(H(mc, cw * a + 5 - k, cw * b, cw, cw), r("mnb", 0, W), F.Identity, bias=-192.0, off=M("off1", e * k + a // 16, e * k + b // 16))
+                    if k == (SPL if t else 0) + LATE:
+                        gat[a // SUB] = o["id"]
+            nc = -(-cw * n // 448)
+            for a, b in ((n * c // nc, n * (c + 1) // nc) for c in range(nc)):
+                bk = bank("dif")
+                mm(r(bk, cw - 1, cw * (b - a), cw), blk("iw", 0), H("act", a, b), True, True)["x"].append(gat[a // SUB])
                 for jj in range(cw - 1):
-                    mm(r(bk, jj, cw * (b - a), cw), blk("dl", jj) if jj < K else r("rk", 0, 128), rfin(a, b), True, True)
+                    mm(r(bk, jj, cw * (b - a), cw), blk("dl", jj) if jj < K else r("rk", 0, 128), rfin(a, b), True, True)["x"].append(len(ops) - 2)
                 scan(H("scn", cw * a, cw * b, 1, 8), r(bk, 0, cw * (b - a)), H(mc, cw * a, cw * b, 1, cw), A.add, A.min)
             x0 = l0 + 16 * p
-            SS = r("pb7", 256 + l0, 256 + l0 + n)
+            SS = O(384, 384 + n)
             tr(r("xs", x0 + 16, x0 + 16 + n), H("scn", cw - 1, cw * n, cw, 8))
-            scan(SS, r("xs", x0 + 15, x0 + 15 + n), r("fss", 0, n), A.min, A.max)
+            early = scan(SS, r("xs", x0 + 15, x0 + 15 + n), r("fss", 0, n), A.min, A.max)
             tt(r("ge", x0, x0 + n), r("xs", x0 + 16, x0 + 16 + n), SS, A.is_ge)
-            lastps = scan(H("ps"), r("fpar", 0, n), r("ge", x0, x0 + n), A.add, A.mult)
-            scan(rev("step", l0, l0 + n), rev("ge", x0 + 1, x0 + 1 + n), rev("frv", 0, n), A.min, A.max)
-            tr(H("stg"), H("step"))
-            pab, pa0 = ("pb%d" % (p % 2), 448) if t else ("pb%d" % (2 + 2 * (p % 2)), 0)
-            PA = lambda a, b, s=1: r(pab, pa0 + a, pa0 + b, s)
-            for k in range(REP if REP > 1 else 0):
-                act(M("p6", e * k, e * k + e), H("ps", 15, n, 16), F.Copy)
-            if t == 0:
-                mm(PA(0, m), r("idf", 0, 128), M("sf0"), True, False)["x"].append(lastps["id"])
+            direct = W0 and t == 0
+            if not direct:
+                scan(H("ps"), r("fpar", 0, n), r("ge", x0, x0 + n), A.add, A.mult)
+            if MV or direct:
+                tr(H("stg"), r("ge", x0, x0 + n))
             else:
-                mm(PA(0, m), r("zero", 0, 128), r("zero", 0, m), True, False)["x"].append(lastps["id"])
-                turn_lists(PA, zin, "iwm", 1, False, False)
-            for k in range(0, K, REP):
-                turn_lists(lambda a, b, s: PA(e * k + a, e * k + b, s), lambda h0: H("ps", 15 + 16 * h0, n, 32) if REP == 1 else M("p6", h0, e * REP, 2),
-                           "iwb", 0, False, k == K - REP, e * REP)
-            mm(Mp, r("dm", 0, 128), H("stg"), True, True)
-            ts(M("off2"), PA(0, m), 2048.0, 1023.5, A.mult, A.add)
-            cm_ = act(H("msk"), Mp, F.Copy)
+                scan(rev("step", l0, l0 + n), rev("ge", x0 + 1, x0 + 1 + n), rev("frv", 0, n), A.min, A.max)
+                tr(H("stg"), H("step"))
+            for k in range(REP if REP > 1 and not direct else 0):
+                act(M("p6", e * k, e * k + e), H("ps", 15, n, 16), F.Copy)
+            for k0 in range(0, 0 if direct else K, KO):
+                pab = bank("par")
+                PA = lambda a, b, s=1: r(pab, 448 + a, 448 + b, s)
+                c0, c1 = e * k0, e * (k0 + KO)
+                if t == 0:
+                    mm(PA(0, c1 - c0), blk("idb", 0), M("sf0", c0, c1), True, False)["x"].append(early["id"])
+                else:
+                    mm(PA(0, c1 - c0), r("zero", 0, 128), r("zero", 0, c1 - c0), True, False)["x"].append(early["id"])
+                    turn_lists(PA, lambda h0: M("zdl", c0 + h0, c1, 2, t - 1), "iwb", 1, False, False, c1 - c0)
+                for k in range(0, KO, REP):
+                    turn_lists(lambda a, b, s: PA(e * k + a, e * k + b, s), lambda h0: H("ps", 15 + 16 * h0, n, 32) if REP == 1 else M("p6", h0, e * REP, 2),
+                               "iwb", 0, False, k == KO - REP, e * REP)
+                ts(M("off2", c0, c1), PA(0, c1 - c0), 2048.0, 1023.5, A.mult, A.add)
+            mm(Mp, r("dm0" if direct else "dm", 0, 128), H("stg"), True, True)
+            if direct:
+                cm_ = act(H("msk"), Mp, F.Relu, bias=ccol(30))
+            else:
+                cm_ = ts(H("msk"), Mp, pcol(15), None, A.is_gt) if MV else act(H("msk"), Mp, F.Copy)
             mm(Fp, r("ra", 0, 128), rfin(0, n), True, False)["x"].append(cm_["id"])
-            for k in range(K):
-                tt(H("mg", n * k, n * (k + 1), 1, 6), r("win", 0, 2 * W), H("msk"), A.mult, off=M("off2", e * k, e * (k + 1)))
-                mm(Fp, r("self", 8 - k, 136 - k), H("mg", n * k, n * k + n, 1, 6), False, k == K - 1)
+            for i in range(2 * K if direct else K):
+                k, MG = i % K, H("mg", n * i, n * i + n, 1, 12)
+                if direct:
+                    lastg = tt(MG, r("hi" if i >= K else "lo", 0, W), H("msk"), A.mult, off=M("off1", e * k, e * k + e))
+                    mm(Fp, r("self0", 15 - i, 143 - i), MG, False, i == 2 * K - 1)
+                else:
+                    lastg = tt(MG, r("win", 0, 2 * W), H("msk"), A.mult, off=M("off2", e * k, e * k + e))
+                    mm(Fp, r("self", 8 - k, 136 - k), MG, False, k == K - 1)
             ts(H("cc"), Fp, MAG, MAG, A.add, A.subtract)
             tt(H("dfr"), Fp, H("cc"), A.subtract)
-            order = list(range(NS, 4)) + list(range(NS)) + [4]
-            place = lambda b: r("pb7", n * (b - NS), n * (b - NS + 1)) if NS <= b < 4 else r("pb3", n * min(b, NS), n * min(b, NS) + n)
-            for b in order:
-                mm(place(b), blk("dc", b), H("cc"), True, False)
-                mm(place(b), blk("dd", b), H("dfr"), False, True)
+            (vb, v0), stb = (bank("vt"), 0) if BANKS["vt"] else (pb, 64), bank("st")
+            place = lambda b: r(vb, v0 + n * (b - NS), v0 + n * (b - NS + 1)) if NS <= b < 4 else r(stb, n * min(b, NS), n * min(b, NS) + n)
+            sets = [list(range(NS, 4)), list(range(NS)) + [4]]
+            for bs in sets[::-1] if SF else sets:
+                if ZS:
+                    whole = r(stb, 0, n * (NS + 1)) if 4 in bs else r(vb, v0, v0 + n * VS)
+                    mm(whole, r("zero", 0, 128), r("zero", 0, whole["w"]), True, False)["x"].append(lastg["id"])
+                    for b in bs:
+                        mm(place(b), blk("dc", b), H("cc"), False, False)
+                    for b in bs:
+                        mm(place(b), blk("dd", b), H("dfr"), False, b == bs[-1])
+                else:
+                    for b in bs:
+                        mm(place(b), blk("dc", b), H("cc"), True, False)["x"].append(len(ops) - 2)
+                        mm(place(b), blk("dd", b), H("dfr"), False, True)
             SG = lambda a, b: H("sg", n * a, n * b, 1, 13)
             CQ = 1.5 * 2.0 ** 21
             kills = []
             for v in range(2):
-                ts(SG(VS * v, VS * v + VS), r("pb7", 0, n * VS), CQ, CQ - 0.25 * v, A.add, A.is_equal)
+                ts(SG(VS * v, VS * v + VS), r(vb, v0, v0 + n * VS), CQ, CQ - 0.25 * v, A.add, A.is_equal)
                 kills += [(blk("klb" if v else "kla", NS + b), VS * v + b) for b in range(VS)]
             s0 = 2 * VS
-            act(SG(s0, s0 + NS + 1), r("pb3", 0, n * (NS + 1)), F.Sign)
-            kills += [(blk("kl0", b), s0 + b) for b in range(NS)] + [(r("kls", 0, 128), s0 + NS)]
+            act(SG(s0, s0 + NS + 1), r(stb, 0, n * (NS + 1)), F.Sign)
+            kills += [(blk("kl0", b), s0 + b) for b in range(NS + 1)]
             for v in range(2):
                 s1 = s0 + NS + 1 + NS * v
-                act(SG(s1, s1 + NS), r("pb3", 0, n * NS), F.Sign, bias=0.25, scale=1.0 if v else -1.0)
+                act(SG(s1, s1 + NS), r(stb, 0, n * NS), F.Sign, bias=0.25, scale=1.0 if v else -1.0)
                 kills += [(blk("klb" if v else "kla", b), s1 + b) for b in range(NS)]
             Xp = Mp
             for i, (lh, s) in enumerate(kills):
                 mm(Xp, lh, SG(s, s + 1), i == 0, False)
             mm(Xp, r("ccx", 0, 128), H("cc"), False, False)
-            mm(Xp, r("idf", 0, 128), H("dfr"), False, True)
+            mm(Xp, blk("idb", 0), H("dfr"), False, True)
             tr(H("xt"), Xp)
             sb = 6 * l0 + 16 * p + 16
             S1 = lambda a, b, s=1: r("s1", sb + a, sb + b, s)
             for k in range(K):
                 scan(S1(n * k, n * k + n), H("xt"), r("fs1", 0, n) if k == 0 else S1(n * k - n - 1, n * k - 1), A.min, A.max)
-                act(Q("kr", k, n // 2, 8), S1(n * k + 12, n * k + n, 16), F.Identity, bias=MAG, scale=1.0 / 16)
+                if k < K - KV:
+                    act(Q("kr", k, n // 2, 8), S1(n * k + 12, n * k + n, 16), F.Identity, bias=MAG, scale=1.0 / 16)
+                else:
+                    ts(Q("kr", k, n // 2, 8), S1(n * k + 12, n * k + n, 16), 1.0 / 16, MAG, A.mult, A.add)
             zd = lambda a=0, s=1: M("zds", a, m, s, t)
-            ts(M("ka"), S1(12, 6 * n, 16), MAG, MAG, A.add, A.subtract)
-            tt(zd(), S1(12, 6 * n, 16), M("ka"), A.subtract)
-            if t < V - 1:
-                add("G", None, [], [zd()], ISSUE, send=("o", j), lat=LATS, to=M("zdl", 0, m, 1, t))
-            turn_lists(lambda a, b, s: O(304 + a, 304 + b, s), lambda h0: zd(h0, 2), "iwm", 0, True, True)
-            ts(M("offu"), O(304, 304 + m), 2048.0, 1023.5, A.mult, A.add)
+            for nm, c0, c1 in waves if t < V - 1 else [("o", 0, m)]:
+                ts(M("ka", c0, c1), S1(16 * c0 + 12, 16 * c1, 16), MAG, MAG, A.add, A.subtract)
+                tt(M("zds", c0, c1, 1, t), S1(16 * c0 + 12, 16 * c1, 16), M("ka", c0, c1), A.subtract)
+                if t < V - 1:
+                    add("G", None, [], [M("zds", c0, c1, 1, t)], ISSUE, send=(nm, j), lat=LATS, to=M("zdl", c0, c1, 1, t))
+            turn_lists(lambda a, b, s: O(304 + a, 304 + b, s), lambda h0: zd(h0, 2), "iwb", 0, True, True)
+            lists(M("offu"), O(304, 304 + m), OUS)
             tt(Q("df", 1), Q("kr", 1), Q("kr", 0, n // 2 - 1), A.subtract)
             tt(H("rt", 1, n, 2), Q("kr"), r("thr", 0, n // 2), A.is_lt)
             scan(H("rt", 0, n, 2), Q("df"), H("rt", 1, n, 2), A.add, A.mult)
@@ -411,60 +522,85 @@ def build():
             tr(rfo(), H("rt"))
             if t < V - 1:
                 add("G", None, [], [rfo()], ISSUE, send=("r", j), lat=LATS, to=r("rfl", L * t + l0, L * t + l0 + n))
-            for k0, k1 in ((1, 4), (4, 6)):
-                for k in range(k0, k1):
-                    mm(r("pb2", n * (k - k0), n * (k - k0 + 1)), r("rk", 144 * k + 16, 144 * k + 144), rfo(), True, True)
-                turn[1] += 1
-                act(H("ww", n * k0, n * k1, 1, 6), r("pb2", 0, n * (k1 - k0)), F.Exp, scale=-0.125, extra=1300.0 if turn[1] == 1 else 0.0)
             XX = lambda a, b, s=1: r("xx", 6 * L * t + 6 * l0 + a, 6 * L * t + 6 * l0 + b, s)
+            xs = XS if t < V - 1 else min(XS, 1)
+            for k0, k1 in ((1, 4), (4, 6)) if 5 * n > 448 else ((1, 6),):
+                bk = bank("pay")
+                for k in range(k0, k1):
+                    mm(r(bk, n * (k - k0), n * (k - k0 + 1)), r("rk", 144 * k + 16, 144 * k + 144), rfo(), True, True)
+                turn[1] += 1
+                if k0 < xs:
+                    act(H("pg", n * k0, n * k1, 1, 6), r("payt", 0, W), F.Copy, off=M("offu", e * k0, e * k1))
+                    act(r(bk, 0, n * (k1 - k0)), r(bk, 0, n * (k1 - k0)), F.Exp, scale=-0.125, extra=1300.0 if turn[1] == 1 else 0.0)
+                    tt(XX(n * k0, n * k1), H("pg", n * k0, n * k1, 1, 6), r(bk, 0, n * (k1 - k0)), A.mult)
+                else:
+                    act(H("ww", n * k0, n * k1, 1, 6), r(bk, 0, n * (k1 - k0)), F.Exp, scale=-0.125, extra=1300.0 if turn[1] == 1 else 0.0)
             rotm = r("iw", 16 * t, 16 * t + 128)
             if t < V - 1:
-                for k in range(0, K, GP):
-                    tt(XX(n * k, n * (k + GP)), r("payt", 0, W), H("ww", n * k, n * (k + GP), 1, 6), A.mult, off=M("offu", e * k, e * (k + GP)))
+                if XS:
+                    act(XX(0, n), r("payt", 0, W), F.Copy, off=M("offu", 0, e))
+                for k in range(XS, K, GP):
+                    k1 = min(K, k + GP)
+                    tt(XX(n * k, n * k1), r("payt", 0, W), H("ww", n * k, n * k1, 1, 6), A.mult, off=M("offu", e * k, e * k1))
                 LD = lambda b: r("land", 2 * L * t + 2 * l0 + n * b, 2 * L * t + 2 * l0 + n * b + n)
-                add("G", None, [], [XX(0, 6 * n)], ISSUE, send=("x", j), lat=LATX, srcs=[XX(n * k, n * k + n) for k in range(K)], to=[LD(0), LD(1)])
+                add("G", None, [], [XX(0, 6 * n)], ISSUE, send=("x", j), lat=LATX if t < DIRECT else LATD,
+                    behind=("r", NP * t + NP - 1) if t >= DIRECT else None, srcs=[XX(n * k, n * k + n) for k in range(K)], to=[LD(0), LD(1)])
                 add("R", None, [LD(0), LD(1)], [], 0, recv="ax%d" % j, after=("x", j))
                 sums += [(r("pb4", L * b + l0, L * b + l0 + n), rotm, LD(b)) for b in range(2)]
-                if j == NP - 1:
+                if j == 0:
                     mm(r("pb4", 0, 512), r("zero", 0, 128), r("zero", 0, 512), True, False)
-                while sums and j >= NP - 1:
+                while sums:
                     mm(*sums.pop(), False, False, True)
             else:
+                if p == 0:
+                    act(r("accb", 0, 512), r("pb4", 0, 512), F.Copy)
+                mb = bank("fin")
                 for k in range(K):
-                    tt(XX(k, 6 * n, 6), r("payt", 0, W), H("ww", n * k, n * k + n, 1, 6), A.mult, off=M("offu", e * k, e * k + e))
-                    mm(r("pb4", l0, l0 + n), rotm, XX(k, 6 * n, 6), False, False, True)
-                scan(H("mx", 0, 6 * n, 1, 6), r("f6", 0, 6 * n), XX(0, 6 * n), A.mult, A.max)
-                mm(r("pb4", L + l0, L + l0 + n), rotm, H("mx", 5, 6 * n, 6, 6), False, False, True)
-    act(r("outb", 0, 512), r("pb4", 0, 512), F.Copy)
-    dma("Y", "dout", lambda T: T.ys[:, :], r("outb", 0, 256), 2 ** 17)
-    dma("S", "dout", lambda T: T.ym[:, :], r("outb", 256, 512), 2 ** 17)
+                    if k < xs:
+                        act(XX(k, 6 * n, 6), r("payt", 0, W), F.Copy, off=M("offu", 0, e))
+                    else:
+                        tt(XX(k, 6 * n, 6), r("payt", 0, W), H("ww", n * k, n * k + n, 1, 6), A.mult, off=M("offu", e * k, e * k + e))
+                    last = mm(Fp, rotm, XX(k, 6 * n, 6), k == 0, False)
+                    if MT and k:
+                        to = H("mx", 5, 6 * n, 6, 6) if k == K - 1 else O(384, 384 + n)
+                        tt(to, XX(k, 6 * n, 6), XX(0, 6 * n, 6) if k == 1 else O(384, 384 + n), A.max)
+                mm(Fp, blk("iw", 0), r("accb", l0, l0 + n), False, True)
+                if not MT:
+                    scan(H("mx", 0, 6 * n, 1, 6), r("f6", 0, 6 * n), XX(0, 6 * n), A.mult, A.max)
+                mm(r(mb, 0, n), blk("iw", 0), r("accb", L + l0, L + l0 + n), True, False)["x"].append(last["id"])
+                mm(r(mb, 0, n), rotm, H("mx", 5, 6 * n, 6, 6), False, True)
+                act(r("outb", l0, l0 + n), Fp, F.Copy)
+                act(r("outb", L + l0, L + l0 + n), r(mb, 0, n), F.Copy)
+                dma("Y", "dout", lambda T, l0=l0, n=n: T.ys[:, l0:l0 + n], r("outb", l0, l0 + n), 2 ** 16)
+                dma("Y", "dout", lambda T, l0=l0, n=n: T.ym[:, l0:l0 + n], r("outb", L + l0, L + l0 + n), 2 ** 16)
     return ops
 
 
 def kind(o):
-    return "%s%s%d" % (o["e"], (o["o"] or o["i"])[0]["n"], o["part"])
+    x = o["i"][1] if o["e"] == "P" else (o["o"] or o["i"])[0]
+    return "%s%s%d" % (o["e"], x["n"], o["part"])
 
 
 def meet(a, b):
     return a["cm"] & b["cm"] and a["pm"] & b["pm"]
 
 
-def plan():
+def prepare():
     ops = build()
     n = len(ops)
     hist, sends, groups = {}, {}, {}
     for o in ops:
         deps = set(o["x"])
         for x in o["i"]:
-            deps.update(p for (p, y, w) in hist.get(x["n"], []) if w and meet(x, y))
+            deps.update(p for (p, y, w) in hist.get(x["key"], []) if w and meet(x, y))
         for x in o["o"]:
-            deps.update(p for (p, y, w) in hist.get(x["n"], []) if meet(x, y) and not (o.get("acc") and ops[p].get("acc")))
+            deps.update(p for (p, y, w) in hist.get(x["key"], []) if meet(x, y) and not (o.get("acc") and ops[p].get("acc")))
         for x in o["o"]:
             if not o.get("acc"):
-                hist[x["n"]] = [e for e in hist.get(x["n"], []) if (e[1]["cm"] & ~x["cm"]) or (e[1]["pm"] & ~x["pm"])]
-            hist.setdefault(x["n"], []).append((o["id"], x, True))
+                hist[x["key"]] = [e for e in hist.get(x["key"], []) if (e[1]["cm"] & ~x["cm"]) or (e[1]["pm"] & ~x["pm"])]
+            hist.setdefault(x["key"], []).append((o["id"], x, True))
         for x in o["i"]:
-            hist.setdefault(x["n"], []).append((o["id"], x, False))
+            hist.setdefault(x["key"], []).append((o["id"], x, False))
         if "send" in o:
             sends[o["send"]] = o["id"]
         if "after" in o:
@@ -473,7 +609,12 @@ def plan():
             groups.setdefault(o["dma"], []).append(o["id"])
         deps.discard(o["id"])
         o["d"] = deps
-        o["banks"] = set(x["n"] for x in o["i"] + o["o"] if psum(x))
+        o["ps"] = [x for x in o["o"] + o["i"] if psum(x)]
+        o["loan"] = ([x["loan"] for x in o["ps"] if x["loan"]] + [None])[0]
+        o["kind"] = kind(o)
+    for o in ops:
+        if o.get("behind"):
+            o["d"].add(sends[o["behind"]])
     for o in ops:
         for p in list(o["d"]):
             if "dma" in ops[p] and o.get("dma") != ops[p]["dma"]:
@@ -486,6 +627,8 @@ def plan():
     def gap(p, o):
         if p["e"] == "P" and o["e"] == "P":
             return 0.0
+        if "send" in p and "send" in o:
+            return -p["lat"]
         return SAME if p["e"] == o["e"] else CROSS
     order, left = [], [len(o["d"]) for o in ops]
     st = [o["id"] for o in ops if not o["d"]]
@@ -500,8 +643,19 @@ def plan():
     for a in reversed(order):
         o = ops[a]
         pr[a] = o["cost"] + o.get("lat", 0.0) + max([pr[s] + gap(o, ops[s]) for s in succ[a]] + [0.0])
-    pr = [pr[a] + BIAS.get(kind(ops[a]), 0.0) for a in range(n)]
-    free, bank, opened = {}, {}, set()
+    return ops, succ, pr, gap
+
+
+def plan(bias=None, pre=None):
+    ops, succ, pr, gap = pre or prepare()
+    n = len(ops)
+    bias = BIAS if bias is None else bias
+    pr = [pr[a] + bias.get(ops[a]["kind"], 0.0) - STAG * ops[a]["part"] for a in range(n)]
+    for o in ops:
+        if o["loan"]:
+            o["loan"]["bank"] = None
+            o["loan"]["ops"].add(o["id"])
+    free, bank, opened, held = {}, {}, set(), set()
     end, rdy = [0.0] * n, [0.0] * n
     left = [len(o["d"]) for o in ops]
     ready = [o["id"] for o in ops if not o["d"]]
@@ -510,14 +664,21 @@ def plan():
         est = {}
         for a in ready:
             o = ops[a]
-            if o.get("start") and o["o"][0]["n"] in opened:
-                continue
-            s = max(rdy[a], free.get(o["e"], 0.0))
-            for b in o["banks"]:
-                for e2, t2 in bank.get(b, {}).items():
-                    if e2 != o["e"]:
-                        s = max(s, t2 + CROSS)
-            est[a] = s
+            loan = o["loan"]
+            if loan and loan["bank"] is None:
+                choice = [["pb%d" % b] for b in BANKS[loan["use"]] if ("pb%d" % b, loan["use"] == "par") not in held]
+            else:
+                choice = [[place_of(x) for x in o["ps"]]]
+            for banks in choice:
+                if o.get("start") and banks[0] in opened:
+                    continue
+                s = max(rdy[a], free.get(o["e"], 0.0))
+                for b in banks:
+                    for e2, t2 in bank.get(b, {}).items():
+                        if e2 != o["e"]:
+                            s = max(s, t2 + CROSS)
+                if a not in est or s < est[a]:
+                    est[a], o["banks"] = s, banks
         a0 = min(est, key=lambda a: est[a])
         e = ops[a0]["e"]
         a = max([c for c in est if ops[c]["e"] == e and est[c] <= est[a0] + LOOK], key=lambda c: pr[c])
@@ -529,13 +690,24 @@ def plan():
         ready.remove(a)
         seq.append(a)
         o["t0"] = est[a]
+        loan = o["loan"]
+        if loan:
+            if loan["bank"] is None:
+                loan["bank"] = o["banks"][0]
+                held.add((loan["bank"], loan["use"] == "par"))
+            loan["ops"].remove(a)
+            if not loan["ops"]:
+                held.discard((loan["bank"], loan["use"] == "par"))
         if o.get("start"):
-            opened.add(o["o"][0]["n"])
+            opened.add(o["banks"][0])
         if o.get("stop"):
-            opened.discard(o["o"][0]["n"])
+            opened.discard(o["banks"][0])
         if e != "R":
             free[e] = est[a] + o["cost"]
         end[a] = est[a] + o["cost"] + o.get("lat", 0.0)
+        if "nb" in o:
+            free["D"] = max(free.get("D", 0.0), est[a] + 1300) + o["nb"] / BW
+            end[a] = free["D"] + 300
         for b in o["banks"]:
             bank.setdefault(b, {})[e] = est[a] + o["cost"]
         for s in succ[a]:
@@ -543,6 +715,8 @@ def plan():
             left[s] -= 1
             if left[s] == 0:
                 ready.append(s)
+    if pre:
+        return seq
     lastb = {}
     for a in seq:
         o = ops[a]
@@ -570,7 +744,7 @@ def rank_program(g, core, T, topo):
     if rank is None:
         for q in range(N):
             if helper_of(T.cores[q], T, topo) == core:
-                for j in range(NP * (V - 1)):
+                for j in range(NP * DIRECT):
                     t, p = j // NP, j % NP
                     owner = T.cores[(q - t) % N]
                     rid, pid = topo.addr(owner, core)
@@ -578,7 +752,7 @@ def rank_program(g, core, T, topo):
                     g.wait_ge(T.sem["ao%d" % j], 8)
                     g.remote_dma(T.land[:, a:a + 2 * PARTS[p]], T.land[:, a:a + 2 * PARTS[p]], T.sem["ax%d" % j], T.sem.loc,
                                  pid, rid, bits(topo.engines(core, owner)[:8]))
-                g.wait_ge(T.sem.loc, 8 * NP * (V - 1))
+                g.wait_ge(T.sem.loc, 8 * NP * DIRECT)
         return
     if not PLAN:
         PLAN.append(plan())
@@ -603,7 +777,7 @@ def rank_program(g, core, T, topo):
             continue
         want = {}
         for p in o["d"]:
-            if not (e == "P" and ops[p]["e"] == "P"):
+            if not (e == "P" and ops[p]["e"] == "P") and "send" not in ops[p]:
                 want[tok[p][0]] = max(want.get(tok[p][0], 0), tok[p][1])
         for s in sorted(want):
             if waited.get((e, s), 0) < want[s]:
@@ -616,8 +790,12 @@ def rank_program(g, core, T, topo):
                              bits(en))
                 loc += 8
             else:
-                g.remote_dma_fused([RemoteDMATransfer(dst_ids=[DstId(rid=hrid, pnc=hpid)], dma_engine_mask=bits(eh[4 * b:4 * b + 4]),
-                                                      remote_sem=T.sem["ao%d" % j], srcs=[ap(T, x) for x in o["srcs"]],
+                rid, pid, eng, sem = hrid, hpid, eh, "ao%d" % j
+                if j >= NP * DIRECT:
+                    owner = T.cores[(rank - j // NP) % N]
+                    (rid, pid), eng, sem = topo.addr(owner, core), topo.engines(core, owner)[-8:], "ax%d" % j
+                g.remote_dma_fused([RemoteDMATransfer(dst_ids=[DstId(rid=rid, pnc=pid)], dma_engine_mask=bits(eng[4 * b:4 * b + 4]),
+                                                      remote_sem=T.sem[sem], srcs=[ap(T, x) for x in o["srcs"]],
                                                       dsts=[ap(T, o["to"][b])], alu_op=1 + b) for b in range(2)], local_sem=T.sem.loc)
                 loc += 8
             continue

@@ -6,25 +6,29 @@ W, K, L, V = 2048, 6, 256, 5
 PARTS = [128, 128]
 VS = 2
 SUB = 128
-LATE = 0
+LATE = -1
 GV = [2, 0, 0, 0]
 MV = 1
 KO = 3
-SF = 0
+SF = 1
 ZS = 0
-TS = 1
+TS = 128
 MT = 0
 O1S = 1
 OUS = 1
+O2S = 0
 SPL = 0
 KV = 0
+WIDE = 1
+FV = 1
+EARLY = 0
 W0 = 0
-ZC = "GG"
+ZC = "SG"
 XS = 1
 REP = 3
 GP = 3
-NCH = 4
-CW = W // NCH
+CUTS = [0, 256, 768, 1280, 1792, 1920, 2048]
+NCH = len(CUTS) - 1
 NP = len(PARTS)
 BANKS = {"own": [5, 6], "dif": [0, 1, 2], "par": [0, 1, 2], "st": [3], "vt": [7], "pay": [0, 1, 2], "fin": [3, 7]}
 PCY = 0.45
@@ -32,13 +36,13 @@ CYC, FIX = 0.83, 30.0
 SAME, CROSS, LOOK = 150.0, 280.0, 0.0
 ALPHA = 0.6
 STAG = 2000.0
-BIAS = {'Sra0': -3700, 'Pxx1': -9800, 'Pmg0': -300, 'Vs11': 4700, 'Pcc0': 8700, 'Gmc00': -3300, 'Vpq0': -9800, 'Vmg0': -2600, 'Pdfr0': 12600, 'Gval0': 16000, 'Gfss0': -3400, 'Pzdl0': 6800, 'Gdm0': -5800, 'Vmsk1': -10200, 'Gccx0': -2700, 'Pp61': 400, 'Voff21': -5700, 'Skla0': -1800, 'Vxx0': -1500, 'Gs10': 2700, 'Smc01': -2000, 'Vmc00': -15000, 'Vpb61': 1500, 'Sxx1': 5300}
+BIAS = {'Vs11': 18000, 'Pcc0': 17100, 'Vmg0': -8100, 'Pdfr0': 14300, 'Pp61': 5900, 'Voff21': -14000, 'Sxx1': 12600, 'Swin0': 13500, 'Voutb0': -16800, 'Sww1': 6100, 'Vmsk0': -23600, 'Gdm0': -5400, 'Vxs1': 5000, 'Vpq0': -500, 'Pact1': -7300, 'Smc00': 6400, 'Vstg0': 13300, 'Pland1': -4900, 'Vpb50': 3500, 'Vcr0': 6800, 'Ssg1': 13500, 'Gmc00': -2300, 'Sra0': -11200, 'Vlo0': -3100, 'Pland0': -11600, 'Vklb0': -1400, 'Vhi0': 1400, 'Gfss0': 600, 'Gval0': -1000, 'Vscn1': 1400, 'Giw0': -2000, 'Vxx0': -300, 'Vpc0': -1000}
 LATS = 3000.0
 LATX = 19000.0
 LATD = 11000.0
 DIRECT = 3
 ISSUE = 400.0
-BW = 180.0
+BW = 230.0
 
 f32, bf, f16, i32, u16 = "float32", "bfloat16", "float16", "int32", "uint16"
 LP = L + 16 * NP
@@ -199,8 +203,8 @@ def build():
     SENT = 1900.5 - E12
     NS = 4 - VS
     for c in range(NCH):
-        dma("Y", "dar%d" % c, blk("raw", c, CW), lambda T, c=c: T.arcs[:, c * CW:(c + 1) * CW], 128 * CW * 4)
-    dma("S", "dst", view("sti", (slice(0, K), slice(0, 16))), lambda T: T.st0[:, :], 49152)
+        dma("Y", "dar%d" % c, r("raw", CUTS[c], CUTS[c + 1]), lambda T, c=c: T.arcs[:, CUTS[c]:CUTS[c + 1]], 512 * (CUTS[c + 1] - CUTS[c]))
+    dma("Y", "dst", view("sti", (slice(0, K), slice(0, 16))), lambda T: T.st0[:, :], 49152)
     ms(r("rsi", 0, L), 1)
     for gq in range(8):
         p = 16 * ((gq - 1) % 8)
@@ -302,12 +306,13 @@ def build():
         act(r("kla", 128 * b + 13, 128 * b + 128, 16), r("bm", 16, 144, 16), F.Identity, scale=pq(9, b, b + 1))
         if b >= NS:
             act(r("kla", 128 * b + 14, 128 * b + 128, 16), r("bm", 16, 144, 16), F.Identity, scale=pcol(14) if b == 4 else -2.0 ** 19)
-        to = r("pb%d" % (5 + b // 4), 128 * (b % 4), 128 * (b % 4) + 128)
+        to = r("pb7" if b // 4 else "pb3", 128 * (b % 4), 128 * (b % 4) + 128)
         mm(to, blk("kla", b), blk("idb", 0), True, False)
         mm(to, blk("klb", b), blk("idb", 1), False, True)
-    for a, b, pbk in ((0, 512, "pb5"), (512, 640, "pb6")):
-        act(r("dc", a, b), r(pbk, 0, b - a), F.Identity, scale=2.0 ** -22)
-        act(r("dd", a, b), r(pbk, 0, b - a), F.Identity, scale=0.25)
+    made = []
+    for a, b, pbk in ((0, 512, "pb3"), (512, 640, "pb7")):
+        made.append(act(r("dc", a, b), r(pbk, 0, b - a), F.Identity, scale=2.0 ** -22)["id"])
+        made.append(act(r("dd", a, b), r(pbk, 0, b - a), F.Identity, scale=0.25)["id"])
     mm(r("pb4", 0, 128 * NS), blk("idb", 0), r("kla", 0, 128 * NS), True, False)
     mm(r("pb4", 0, 128 * NS), blk("idb", 1), r("klb", 0, 128 * NS), False, True)
     for b in range(2):
@@ -334,16 +339,20 @@ def build():
         fill(r("ww", 6 * l0, 6 * l0 + n), 1)
     act(r("rf0", 0, L), r("rsi", 0, L), F.Copy)
     for c in range(NCH):
-        a, b = c * CW, (c + 1) * CW
+        a, b = CUTS[c], CUTS[c + 1]
+        CW, first = b - a, len(ops)
         ts(r("hi", a, b), r("raw", a, b), 15, None, A.logical_shift_right)
         lo = r("win", W + a, W + b) if len(ZC) == 1 else r("lo", a, b)
         lolast = ts(lo, r("raw", a, b), 32767, None, A.bitwise_and)
-        if TS:
-            act(r("pb%d" % (c % 4), 0, CW), r("hi", a, b), F.Copy)
-            tt(r("mn", a, b), lo, r("pb%d" % (c % 4), 0, CW), A.min)
+        if CW > TS:
+            act(r("pb%d" % (c % 3), 0, CW), r("hi", a, b), F.Copy)
+            tt(r("mn", a, b), lo, r("pb%d" % (c % 3), 0, CW), A.min)
         else:
             tt(r("mn", a, b), lo, r("hi", a, b), A.min)
-        act(r("mnb", a, b), r("mn", a, b), F.Identity, bias=191.5 + E12, scale=1.0 / 2048)
+        vlast = len(ops) - 1
+        mnlast = act(r("mnb", a, b), r("mn", a, b), F.Identity, bias=191.5 + E12, scale=1.0 / 2048)
+        for o in ops[first:]:
+            o["boost"] = 50000.0 - 3000.0 * c
         for q, to, src in zip(ZC, (r("win", a, b), r("win", W + a, W + b)), (r("hi", a, b), lo)):
             if q == "S":
                 act(to, src, F.Copy)
@@ -360,6 +369,11 @@ def build():
                     o = (1 - par) * W
                     dma("Y", "dw%d" % (a // (W // 2)), r("win", o + a, o + b, 1, u, 128, 2), r(nm, a, b, 1, par, 128, 2), 2 ** 18)
     dma("Y", "dpay", r("payt", 0, W), lambda T: T.pay[:, :], 2 ** 19)["x"].append(lolast["id"])
+    for o in ops:
+        if o["e"] == "S" and o["o"][0]["n"] in ("dc", "dd", "kl0", "iwb", "tmpc"):
+            o["x"].append(mnlast["id"])
+        if o.get("dma", "")[:3] == "dar":
+            o["boost"] = 90000.0 - 5000.0 * o["id"]
 
     def lists(out, src, scalar):
         if scalar:
@@ -400,6 +414,7 @@ def build():
                 for nm, c0, c1 in waves:
                     add("R", None, [M("zdl", c0, c1, 1, t - 1)], [], 0, recv="a%s%d" % (nm, jl), after=(nm, jl))
                     turn_lists(lambda a, b, s: O(256 + c0 + a, 256 + c0 + b, s), lambda h0: M("zdl", c0 + h0, c1, 2, t - 1), "iwb", 1, True, True, c1 - c0)
+                    conv = ops[-1]
                     lists(M("off1", c0, c1), O(256 + c0, 256 + c1), O1S)
             cw = 8 if t == 0 else 7
             mc = "mc0" if t == 0 else "mc"
@@ -412,20 +427,22 @@ def build():
                 for a in range(0, n, sub):
                     b = min(n, a + sub)
                     o = act(H(mc, cw * a + 5 - k, cw * b, cw, cw), r("mnb", 0, W), F.Identity, bias=-192.0, off=M("off1", e * k + a // 16, e * k + b // 16))
-                    if k == (SPL if t else 0) + LATE:
+                    if k <= (SPL if t else 0) + max(LATE, 0):
                         gat[a // SUB] = o["id"]
             nc = -(-cw * n // 448)
             for a, b in ((n * c // nc, n * (c + 1) // nc) for c in range(nc)):
                 bk = bank("dif")
-                mm(r(bk, cw - 1, cw * (b - a), cw), blk("iw", 0), H("act", a, b), True, True)["x"].append(gat[a // SUB])
+                mm(r(bk, cw - 1, cw * (b - a), cw), blk("iw", 0), H("act", a, b), True, True)["x"].append(
+                    vlast if j == 0 else gat[a // SUB] if LATE >= 0 or not t else conv["id"])
                 for jj in range(cw - 1):
                     mm(r(bk, jj, cw * (b - a), cw), blk("dl", jj) if jj < K else r("rk", 0, 128), rfin(a, b), True, True)["x"].append(len(ops) - 2)
-                scan(H("scn", cw * a, cw * b, 1, 8), r(bk, 0, cw * (b - a)), H(mc, cw * a, cw * b, 1, cw), A.add, A.min)
+                lastscn = scan(H("scn", cw * a, cw * b, 1, 8), r(bk, 0, cw * (b - a)), H(mc, cw * a, cw * b, 1, cw), A.add, A.min)
             x0 = l0 + 16 * p
             SS = O(384, 384 + n)
             tr(r("xs", x0 + 16, x0 + 16 + n), H("scn", cw - 1, cw * n, cw, 8))
             early = scan(SS, r("xs", x0 + 15, x0 + 15 + n), r("fss", 0, n), A.min, A.max)
             tt(r("ge", x0, x0 + n), r("xs", x0 + 16, x0 + 16 + n), SS, A.is_ge)
+            early = lastscn if EARLY else early
             direct = W0 and t == 0
             if not direct:
                 scan(H("ps"), r("fpar", 0, n), r("ge", x0, x0 + n), A.add, A.mult)
@@ -448,7 +465,7 @@ def build():
                 for k in range(0, KO, REP):
                     turn_lists(lambda a, b, s: PA(e * k + a, e * k + b, s), lambda h0: H("ps", 15 + 16 * h0, n, 32) if REP == 1 else M("p6", h0, e * REP, 2),
                                "iwb", 0, False, k == KO - REP, e * REP)
-                ts(M("off2", c0, c1), PA(0, c1 - c0), 2048.0, 1023.5, A.mult, A.add)
+                lists(M("off2", c0, c1), PA(0, c1 - c0), O2S > (k0 == 0))
             mm(Mp, r("dm0" if direct else "dm", 0, 128), H("stg"), True, True)
             if direct:
                 cm_ = act(H("msk"), Mp, F.Relu, bias=ccol(30))
@@ -471,14 +488,14 @@ def build():
             for bs in sets[::-1] if SF else sets:
                 if ZS:
                     whole = r(stb, 0, n * (NS + 1)) if 4 in bs else r(vb, v0, v0 + n * VS)
-                    mm(whole, r("zero", 0, 128), r("zero", 0, whole["w"]), True, False)["x"].append(lastg["id"])
+                    mm(whole, r("zero", 0, 128), r("zero", 0, whole["w"]), True, False)["x"] += [lastg["id"]] + made * (t == 0)
                     for b in bs:
                         mm(place(b), blk("dc", b), H("cc"), False, False)
                     for b in bs:
                         mm(place(b), blk("dd", b), H("dfr"), False, b == bs[-1])
                 else:
                     for b in bs:
-                        mm(place(b), blk("dc", b), H("cc"), True, False)["x"].append(len(ops) - 2)
+                        mm(place(b), blk("dc", b), H("cc"), True, False)["x"] += [len(ops) - 2] if b != bs[0] else made * (t == 0)
                         mm(place(b), blk("dd", b), H("dfr"), False, True)
             SG = lambda a, b: H("sg", n * a, n * b, 1, 13)
             CQ = 1.5 * 2.0 ** 21
@@ -493,6 +510,9 @@ def build():
                 s1 = s0 + NS + 1 + NS * v
                 act(SG(s1, s1 + NS), r(stb, 0, n * NS), F.Sign, bias=0.25, scale=1.0 if v else -1.0)
                 kills += [(blk("klb" if v else "kla", b), s1 + b) for b in range(NS)]
+            if SF:
+                a, b = 2 * VS + NS + 1, 2 * VS + 2 * NS + 1
+                kills = kills[2 * VS:a] + kills[:VS] + kills[a:b] + kills[VS:2 * VS] + kills[b:]
             Xp = Mp
             for i, (lh, s) in enumerate(kills):
                 mm(Xp, lh, SG(s, s + 1), i == 0, False)
@@ -527,7 +547,7 @@ def build():
             for k0, k1 in ((1, 4), (4, 6)) if 5 * n > 448 else ((1, 6),):
                 bk = bank("pay")
                 for k in range(k0, k1):
-                    mm(r(bk, n * (k - k0), n * (k - k0 + 1)), r("rk", 144 * k + 16, 144 * k + 144), rfo(), True, True)
+                    mm(r(bk, n * (k - k0), n * (k - k0 + 1)), r("rk", 144 * k + 16, 144 * k + 144), rfo(), True, True)["boost"] = 5000.0 * (t == V - 1)
                 turn[1] += 1
                 if k0 < xs:
                     act(H("pg", n * k0, n * k1, 1, 6), r("payt", 0, W), F.Copy, off=M("offu", e * k0, e * k1))
@@ -553,7 +573,7 @@ def build():
                     mm(*sums.pop(), False, False, True)
             else:
                 if p == 0:
-                    act(r("accb", 0, 512), r("pb4", 0, 512), F.Copy)
+                    act(r("accb", 0, L if FV else 512), r("pb4", 0, L if FV else 512), F.Copy)
                 mb = bank("fin")
                 for k in range(K):
                     if k < xs:
@@ -567,10 +587,14 @@ def build():
                 mm(Fp, blk("iw", 0), r("accb", l0, l0 + n), False, True)
                 if not MT:
                     scan(H("mx", 0, 6 * n, 1, 6), r("f6", 0, 6 * n), XX(0, 6 * n), A.mult, A.max)
-                mm(r(mb, 0, n), blk("iw", 0), r("accb", L + l0, L + l0 + n), True, False)["x"].append(last["id"])
-                mm(r(mb, 0, n), rotm, H("mx", 5, 6 * n, 6, 6), False, True)
                 act(r("outb", l0, l0 + n), Fp, F.Copy)
-                act(r("outb", L + l0, L + l0 + n), r(mb, 0, n), F.Copy)
+                if FV:
+                    for a, b in ((0, 64), (64, 0)):
+                        tt(r("outb", L + l0, L + l0 + n, 1, a, a + 64), r("mx", 6 * l0 + 5, 6 * l0 + 6 * n, 6, b, b + 64), r("pb4", L + l0, L + l0 + n, 1, a, a + 64), A.add)
+                else:
+                    mm(r(mb, 0, n), blk("iw", 0), r("accb", L + l0, L + l0 + n), True, False)["x"].append(last["id"])
+                    mm(r(mb, 0, n), rotm, H("mx", 5, 6 * n, 6, 6), False, True)
+                    act(r("outb", L + l0, L + l0 + n), r(mb, 0, n), F.Copy)
                 dma("Y", "dout", lambda T, l0=l0, n=n: T.ys[:, l0:l0 + n], r("outb", l0, l0 + n), 2 ** 16)
                 dma("Y", "dout", lambda T, l0=l0, n=n: T.ym[:, l0:l0 + n], r("outb", L + l0, L + l0 + n), 2 ** 16)
     return ops
@@ -650,7 +674,7 @@ def plan(bias=None, pre=None):
     ops, succ, pr, gap = pre or prepare()
     n = len(ops)
     bias = BIAS if bias is None else bias
-    pr = [pr[a] + bias.get(ops[a]["kind"], 0.0) - STAG * ops[a]["part"] for a in range(n)]
+    pr = [pr[a] + ops[a].get("boost", 0.0) + bias.get(ops[a]["kind"], 0.0) - STAG * ops[a]["part"] for a in range(n)]
     for o in ops:
         if o["loan"]:
             o["loan"]["bank"] = None
@@ -738,6 +762,10 @@ def bits(engines):
     return sum(1 << e for e in engines)
 
 
+def lanes_engines(src, dst, j, topo):
+    return topo.engines(src, dst)[:16 if j >= NP and WIDE else 8]
+
+
 def rank_program(g, core, T, topo):
     rank = T.rank_of(core)
     N = len(T.cores)
@@ -772,7 +800,7 @@ def rank_program(g, core, T, topo):
         o = ops[a]
         e = o["e"]
         if e == "R":
-            tok[a] = (o["recv"], 8)
+            tok[a] = (o["recv"], 8 if o["after"][0] == "x" else len(lanes_engines(T.cores[(rank - 1) % N], core, o["after"][1], topo)))
             cnt[o["recv"]] = tok[a][1]
             continue
         want = {}
@@ -786,9 +814,9 @@ def rank_program(g, core, T, topo):
         if "send" in o:
             kind, j = o["send"]
             if kind != "x":
-                g.remote_dma(ap(T, o["to"]), ap(T, o["i"][0]), T.sem["a%s%d" % (kind, j)], T.sem.loc, npid, nrid,
-                             bits(en))
-                loc += 8
+                eng = lanes_engines(core, nxt, j, topo)
+                g.remote_dma(ap(T, o["to"]), ap(T, o["i"][0]), T.sem["a%s%d" % (kind, j)], T.sem.loc, npid, nrid, bits(eng))
+                loc += len(eng)
             else:
                 rid, pid, eng, sem = hrid, hpid, eh, "ao%d" % j
                 if j >= NP * DIRECT:

import numpy as np
from concourse.bass import DstId, RemoteDMATransfer
from concourse.mybir import AluOpType as A, ActivationFunctionType as F

W, K, L, V = 2048, 6, 256, 5
PARTS = [128, 128]
VS = 2
SUB = 128
LATE = -1
GV = [2, 0, 0, 0]
MV = 1
KO = 3
SF = 1
ZS = 0
TS = 128
MT = 0
O1S = 1
OUS = 1
O2S = 0
SPL = 0
KV = 0
WIDE = 1
FV = 1
EARLY = 0
W0 = 0
ZC = "SG"
XS = 1
REP = 3
GP = 3
CUTS = [0, 256, 768, 1280, 1792, 1920, 2048]
NCH = len(CUTS) - 1
NP = len(PARTS)
BANKS = {"own": [5, 6], "dif": [0, 1, 2], "par": [0, 1, 2], "st": [3], "vt": [7], "pay": [0, 1, 2], "fin": [3, 7]}
PCY = 0.45
CYC, FIX = 0.83, 30.0
SAME, CROSS, LOOK = 150.0, 280.0, 0.0
ALPHA = 0.6
STAG = 2000.0
BIAS = {'Vs11': 18000, 'Pcc0': 17100, 'Vmg0': -8100, 'Pdfr0': 14300, 'Pp61': 5900, 'Voff21': -14000, 'Sxx1': 12600, 'Swin0': 13500, 'Voutb0': -16800, 'Sww1': 6100, 'Vmsk0': -23600, 'Gdm0': -5400, 'Vxs1': 5000, 'Vpq0': -500, 'Pact1': -7300, 'Smc00': 6400, 'Vstg0': 13300, 'Pland1': -4900, 'Vpb50': 3500, 'Vcr0': 6800, 'Ssg1': 13500, 'Gmc00': -2300, 'Sra0': -11200, 'Vlo0': -3100, 'Pland0': -11600, 'Vklb0': -1400, 'Vhi0': 1400, 'Gfss0': 600, 'Gval0': -1000, 'Vscn1': 1400, 'Giw0': -2000, 'Vxx0': -300, 'Vpc0': -1000}
LATS = 3000.0
LATX = 19000.0
LATD = 11000.0
DIRECT = 3
ISSUE = 400.0
BW = 230.0

f32, bf, f16, i32, u16 = "float32", "bfloat16", "float16", "int32", "uint16"
LP = L + 16 * NP


def _sb(n, d):
    return ("sbuf", [128, n], d)


SCRATCH = {
    "raw": _sb(W, i32), "lo": _sb(W, i32), "hi": _sb(W, i32), "mn": _sb(W, f32), "mnb": _sb(W, bf), "win": _sb(2 * W, i32),
    "payt": _sb(W, bf), "act": _sb(L, f32), "sti": ("sbuf", [128, K, 16], i32), "rsi": _sb(L, i32),
    "sf0": _sb(96, f16), "rf0": _sb(L, bf),
    "val": _sb(144, bf), "bm": _sb(144, bf), "cob": _sb(128, bf), "col": _sb(144, f32), "self0": _sb(144, f32), "dm0": _sb(128, bf), "pi": _sb(8, i32), "pc": _sb(16, f32),
    "ee": _sb(16, f32), "cr": _sb(32, f32), "pq": _sb(96, f32),
    "rk": _sb(6 * 144, bf), "dl": _sb(6 * 128, bf), "one": _sb(128, f32), "self": _sb(136, f32),
    "ra": _sb(128, bf), "tmpc": _sb(256, bf), "dm": _sb(128, bf), "iw": _sb(256, f32), "iwb": _sb(512, bf),
    "idb": _sb(256, bf), "ccx": _sb(128, bf), "kla": _sb(640, bf), "klb": _sb(640, bf), "kl0": _sb(512, bf),
    "dc": _sb(640, bf), "dd": _sb(640, bf), "accb": _sb(512, f32),
    "fss": _sb(128, f32), "fs1": _sb(128, f32), "frv": _sb(128, bf), "fpar": _sb(128, bf), "thr": _sb(64, f32), "f6": _sb(768, bf),
    "zero": _sb(512, bf),
    "mc0": _sb(8 * L, bf), "mc": _sb(7 * L, bf), "scn": _sb(8 * L, f32), "xs": _sb(LP, f32), "ge": _sb(LP, bf),
    "step": _sb(L, bf), "ps": _sb(L, bf), "stg": _sb(L, bf), "msk": _sb(L, f32), "p6": _sb(96, bf),
    "off1": _sb(96, u16), "off2": _sb(96, u16), "offu": _sb(96, u16), "mg": _sb(12 * L, f32), "cc": _sb(L, bf), "dfr": _sb(L, f16),
    "sg": _sb(13 * L, bf), "xt": _sb(L, f32), "s1": _sb(6 * L + 16 * NP, f32), "ka": _sb(96, f32),
    "kr": _sb(128, f32), "df": _sb(128, f32), "rt": _sb(L, bf), "ww": _sb(6 * L, f32), "pg": _sb(6 * L, bf), "mx": _sb(6 * L, f32), "outb": _sb(512, f32),
    "zds": _sb(5 * 96, f16), "zdl": _sb(4 * 96, f16), "rfs": _sb(5 * L, bf), "rfl": _sb(4 * L, bf),
    "xx": _sb(30 * L, f32), "land": _sb(8 * L, f32),
}
for _b in range(8):
    SCRATCH["pb%d" % _b] = ("psum", [128, 512], f32)

SEMAPHORES = (["eV", "eS", "eP", "eG", "loc", "dst", "drs", "dac", "dpay", "dw0", "dw1", "dout"] + ["d%s%d" % (s, c) for s in ("ar", "wa", "wb") for c in range(NCH)]
              + ["a%s%d" % (s, j) for s in "eorx" for j in range(4 * NP)])


def bitmask(idx):
    m = np.zeros(int(np.max(idx)) + 1, np.uint8)
    m[idx] = 1
    return int.from_bytes(np.packbits(m, bitorder="little").tobytes(), "little")


def view(name, cols, part=slice(0, 128)):
    loan = name if isinstance(name, dict) else None
    name = "pb0" if loan else name
    shape = SCRATCH[name][1][1:]
    idx = np.arange(int(np.prod(shape))).reshape(shape)[cols].ravel()
    return {"n": name, "loan": loan, "key": loan["key"] if loan else name, "ix": (part,) + cols, "cm": bitmask(idx), "pm": bitmask(np.arange(128)[part]), "w": len(idx)}


def reg(name, c0, c1, cs=1, p0=0, p1=128, ps=1):
    return view(name, (slice(c0, c1) if cs == 1 else slice(c0, c1, cs),), slice(p0, p1) if ps == 1 else slice(p0, p1, ps))


def rev(name, c0, c1):
    return view(name, (slice(c1 - 1, c0 - 1 if c0 else None, -1),))


def place_of(r):
    return r["loan"]["bank"] if r["loan"] else r["n"]


def ap(T, r):
    return T[place_of(r)][r["ix"]] if isinstance(r, dict) else r


def two(r):
    return SCRATCH[r["n"]][2] in (bf, u16, f16)


def psum(r):
    return SCRATCH[r["n"]][0] == "psum"


def build():
    ops = []
    grp = [0, None, False]

    def add(eng, emit, outs, ins, cost, **kw):
        o = {"e": eng, "f": emit, "o": outs, "i": [x for x in ins if isinstance(x, dict)], "cost": cost, "id": len(ops), "x": [], "part": grp[0], "last": grp[2]}
        o.update(kw)
        ops.append(o)
        return o

    def vc(n):
        return FIX + max(64, n) * CYC

    def half(rs):
        return 0.5 if all(two(r) for r in rs) else 1.0

    def ts(out, in0, s1, s2, op0, op1=None):
        def f(g, T):
            if op1 is None:
                return g.vector.tensor_scalar(ap(T, out), ap(T, in0), ap(T, s1), None, op0)
            return g.vector.tensor_scalar(ap(T, out), ap(T, in0), ap(T, s1), ap(T, s2), op0, op1)
        return add("V", f, [out], [in0, s1, s2], vc(out["w"] * half([out, in0])))

    def tt(out, a, b, op, off=None):
        if off:
            return add("V", lambda g, T: g.vector.tensor_tensor(ap(T, out), ap(T, a).indirect(ap(T, off)), ap(T, b), op), [out], [a, b, off],
                       50 + out["w"] * 1.56 * CYC, gat=out["w"])
        return add("V", lambda g, T: g.vector.tensor_tensor(ap(T, out), ap(T, a), ap(T, b), op), [out], [a, b],
                   vc(out["w"] * (1 if (psum(a) or psum(b)) else 2)))

    def tsg(out, a, c, off):
        return add("V", lambda g, T: g.vector.tensor_scalar(ap(T, out), ap(T, a).indirect(ap(T, off)), c, None, A.add), [out], [a, off],
                   50 + out["w"] * 1.56 * CYC, gat=out["w"])

    def cp(out, a):
        return add("V", lambda g, T: g.vector.tensor_copy(ap(T, out), ap(T, a)), [out], [a], vc(out["w"] * half([out, a])))

    def scan(out, d0, d1, op0, op1):
        return add("V", lambda g, T: g.vector.tensor_tensor_scan(ap(T, out), ap(T, d0), ap(T, d1), 0.0, op0, op1), [out], [d0, d1],
                   vc(out["w"] * half([out, d0, d1])))

    def tr(out, a):
        return add("V", lambda g, T: g.vector.transpose(ap(T, out), ap(T, a)), [out], [a], vc(out["w"] * half([out, a])))

    def ms(out, v):
        return add("V", lambda g, T: g.vector.memset(ap(T, out), v), [out], [], vc(out["w"] * half([out])))

    def act(out, a, func, bias=0.0, scale=1.0, off=None, extra=0.0):
        def f(g, T):
            src = ap(T, a).indirect(ap(T, off)) if off else ap(T, a)
            if func == F.Copy:
                return g.scalar.activation(ap(T, out), src, func)
            return g.scalar.activation(ap(T, out), src, func, bias=ap(T, bias), scale=ap(T, scale))
        return add("S", f, [out], [a, off, bias, scale], extra + ((65 + out["w"] * 1.56 * CYC) if off else vc(out["w"])), gat=out["w"] if off else 0)

    def mm(out, l, r_, start, stop, acc=False):
        o = add("P", lambda g, T, close=False: g.tensor.matmul(ap(T, out), ap(T, l), ap(T, r_), start, stop or close), [out], [l, r_],
                max(64, out["w"]) * (1 if two(l) else 4) * PCY + 5, start=start, stop=stop, acc=acc)
        if not acc:
            if not start:
                o["x"].append(grp[1])
            grp[1] = o["id"]
        return o

    def iota(out, pat, base, cm):
        def f(g, T):
            if SCRATCH[out["n"]][2] == i32:
                return g.iota(ap(T, out), pat, base, cm)
            return g.iota(ap(T, out), pat, base, cm, allow_small_or_imprecise_dtypes=True)
        return add("G", f, [out], [], 130 + 2 * out["w"] * CYC)

    def sel(out, a, pat, op, fill, base, cm):
        return add("G", lambda g, T: g.affine_select(ap(T, out), ap(T, a), pat, op, fill, base, cm), [out], [a], 170 + 2 * out["w"] * CYC)

    def dma(q, sem, out, src, nbytes):
        def f(g, T):
            return (g.sync if q == "Y" else g.scalar).dma_start(ap(T, out) if isinstance(out, dict) else out(T),
                                                                ap(T, src) if isinstance(src, dict) else src(T))
        return add(q, f, [out] if isinstance(out, dict) else [], [src], 60, dma=sem, lat=1600 + nbytes / BW, nb=nbytes)

    r = reg
    blk = lambda n, j, w=128: r(n, w * j, w * j + w)
    E12, MAG, KILL = 2.0 ** -12, 1.5 * 2.0 ** 23, 4096.0
    SENT = 1900.5 - E12
    NS = 4 - VS
    for c in range(NCH):
        dma("Y", "dar%d" % c, r("raw", CUTS[c], CUTS[c + 1]), lambda T, c=c: T.arcs[:, CUTS[c]:CUTS[c + 1]], 512 * (CUTS[c + 1] - CUTS[c]))
    dma("Y", "dst", view("sti", (slice(0, K), slice(0, 16))), lambda T: T.st0[:, :], 49152)
    ms(r("rsi", 0, L), 1)
    for gq in range(8):
        p = 16 * ((gq - 1) % 8)
        dma("S", "drs", r("rsi", 0, L, 1, p, p + 12, 2), lambda T, gq=gq: T.rs0[gq, :], 6144)
    dma("Y", "dac", r("act", 0, L), lambda T: T.ac[:, :], 2 ** 17)
    iota(r("pi", 0, 1), [[0, 1]], 0, 1)
    iota(r("val", 0, 16), [[0, 16]], -112, 1)
    iota(r("val", 16, 144), [[-16, 8], [0, 16]], 0, 1)
    iota(r("col", 0, 144), [[1, 144]], -16, 0)
    iota(r("one", 0, 128), [[0, 128]], 1, 0)
    for b in range(2):
        sel(blk("iw", b), r("one", 0, 128), [[-1, 128]], A.is_equal, 0.0, 0, 1)
    iota(r("cob", 0, 128), [[1, 128]], 0, 0)
    fill = lambda out, v: iota(out, [[0, out["w"]]], int(v), 0)
    pcol = lambda j: r("pc", j, j + 1)
    picol = lambda j: r("pi", j, j + 1)
    ecol = lambda j: r("ee", j, j + 1)
    ccol = lambda j: r("cr", j, j + 1)
    ts(picol(1), picol(0), 0x70, None, A.bitwise_and)
    ts(picol(2), picol(0), 1, None, A.bitwise_and)
    ts(picol(3), picol(0), 15, None, A.bitwise_and)
    ts(picol(5), picol(0), 4, 1, A.logical_shift_right, A.bitwise_and)
    cp(pcol(3), picol(3))
    ts(r("bm", 0, 144), r("val", 0, 144), pcol(3), None, A.is_equal)
    ts(r("ee", 0, 16), r("col", 16, 32), pcol(3), None, A.is_equal)
    ts(pcol(4), ecol(13), 64.0, None, A.mult)
    ts(r("cr", 25, 30), r("ee", 3, 12, 2), -64.0, pcol(4), A.mult, A.add)
    tt(r("cr", 1, 6), r("ee", 2, 12, 2), r("cr", 25, 30), A.add)
    cp(ccol(0), ecol(0))
    ts(ccol(8), ecol(13), 1024.0, None, A.mult)
    tt(r("cr", 9, 14), rev("cr", 1, 6), rev("cr", 0, 5), A.subtract)
    ts(pcol(10), ecol(15), E12, None, A.mult)
    ts(pcol(11), ecol(13), -64.5, pcol(10), A.mult, A.add)
    ts(r("cr", 16, 22), r("cr", 0, 6), pcol(11), None, A.add)
    for j in range(K):
        act(blk("dl", j), r("bm", 0, 128), F.Identity, scale=ccol(8 + j))
    for k in range(K):
        act(blk("rk", k, 144), r("bm", 0, 144), F.Identity, scale=ccol(k))
    fill(r("ra", 0, 128, 16), 0)
    fill(r("ra", 15, 128, 16), 0)
    for y in range(1, 15):
        act(r("ra", y, 128, 16), r("bm", y, 128, 16), F.Identity, scale=ccol(16 + (y - 1) % 6) if y < 13 else ecol(13))
    ts(pcol(0), picol(2), 6.0, 1.0, A.mult, A.add)
    tt(pcol(1), pcol(0), picol(1), A.add)
    ts(pcol(6), picol(5), 0.0, None, A.is_equal)
    ts(pcol(7), picol(5), 1.0, None, A.is_equal)
    ts(r("self", 0, 136), r("col", 8, 144), pcol(1), 1.0 / 2048, A.is_equal, A.mult)
    dm, pair, group = r("dm", 0, 128), [[-2, 64], [0, 2]], [[-16, 8], [0, 16]]
    if W0:
        cp(ccol(31), picol(1))
        ts(r("self0", 0, 144), r("col", 0, 144), ccol(31), 1.0 / 2048, A.is_equal, A.mult)
        ts(ccol(30), pcol(3), -14.0, None, A.add)
        dm0 = r("dm0", 0, 128)
        fill(dm0, 1)
        sel(dm0, dm0, [[-1, 128]], A.is_gt, 0.0, 0, 1)
        sel(dm0, dm0, [[-1, 128]], A.not_equal, -1.0, 0, 1)
        sel(dm0, dm0, [[16, 8], [0, 16]], A.is_ge, 0.0, 15, -1)
    if MV:
        fill(dm, 2)
        sel(dm, dm, pair, A.is_ge, -1.0, -2, 1)
        sel(dm, dm, pair, A.is_ge, 0.0, 0, 1)
        sel(dm, dm, [[16, 8], [0, 16]], A.is_ge, 0.0, 15, -1)
        tt(pcol(5), picol(3), picol(2), A.subtract)
        ts(pcol(15), pcol(5), -2.0, 26.5, A.mult, A.add)
    else:
        fill(dm, 0)
        sel(dm, dm, pair, A.not_equal, 1.0, -1, 1)
        sel(dm, dm, pair, A.not_equal, -1.0, 1, 1)
        sel(dm, dm, group, A.is_ge, 0.0, 0, 1)
    for c0 in range(2):
        act(blk("iwb", c0, 256), r("iw", 0, 256), F.Identity, scale=pcol(6 + c0))
        act(blk("idb", c0), blk("iw", 0), F.Identity, scale=1.0 - 2 * c0)
    pq = lambda j, a=0, b=5: r("pq", 8 * j + a, 8 * j + b)
    ts(pq(0), r("col", 16, 96, 16), pcol(3), None, A.add)
    ts(pq(0, 4, 5), picol(2), 64.0, None, A.add)
    ts(pq(1), pq(0), 1.0 / 12, -11.0 / 24, A.mult, A.add)
    ts(pq(2), pq(1), MAG, MAG, A.add, A.subtract)
    ts(pq(3), pq(2), -12.0, None, A.mult)
    tt(pq(4), pq(3), pq(0), A.add)
    ts(pq(5), pq(2), 1.0, None, A.add)
    tt(pq(6), pq(5), pq(4), A.add)
    ts(pq(7), pq(6), 11.5, -12.0, A.is_gt, A.mult)
    tt(pq(8), pq(6), pq(7), A.add)
    tt(pq(9), pq(4), pq(8), A.subtract)
    ts(pq(9), pq(9), 2.0 ** 8, None, A.mult)
    ts(pcol(8), picol(1), 1.0, None, A.add)
    ts(pq(10), pq(4), pcol(8), None, A.add)
    ts(pq(11), pq(8), pcol(8), None, A.add)
    ts(pcol(9), pcol(3), 5.5, KILL, A.is_lt, A.mult)
    for b in range(5):
        ts(blk("kla", b), r("cob", 0, 128), pq(10, b, b + 1), KILL if b < 4 else pcol(9), A.is_equal, A.mult)
        ts(blk("klb", b), r("cob", 0, 128), pq(11, b, b + 1), KILL if b < 4 else pcol(9), A.is_equal, A.mult)
    tt(r("cr", 24, 27), r("ee", 0, 6, 2), r("ee", 1, 6, 2), A.add)
    tt(pcol(12), ccol(24), ccol(25), A.subtract)
    tt(pcol(13), ccol(26), ccol(24), A.subtract)
    tt(pcol(2), ccol(26), ccol(25), A.subtract)
    ts(pcol(14), pcol(2), 2.0 ** 20, None, A.mult)
    for b in range(5):
        act(r("kla", 128 * b + 13, 128 * b + 128, 16), r("bm", 16, 144, 16), F.Identity, scale=pq(9, b, b + 1))
        if b >= NS:
            act(r("kla", 128 * b + 14, 128 * b + 128, 16), r("bm", 16, 144, 16), F.Identity, scale=pcol(14) if b == 4 else -2.0 ** 19)
        to = r("pb7" if b // 4 else "pb3", 128 * (b % 4), 128 * (b % 4) + 128)
        mm(to, blk("kla", b), blk("idb", 0), True, False)
        mm(to, blk("klb", b), blk("idb", 1), False, True)
    made = []
    for a, b, pbk in ((0, 512, "pb3"), (512, 640, "pb7")):
        made.append(act(r("dc", a, b), r(pbk, 0, b - a), F.Identity, scale=2.0 ** -22)["id"])
        made.append(act(r("dd", a, b), r(pbk, 0, b - a), F.Identity, scale=0.25)["id"])
    mm(r("pb4", 0, 128 * NS), blk("idb", 0), r("kla", 0, 128 * NS), True, False)
    mm(r("pb4", 0, 128 * NS), blk("idb", 1), r("klb", 0, 128 * NS), False, True)
    for b in range(2):
        act(blk("tmpc", b), blk("iw", 0), F.Identity, scale=pcol(12 + b))
        mm(blk("pb4", NS), blk("tmpc", b), blk("klb" if b else "kla", 4), b == 0, b == 1)
    act(r("kl0", 0, 128 * NS + 128), r("pb4", 0, 128 * NS + 128), F.Copy)
    ccx = r("ccx", 0, 128)
    iota(ccx, [[0, 8], [1, 16]], -7, 0)
    sel(ccx, ccx, group, A.is_equal, 0.0, -13, 1)
    sel(ccx, ccx, [[-1, 128]], A.not_equal, 16.0, 0, 1)
    for nm, a, b, s, v in (("mc0", 6, 8 * L, 8, 4096), ("mc0", 7, 8 * L, 8, 4096), ("fss", 0, 128, 1, -1), ("fss", 0, 128, 16, 8192),
                           ("fpar", 0, 128, 2, -1), ("fpar", 1, 128, 2, 1), ("frv", 0, 128, 1, 0), ("frv", 15, 128, 16, 1), ("zero", 0, 512, 1, 0),
                           ("fs1", 0, 128, 1, -8192), ("kr", 0, 128, 1, MAG), ("df", 0, 128, 1, 0), ("thr", 0, 64, 1, MAG + 100), ("thr", 0, 64, 8, -1),
                           ("thr", 6, 64, 8, MAG + 999), ("thr", 7, 64, 8, MAG + 999), ("mc", 6, 7 * L, 7, 4096), ("f6", 0, 768, 1, 1), ("f6", 0, 768, 6, 0)):
        if (nm != "frv" or not MV) and (nm != "f6" or not MT):
            fill(r(nm, a, b, s), v)
    ms(r("fs1", 0, 128, 16), SENT)
    for p in range(NP):
        n, l0 = PARTS[p], sum(PARTS[:p])
        fill(r("xs", l0 + 16 * p, l0 + 16 * p + 16), 0)
        if not MV:
            fill(r("ge", l0 + 16 * p + n, l0 + 16 * p + n + 16), 0)
        fill(r("s1", 6 * l0 + 16 * p, 6 * l0 + 16 * p + 16), 0)
        fill(r("ww", 6 * l0, 6 * l0 + n), 1)
    act(r("rf0", 0, L), r("rsi", 0, L), F.Copy)
    for c in range(NCH):
        a, b = CUTS[c], CUTS[c + 1]
        CW, first = b - a, len(ops)
        ts(r("hi", a, b), r("raw", a, b), 15, None, A.logical_shift_right)
        lo = r("win", W + a, W + b) if len(ZC) == 1 else r("lo", a, b)
        lolast = ts(lo, r("raw", a, b), 32767, None, A.bitwise_and)
        if CW > TS:
            act(r("pb%d" % (c % 3), 0, CW), r("hi", a, b), F.Copy)
            tt(r("mn", a, b), lo, r("pb%d" % (c % 3), 0, CW), A.min)
        else:
            tt(r("mn", a, b), lo, r("hi", a, b), A.min)
        vlast = len(ops) - 1
        mnlast = act(r("mnb", a, b), r("mn", a, b), F.Identity, bias=191.5 + E12, scale=1.0 / 2048)
        for o in ops[first:]:
            o["boost"] = 50000.0 - 3000.0 * c
        for q, to, src in zip(ZC, (r("win", a, b), r("win", W + a, W + b)), (r("hi", a, b), lo)):
            if q == "S":
                act(to, src, F.Copy)
            else:
                sel(to, src, [[0, CW]], A.is_ge, 0.0, 0, 0)
        if ZC:
            src = r("win", W + a, W + b, 1, 1, 128, 2) if len(ZC) == 1 else r("lo", a, b, 1, 1, 128, 2)
            dma("Y", "dwa%d" % c, r("win", a, b, 1, 0, 128, 2), src, 256 * CW)
            dma("Y", "dwb%d" % c, r("win", W + a, W + b, 1, 1, 128, 2), r("hi", a, b, 1, 0, 128, 2), 256 * CW)
        elif (c + 1) % (NCH // 2) == 0:
            a = b - W // 2
            for par in range(2):
                for u, nm in enumerate(("lo", "hi")):
                    o = (1 - par) * W
                    dma("Y", "dw%d" % (a // (W // 2)), r("win", o + a, o + b, 1, u, 128, 2), r(nm, a, b, 1, par, 128, 2), 2 ** 18)
    dma("Y", "dpay", r("payt", 0, W), lambda T: T.pay[:, :], 2 ** 19)["x"].append(lolast["id"])
    for o in ops:
        if o["e"] == "S" and o["o"][0]["n"] in ("dc", "dd", "kl0", "iwb", "tmpc"):
            o["x"].append(mnlast["id"])
        if o.get("dma", "")[:3] == "dar":
            o["boost"] = 90000.0 - 5000.0 * o["id"]

    def lists(out, src, scalar):
        if scalar:
            act(out, src, F.Identity, bias=1023.5, scale=2048.0)
        else:
            ts(out, src, 2048.0, 1023.5, A.mult, A.add)

    turn, sums = [0, 0], []
    for t in range(V):
        for p in range(NP):
            n, l0 = PARTS[p], sum(PARTS[:p])
            grp[0], grp[2] = p, t == V - 1
            e, m = n // 16, 6 * n // 16
            j, jl = NP * t + p, NP * (t - 1) + p
            H = lambda nm, a=0, b=n, s=1, w=1: r(nm, w * l0 + a, w * l0 + b, s)
            M = lambda nm, a=0, b=m, s=1, tt_=0: r(nm, 96 * tt_ + 6 * l0 // 16 + a, 96 * tt_ + 6 * l0 // 16 + b, s)
            Q = lambda nm, a=0, b=n // 2, s=1: r(nm, l0 // 2 + a, l0 // 2 + b, s)
            bank = lambda use: {"use": use, "key": "%s%d" % (use, len(ops)), "bank": None, "ops": set()}
            pb = "pb%d" % BANKS["own"][p]
            O = lambda a, b, s=1: r(pb, a, b, s)
            Fp, Mp = O(0, n), O(128, 128 + n)

            def turn_lists(out, src, mat, rot, first, last, w=m):
                for c0 in range(2):
                    for h0 in range(2):
                        o = 256 * c0 + (16 * (c0 - h0 - rot)) % 128
                        mm(out(c0, w, 2), r(mat, o, o + 128), src(h0), first and h0 == 0, (h0 == 1) if first else (last and c0 == 1 and h0 == 1))

            waves = ([("e", 0, e * SPL)] if SPL else []) + [("o", e * SPL, m)]
            if t == 0:
                st3 = view("sti", (slice(0, K), slice(l0 // 16, l0 // 16 + e)))
                cp(M("off1"), st3)
                ts(M("sf0"), st3, 1.0 / 2048, -1023.5 / 2048, A.mult, A.add)
                rfin = lambda a, b: H("rf0", a, b)
            else:
                rfin = lambda a, b: r("rfl", L * (t - 1) + l0 + a, L * (t - 1) + l0 + b)
                add("R", None, [rfin(0, n)], [], 0, recv="ar%d" % jl, after=("r", jl))
                for nm, c0, c1 in waves:
                    add("R", None, [M("zdl", c0, c1, 1, t - 1)], [], 0, recv="a%s%d" % (nm, jl), after=(nm, jl))
                    turn_lists(lambda a, b, s: O(256 + c0 + a, 256 + c0 + b, s), lambda h0: M("zdl", c0 + h0, c1, 2, t - 1), "iwb", 1, True, True, c1 - c0)
                    conv = ops[-1]
                    lists(M("off1", c0, c1), O(256 + c0, 256 + c1), O1S)
            cw = 8 if t == 0 else 7
            mc = "mc0" if t == 0 else "mc"
            gat = {}
            for k in range(K):
                if k >= K - GV[p]:
                    tsg(H(mc, 5 - k, cw * n, cw, cw), r("mnb", 0, W), -192.0, M("off1", e * k, e * k + e))
                    continue
                sub = n if k < SPL and t else SUB
                for a in range(0, n, sub):
                    b = min(n, a + sub)
                    o = act(H(mc, cw * a + 5 - k, cw * b, cw, cw), r("mnb", 0, W), F.Identity, bias=-192.0, off=M("off1", e * k + a // 16, e * k + b // 16))
                    if k <= (SPL if t else 0) + max(LATE, 0):
                        gat[a // SUB] = o["id"]
            nc = -(-cw * n // 448)
            for a, b in ((n * c // nc, n * (c + 1) // nc) for c in range(nc)):
                bk = bank("dif")
                mm(r(bk, cw - 1, cw * (b - a), cw), blk("iw", 0), H("act", a, b), True, True)["x"].append(
                    vlast if j == 0 else gat[a // SUB] if LATE >= 0 or not t else conv["id"])
                for jj in range(cw - 1):
                    mm(r(bk, jj, cw * (b - a), cw), blk("dl", jj) if jj < K else r("rk", 0, 128), rfin(a, b), True, True)["x"].append(len(ops) - 2)
                lastscn = scan(H("scn", cw * a, cw * b, 1, 8), r(bk, 0, cw * (b - a)), H(mc, cw * a, cw * b, 1, cw), A.add, A.min)
            x0 = l0 + 16 * p
            SS = O(384, 384 + n)
            tr(r("xs", x0 + 16, x0 + 16 + n), H("scn", cw - 1, cw * n, cw, 8))
            early = scan(SS, r("xs", x0 + 15, x0 + 15 + n), r("fss", 0, n), A.min, A.max)
            tt(r("ge", x0, x0 + n), r("xs", x0 + 16, x0 + 16 + n), SS, A.is_ge)
            early = lastscn if EARLY else early
            direct = W0 and t == 0
            if not direct:
                scan(H("ps"), r("fpar", 0, n), r("ge", x0, x0 + n), A.add, A.mult)
            if MV or direct:
                tr(H("stg"), r("ge", x0, x0 + n))
            else:
                scan(rev("step", l0, l0 + n), rev("ge", x0 + 1, x0 + 1 + n), rev("frv", 0, n), A.min, A.max)
                tr(H("stg"), H("step"))
            for k in range(REP if REP > 1 and not direct else 0):
                act(M("p6", e * k, e * k + e), H("ps", 15, n, 16), F.Copy)
            for k0 in range(0, 0 if direct else K, KO):
                pab = bank("par")
                PA = lambda a, b, s=1: r(pab, 448 + a, 448 + b, s)
                c0, c1 = e * k0, e * (k0 + KO)
                if t == 0:
                    mm(PA(0, c1 - c0), blk("idb", 0), M("sf0", c0, c1), True, False)["x"].append(early["id"])
                else:
                    mm(PA(0, c1 - c0), r("zero", 0, 128), r("zero", 0, c1 - c0), True, False)["x"].append(early["id"])
                    turn_lists(PA, lambda h0: M("zdl", c0 + h0, c1, 2, t - 1), "iwb", 1, False, False, c1 - c0)
                for k in range(0, KO, REP):
                    turn_lists(lambda a, b, s: PA(e * k + a, e * k + b, s), lambda h0: H("ps", 15 + 16 * h0, n, 32) if REP == 1 else M("p6", h0, e * REP, 2),
                               "iwb", 0, False, k == KO - REP, e * REP)
                lists(M("off2", c0, c1), PA(0, c1 - c0), O2S > (k0 == 0))
            mm(Mp, r("dm0" if direct else "dm", 0, 128), H("stg"), True, True)
            if direct:
                cm_ = act(H("msk"), Mp, F.Relu, bias=ccol(30))
            else:
                cm_ = ts(H("msk"), Mp, pcol(15), None, A.is_gt) if MV else act(H("msk"), Mp, F.Copy)
            mm(Fp, r("ra", 0, 128), rfin(0, n), True, False)["x"].append(cm_["id"])
            for i in range(2 * K if direct else K):
                k, MG = i % K, H("mg", n * i, n * i + n, 1, 12)
                if direct:
                    lastg = tt(MG, r("hi" if i >= K else "lo", 0, W), H("msk"), A.mult, off=M("off1", e * k, e * k + e))
                    mm(Fp, r("self0", 15 - i, 143 - i), MG, False, i == 2 * K - 1)
                else:
                    lastg = tt(MG, r("win", 0, 2 * W), H("msk"), A.mult, off=M("off2", e * k, e * k + e))
                    mm(Fp, r("self", 8 - k, 136 - k), MG, False, k == K - 1)
            ts(H("cc"), Fp, MAG, MAG, A.add, A.subtract)
            tt(H("dfr"), Fp, H("cc"), A.subtract)
            (vb, v0), stb = (bank("vt"), 0) if BANKS["vt"] else (pb, 64), bank("st")
            place = lambda b: r(vb, v0 + n * (b - NS), v0 + n * (b - NS + 1)) if NS <= b < 4 else r(stb, n * min(b, NS), n * min(b, NS) + n)
            sets = [list(range(NS, 4)), list(range(NS)) + [4]]
            for bs in sets[::-1] if SF else sets:
                if ZS:
                    whole = r(stb, 0, n * (NS + 1)) if 4 in bs else r(vb, v0, v0 + n * VS)
                    mm(whole, r("zero", 0, 128), r("zero", 0, whole["w"]), True, False)["x"] += [lastg["id"]] + made * (t == 0)
                    for b in bs:
                        mm(place(b), blk("dc", b), H("cc"), False, False)
                    for b in bs:
                        mm(place(b), blk("dd", b), H("dfr"), False, b == bs[-1])
                else:
                    for b in bs:
                        mm(place(b), blk("dc", b), H("cc"), True, False)["x"] += [len(ops) - 2] if b != bs[0] else made * (t == 0)
                        mm(place(b), blk("dd", b), H("dfr"), False, True)
            SG = lambda a, b: H("sg", n * a, n * b, 1, 13)
            CQ = 1.5 * 2.0 ** 21
            kills = []
            for v in range(2):
                ts(SG(VS * v, VS * v + VS), r(vb, v0, v0 + n * VS), CQ, CQ - 0.25 * v, A.add, A.is_equal)
                kills += [(blk("klb" if v else "kla", NS + b), VS * v + b) for b in range(VS)]
            s0 = 2 * VS
            act(SG(s0, s0 + NS + 1), r(stb, 0, n * (NS + 1)), F.Sign)
            kills += [(blk("kl0", b), s0 + b) for b in range(NS + 1)]
            for v in range(2):
                s1 = s0 + NS + 1 + NS * v
                act(SG(s1, s1 + NS), r(stb, 0, n * NS), F.Sign, bias=0.25, scale=1.0 if v else -1.0)
                kills += [(blk("klb" if v else "kla", b), s1 + b) for b in range(NS)]
            if SF:
                a, b = 2 * VS + NS + 1, 2 * VS + 2 * NS + 1
                kills = kills[2 * VS:a] + kills[:VS] + kills[a:b] + kills[VS:2 * VS] + kills[b:]
            Xp = Mp
            for i, (lh, s) in enumerate(kills):
                mm(Xp, lh, SG(s, s + 1), i == 0, False)
            mm(Xp, r("ccx", 0, 128), H("cc"), False, False)
            mm(Xp, blk("idb", 0), H("dfr"), False, True)
            tr(H("xt"), Xp)
            sb = 6 * l0 + 16 * p + 16
            S1 = lambda a, b, s=1: r("s1", sb + a, sb + b, s)
            for k in range(K):
                scan(S1(n * k, n * k + n), H("xt"), r("fs1", 0, n) if k == 0 else S1(n * k - n - 1, n * k - 1), A.min, A.max)
                if k < K - KV:
                    act(Q("kr", k, n // 2, 8), S1(n * k + 12, n * k + n, 16), F.Identity, bias=MAG, scale=1.0 / 16)
                else:
                    ts(Q("kr", k, n // 2, 8), S1(n * k + 12, n * k + n, 16), 1.0 / 16, MAG, A.mult, A.add)
            zd = lambda a=0, s=1: M("zds", a, m, s, t)
            for nm, c0, c1 in waves if t < V - 1 else [("o", 0, m)]:
                ts(M("ka", c0, c1), S1(16 * c0 + 12, 16 * c1, 16), MAG, MAG, A.add, A.subtract)
                tt(M("zds", c0, c1, 1, t), S1(16 * c0 + 12, 16 * c1, 16), M("ka", c0, c1), A.subtract)
                if t < V - 1:
                    add("G", None, [], [M("zds", c0, c1, 1, t)], ISSUE, send=(nm, j), lat=LATS, to=M("zdl", c0, c1, 1, t))
            turn_lists(lambda a, b, s: O(304 + a, 304 + b, s), lambda h0: zd(h0, 2), "iwb", 0, True, True)
            lists(M("offu"), O(304, 304 + m), OUS)
            tt(Q("df", 1), Q("kr", 1), Q("kr", 0, n // 2 - 1), A.subtract)
            tt(H("rt", 1, n, 2), Q("kr"), r("thr", 0, n // 2), A.is_lt)
            scan(H("rt", 0, n, 2), Q("df"), H("rt", 1, n, 2), A.add, A.mult)
            rfo = lambda a=0, b=n: r("rfs", L * t + l0 + a, L * t + l0 + b)
            tr(rfo(), H("rt"))
            if t < V - 1:
                add("G", None, [], [rfo()], ISSUE, send=("r", j), lat=LATS, to=r("rfl", L * t + l0, L * t + l0 + n))
            XX = lambda a, b, s=1: r("xx", 6 * L * t + 6 * l0 + a, 6 * L * t + 6 * l0 + b, s)
            xs = XS if t < V - 1 else min(XS, 1)
            for k0, k1 in ((1, 4), (4, 6)) if 5 * n > 448 else ((1, 6),):
                bk = bank("pay")
                for k in range(k0, k1):
                    mm(r(bk, n * (k - k0), n * (k - k0 + 1)), r("rk", 144 * k + 16, 144 * k + 144), rfo(), True, True)["boost"] = 5000.0 * (t == V - 1)
                turn[1] += 1
                if k0 < xs:
                    act(H("pg", n * k0, n * k1, 1, 6), r("payt", 0, W), F.Copy, off=M("offu", e * k0, e * k1))
                    act(r(bk, 0, n * (k1 - k0)), r(bk, 0, n * (k1 - k0)), F.Exp, scale=-0.125, extra=1300.0 if turn[1] == 1 else 0.0)
                    tt(XX(n * k0, n * k1), H("pg", n * k0, n * k1, 1, 6), r(bk, 0, n * (k1 - k0)), A.mult)
                else:
                    act(H("ww", n * k0, n * k1, 1, 6), r(bk, 0, n * (k1 - k0)), F.Exp, scale=-0.125, extra=1300.0 if turn[1] == 1 else 0.0)
            rotm = r("iw", 16 * t, 16 * t + 128)
            if t < V - 1:
                if XS:
                    act(XX(0, n), r("payt", 0, W), F.Copy, off=M("offu", 0, e))
                for k in range(XS, K, GP):
                    k1 = min(K, k + GP)
                    tt(XX(n * k, n * k1), r("payt", 0, W), H("ww", n * k, n * k1, 1, 6), A.mult, off=M("offu", e * k, e * k1))
                LD = lambda b: r("land", 2 * L * t + 2 * l0 + n * b, 2 * L * t + 2 * l0 + n * b + n)
                add("G", None, [], [XX(0, 6 * n)], ISSUE, send=("x", j), lat=LATX if t < DIRECT else LATD,
                    behind=("r", NP * t + NP - 1) if t >= DIRECT else None, srcs=[XX(n * k, n * k + n) for k in range(K)], to=[LD(0), LD(1)])
                add("R", None, [LD(0), LD(1)], [], 0, recv="ax%d" % j, after=("x", j))
                sums += [(r("pb4", L * b + l0, L * b + l0 + n), rotm, LD(b)) for b in range(2)]
                if j == 0:
                    mm(r("pb4", 0, 512), r("zero", 0, 128), r("zero", 0, 512), True, False)
                while sums:
                    mm(*sums.pop(), False, False, True)
            else:
                if p == 0:
                    act(r("accb", 0, L if FV else 512), r("pb4", 0, L if FV else 512), F.Copy)
                mb = bank("fin")
                for k in range(K):
                    if k < xs:
                        act(XX(k, 6 * n, 6), r("payt", 0, W), F.Copy, off=M("offu", 0, e))
                    else:
                        tt(XX(k, 6 * n, 6), r("payt", 0, W), H("ww", n * k, n * k + n, 1, 6), A.mult, off=M("offu", e * k, e * k + e))
                    last = mm(Fp, rotm, XX(k, 6 * n, 6), k == 0, False)
                    if MT and k:
                        to = H("mx", 5, 6 * n, 6, 6) if k == K - 1 else O(384, 384 + n)
                        tt(to, XX(k, 6 * n, 6), XX(0, 6 * n, 6) if k == 1 else O(384, 384 + n), A.max)
                mm(Fp, blk("iw", 0), r("accb", l0, l0 + n), False, True)
                if not MT:
                    scan(H("mx", 0, 6 * n, 1, 6), r("f6", 0, 6 * n), XX(0, 6 * n), A.mult, A.max)
                act(r("outb", l0, l0 + n), Fp, F.Copy)
                if FV:
                    for a, b in ((0, 64), (64, 0)):
                        tt(r("outb", L + l0, L + l0 + n, 1, a, a + 64), r("mx", 6 * l0 + 5, 6 * l0 + 6 * n, 6, b, b + 64), r("pb4", L + l0, L + l0 + n, 1, a, a + 64), A.add)
                else:
                    mm(r(mb, 0, n), blk("iw", 0), r("accb", L + l0, L + l0 + n), True, False)["x"].append(last["id"])
                    mm(r(mb, 0, n), rotm, H("mx", 5, 6 * n, 6, 6), False, True)
                    act(r("outb", L + l0, L + l0 + n), r(mb, 0, n), F.Copy)
                dma("Y", "dout", lambda T, l0=l0, n=n: T.ys[:, l0:l0 + n], r("outb", l0, l0 + n), 2 ** 16)
                dma("Y", "dout", lambda T, l0=l0, n=n: T.ym[:, l0:l0 + n], r("outb", L + l0, L + l0 + n), 2 ** 16)
    return ops


def kind(o):
    x = o["i"][1] if o["e"] == "P" else (o["o"] or o["i"])[0]
    return "%s%s%d" % (o["e"], x["n"], o["part"])


def meet(a, b):
    return a["cm"] & b["cm"] and a["pm"] & b["pm"]


def prepare():
    ops = build()
    n = len(ops)
    hist, sends, groups = {}, {}, {}
    for o in ops:
        deps = set(o["x"])
        for x in o["i"]:
            deps.update(p for (p, y, w) in hist.get(x["key"], []) if w and meet(x, y))
        for x in o["o"]:
            deps.update(p for (p, y, w) in hist.get(x["key"], []) if meet(x, y) and not (o.get("acc") and ops[p].get("acc")))
        for x in o["o"]:
            if not o.get("acc"):
                hist[x["key"]] = [e for e in hist.get(x["key"], []) if (e[1]["cm"] & ~x["cm"]) or (e[1]["pm"] & ~x["pm"])]
            hist.setdefault(x["key"], []).append((o["id"], x, True))
        for x in o["i"]:
            hist.setdefault(x["key"], []).append((o["id"], x, False))
        if "send" in o:
            sends[o["send"]] = o["id"]
        if "after" in o:
            deps.add(sends[o["after"]])
        if "dma" in o:
            groups.setdefault(o["dma"], []).append(o["id"])
        deps.discard(o["id"])
        o["d"] = deps
        o["ps"] = [x for x in o["o"] + o["i"] if psum(x)]
        o["loan"] = ([x["loan"] for x in o["ps"] if x["loan"]] + [None])[0]
        o["kind"] = kind(o)
    for o in ops:
        if o.get("behind"):
            o["d"].add(sends[o["behind"]])
    for o in ops:
        for p in list(o["d"]):
            if "dma" in ops[p] and o.get("dma") != ops[p]["dma"]:
                o["d"].update(groups[ops[p]["dma"]])
    succ = [[] for _ in range(n)]
    for o in ops:
        for p in o["d"]:
            succ[p].append(o["id"])

    def gap(p, o):
        if p["e"] == "P" and o["e"] == "P":
            return 0.0
        if "send" in p and "send" in o:
            return -p["lat"]
        return SAME if p["e"] == o["e"] else CROSS
    order, left = [], [len(o["d"]) for o in ops]
    st = [o["id"] for o in ops if not o["d"]]
    while st:
        a = st.pop()
        order.append(a)
        for s in succ[a]:
            left[s] -= 1
            if left[s] == 0:
                st.append(s)
    pr = [0.0] * n
    for a in reversed(order):
        o = ops[a]
        pr[a] = o["cost"] + o.get("lat", 0.0) + max([pr[s] + gap(o, ops[s]) for s in succ[a]] + [0.0])
    return ops, succ, pr, gap


def plan(bias=None, pre=None):
    ops, succ, pr, gap = pre or prepare()
    n = len(ops)
    bias = BIAS if bias is None else bias
    pr = [pr[a] + ops[a].get("boost", 0.0) + bias.get(ops[a]["kind"], 0.0) - STAG * ops[a]["part"] for a in range(n)]
    for o in ops:
        if o["loan"]:
            o["loan"]["bank"] = None
            o["loan"]["ops"].add(o["id"])
    free, bank, opened, held = {}, {}, set(), set()
    end, rdy = [0.0] * n, [0.0] * n
    left = [len(o["d"]) for o in ops]
    ready = [o["id"] for o in ops if not o["d"]]
    seq = []
    while ready:
        est = {}
        for a in ready:
            o = ops[a]
            loan = o["loan"]
            if loan and loan["bank"] is None:
                choice = [["pb%d" % b] for b in BANKS[loan["use"]] if ("pb%d" % b, loan["use"] == "par") not in held]
            else:
                choice = [[place_of(x) for x in o["ps"]]]
            for banks in choice:
                if o.get("start") and banks[0] in opened:
                    continue
                s = max(rdy[a], free.get(o["e"], 0.0))
                for b in banks:
                    for e2, t2 in bank.get(b, {}).items():
                        if e2 != o["e"]:
                            s = max(s, t2 + CROSS)
                if a not in est or s < est[a]:
                    est[a], o["banks"] = s, banks
        a0 = min(est, key=lambda a: est[a])
        e = ops[a0]["e"]
        a = max([c for c in est if ops[c]["e"] == e and est[c] <= est[a0] + LOOK], key=lambda c: pr[c])
        a = max([c for c in est if ops[c]["e"] == e and est[c] <= est[a] + ALPHA * ops[a]["cost"]], key=lambda c: pr[c])
        for c in est:
            if ops[c]["e"] == "R":
                a, e = c, "R"
        o = ops[a]
        ready.remove(a)
        seq.append(a)
        o["t0"] = est[a]
        loan = o["loan"]
        if loan:
            if loan["bank"] is None:
                loan["bank"] = o["banks"][0]
                held.add((loan["bank"], loan["use"] == "par"))
            loan["ops"].remove(a)
            if not loan["ops"]:
                held.discard((loan["bank"], loan["use"] == "par"))
        if o.get("start"):
            opened.add(o["banks"][0])
        if o.get("stop"):
            opened.discard(o["banks"][0])
        if e != "R":
            free[e] = est[a] + o["cost"]
        end[a] = est[a] + o["cost"] + o.get("lat", 0.0)
        if "nb" in o:
            free["D"] = max(free.get("D", 0.0), est[a] + 1300) + o["nb"] / BW
            end[a] = free["D"] + 300
        for b in o["banks"]:
            bank.setdefault(b, {})[e] = est[a] + o["cost"]
        for s in succ[a]:
            rdy[s] = max(rdy[s], end[a] + gap(o, ops[s]))
            left[s] -= 1
            if left[s] == 0:
                ready.append(s)
    if pre:
        return seq
    lastb = {}
    for a in seq:
        o = ops[a]
        for b in o["banks"]:
            o["d"].update(p for e2, p in lastb.get(b, {}).items() if e2 != o["e"])
            lastb.setdefault(b, {})[o["e"]] = a
    ops[[a for a in seq if ops[a].get("acc")][-1]]["close"] = True
    return ops, seq, max(end)


PLAN = []


def helper_of(core, T, topo):
    return [c for c in topo.cores_of(core) if T.rank_of(c) is None and topo.die(c) == topo.die(core)][0]


def bits(engines):
    return sum(1 << e for e in engines)


def lanes_engines(src, dst, j, topo):
    return topo.engines(src, dst)[:16 if j >= NP and WIDE else 8]


def rank_program(g, core, T, topo):
    rank = T.rank_of(core)
    N = len(T.cores)
    if rank is None:
        for q in range(N):
            if helper_of(T.cores[q], T, topo) == core:
                for j in range(NP * DIRECT):
                    t, p = j // NP, j % NP
                    owner = T.cores[(q - t) % N]
                    rid, pid = topo.addr(owner, core)
                    a = 2 * L * t + 2 * sum(PARTS[:p])
                    g.wait_ge(T.sem["ao%d" % j], 8)
                    g.remote_dma(T.land[:, a:a + 2 * PARTS[p]], T.land[:, a:a + 2 * PARTS[p]], T.sem["ax%d" % j], T.sem.loc,
                                 pid, rid, bits(topo.engines(core, owner)[:8]))
                g.wait_ge(T.sem.loc, 8 * NP * DIRECT)
        return
    if not PLAN:
        PLAN.append(plan())
    ops, seq, _ = PLAN[0]
    nxt = T.cores[(rank + 1) % N]
    hlp = helper_of(core, T, topo)
    nrid, npid = topo.addr(nxt, core)
    hrid, hpid = topo.addr(hlp, core)
    en = topo.engines(core, nxt)[:8]
    eh = [e for e in topo.engines(core, hlp) if e not in en]
    queue = {"V": g.vector, "S": g.scalar, "P": g.tensor, "G": g, "Y": g.sync}
    esem = {"V": "eV", "S": "eS", "P": "eP", "G": "eG"}
    needed = set(p for o in ops for p in o["d"] if not (o["e"] == "P" and ops[p]["e"] == "P") and o["e"] != "R")
    cnt, tok, waited = {}, {}, {}
    loc = 0
    for a in seq:
        o = ops[a]
        e = o["e"]
        if e == "R":
            tok[a] = (o["recv"], 8 if o["after"][0] == "x" else len(lanes_engines(T.cores[(rank - 1) % N], core, o["after"][1], topo)))
            cnt[o["recv"]] = tok[a][1]
            continue
        want = {}
        for p in o["d"]:
            if not (e == "P" and ops[p]["e"] == "P") and "send" not in ops[p]:
                want[tok[p][0]] = max(want.get(tok[p][0], 0), tok[p][1])
        for s in sorted(want):
            if waited.get((e, s), 0) < want[s]:
                queue[e].wait_ge(T.sem[s], want[s])
                waited[(e, s)] = want[s]
        if "send" in o:
            kind, j = o["send"]
            if kind != "x":
                eng = lanes_engines(core, nxt, j, topo)
                g.remote_dma(ap(T, o["to"]), ap(T, o["i"][0]), T.sem["a%s%d" % (kind, j)], T.sem.loc, npid, nrid, bits(eng))
                loc += len(eng)
            else:
                rid, pid, eng, sem = hrid, hpid, eh, "ao%d" % j
                if j >= NP * DIRECT:
                    owner = T.cores[(rank - j // NP) % N]
                    (rid, pid), eng, sem = topo.addr(owner, core), topo.engines(core, owner)[-8:], "ax%d" % j
                g.remote_dma_fused([RemoteDMATransfer(dst_ids=[DstId(rid=rid, pnc=pid)], dma_engine_mask=bits(eng[4 * b:4 * b + 4]),
                                                      remote_sem=T.sem[sem], srcs=[ap(T, x) for x in o["srcs"]],
                                                      dsts=[ap(T, o["to"][b])], alu_op=1 + b) for b in range(2)], local_sem=T.sem.loc)
                loc += 8
            continue
        ins = o["f"](g, T, True) if o.get("close") else o["f"](g, T)
        if "dma" in o:
            s = o["dma"]
            cnt[s] = cnt.get(s, 0) + 16
            ins.then_inc(T.sem[s], 16)
            tok[a] = (s, cnt[s])
        elif a in needed:
            s = esem[e]
            cnt[s] = cnt.get(s, 0) + 1
            ins.then_inc(T.sem[s], 1)
            tok[a] = (s, cnt[s])
    for s in sorted(cnt):
        if max(waited.get((e, s), 0) for e in queue) < cnt[s]:
            g.wait_ge(T.sem[s], cnt[s])
    g.wait_ge(T.sem.loc, loc)
